import numpy as np
import ml_dtypes


def mxq(x, axis, fmt="e4m3"):
    dtype, down = {"e4m3": (ml_dtypes.float8_e4m3fn, 7), "e5m2": (ml_dtypes.float8_e5m2, 14)}[fmt]
    v = np.moveaxis(np.asarray(x, np.float32).astype(ml_dtypes.bfloat16).astype(np.float64), axis, -1)
    blocks = v.reshape(v.shape[:-1] + (-1, 32))
    amax = np.abs(blocks).max(-1, keepdims=True)
    byte = np.maximum(np.where(amax > 0, np.frexp(amax)[1] - 1 + 127, 0) - down, 1)
    scale = np.exp2(byte - 127.0)
    codes = (blocks / scale).astype(np.float32).astype(dtype).astype(np.float64)
    return np.moveaxis((codes * scale).reshape(v.shape), -1, axis)


WIDE = False


def mx_kscale(k):
    if not WIDE:
        return np.ones(k)
    levels = np.array([24, -24, 12, -12, 0])
    if k % 512:
        return np.exp2(np.random.permutation(np.resize(levels, k // 32))).repeat(32)
    a = np.empty((k // 512, 16))
    for p in range(k // 512):
        a[p, :8] = np.random.permutation(np.resize(levels, 8))
        for g in range(8):
            far = levels[np.abs(levels - a[p, g]) >= 10]
            a[p, g + 8] = far[np.random.randint(len(far))]
    return np.exp2(a.ravel()).repeat(32)


def f64(x):
    return np.asarray(x).astype(np.float64)


def striped(idx):
    return np.tile(idx.reshape(-1, 16).T, (8, 1)).astype(np.uint16)


def unstriped(offs):
    return offs[:16].T.reshape(-1).astype(np.int64)


E2M1 = np.array([0.0, 0.5, 1.0, 1.5, 2.0, 3.0, 4.0, 6.0, -0.0, -0.5, -1.0, -1.5, -2.0, -3.0, -4.0, -6.0])


def pack_weight(w, fmt):
    k, n = w.shape
    w = f64(np.asarray(w, np.float32).astype(ml_dtypes.bfloat16)).reshape(k // 32, 32, n)
    amax = np.abs(w).max(1)
    if fmt == "e4m3":
        byte = np.frexp(amax)[1] - 1 + 127 - 7
    else:
        mant, ex = np.frexp(amax / 6.0)
        byte = np.where(mant > 0.5, ex, ex - 1) + 127
    byte = np.clip(np.where(amax > 0, byte, 1), 1, 254)
    scaled = (w * np.exp2(127.0 - byte)[:, None, :]).reshape(k, n).astype(np.float32)
    by_word = np.ascontiguousarray(scaled.reshape(k // 512, 128, 4, n).transpose(0, 1, 3, 2))
    if fmt == "e4m3":
        words = by_word.astype(ml_dtypes.float8_e4m3fn).view(np.uint8)
    else:
        c = by_word.astype(ml_dtypes.float4_e2m1fn).view(np.uint8) & 0xF
        words = (c[..., 0::2] | (c[..., 1::2] << 4)).reshape(k // 512, 128, 2 * n)
    return np.ascontiguousarray(words), np.ascontiguousarray(byte.astype(np.uint8).reshape(k // 512, 16, n))


def unpack_weight(words, scales, fmt):
    g, _, n = scales.shape
    words = np.ascontiguousarray(words).reshape(g, 128, n, -1)
    if fmt == "e4m3":
        vals = words.view(ml_dtypes.float8_e4m3fn).astype(np.float64)
    else:
        nib = np.empty((g, 128, n, 4), np.uint8)
        nib[..., 0::2] = words & 0xF
        nib[..., 1::2] = words >> 4
        vals = E2M1[nib]
    vals = vals * np.repeat(np.exp2(scales.astype(np.float64) - 127.0), 8, axis=1)[..., None]
    return vals.transpose(0, 1, 3, 2).reshape(g * 512, n)


def planes(y):
    n, m = y.shape
    v = y.astype(np.float32).astype(ml_dtypes.bfloat16).astype(np.float64).reshape(n // 32, 32, m)
    top = np.abs(v).max(1)
    byte = np.clip(np.where(top > 0, np.frexp(top)[1] - 1 + 127 - 7, 1), 1, 254)
    codes = (v * np.exp2(127.0 - byte)[:, None, :]).reshape(n, m).astype(np.float32).astype(ml_dtypes.float8_e4m3fn).view(np.uint8)
    words = codes.reshape(n // 512, 128, 4, m).transpose(0, 1, 3, 2)
    return np.ascontiguousarray(words), np.ascontiguousarray(byte.astype(np.uint8).reshape(n // 512, 16, m))


def gelu(f):
    return 0.5 * f * (1.0 + np.tanh(np.sqrt(2.0 / np.pi) * (f + 0.044715 * f**3)))


K, R, N, T, J = 512, 512, 512, 2048, 1024


def setup_inputs():
    n = np.random.standard_normal
    s = mx_kscale(K)[:, None]
    u = mx_kscale(R)[:, None]
    p_tab = pack_weight(n((K, T)) * s, "e4m3")
    p_wu = pack_weight(n((K, R)) / np.sqrt(K) / s, "e2m1")
    p_wd = pack_weight(n((R, N)) / np.sqrt(R) / u, "e4m3")
    return {
        "tab_words": p_tab[0],
        "tab_scales": p_tab[1],
        "wu_words": p_wu[0],
        "wu_scales": p_wu[1],
        "sm": (np.random.uniform(0.5, 2.0, R) * u[:, 0]).astype(np.float32),
        "wd_words": p_wd[0],
        "wd_scales": p_wd[1],
        "wgo": np.tile(np.random.uniform(0.5, 2.0, J), (128, 1)).astype(np.float32),
        "offs": striped(np.random.permutation(T)[:J]),
    }


def reference(tab_words, tab_scales, wu_words, wu_scales, sm, wd_words, wd_scales, wgo, offs):
    idx = unstriped(offs)
    tab_ = unpack_weight(tab_words, tab_scales, "e4m3")[:, idx]
    wu_ = unpack_weight(wu_words, wu_scales, "e2m1")
    a = wu_.T @ tab_
    h = f64(sm)[:, None] * gelu(a)
    h_ = mxq(h, 0, "e4m3")
    wd_ = unpack_weight(wd_words, wd_scales, "e4m3")
    y = wd_.T @ h_
    out = np.zeros((N, T))
    out[:, idx] = f64(wgo)[0] * (y)
    return (out,) + planes(out)

@@ -1,0 +1,237 @@
+from contextlib import ExitStack
+
+import concourse.mybir as mybir
+
+K, R, N, T, J = 512, 512, 512, 2048, 1024
+FLOPS = 2 * K * R * J + 2 * R * N * J
+
+F32 = mybir.dt.float32
+BF16 = mybir.dt.bfloat16
+I32 = mybir.dt.int32
+U32 = mybir.dt.uint32
+U16 = mybir.dt.uint16
+U8 = mybir.dt.uint8
+FP8X4 = mybir.dt.float8_e4m3fn_x4
+FP4X4 = mybir.dt.float4_e2m1fn_x4
+GELU = mybir.ActivationFunctionType.Gelu_apprx_tanh
+COPY = mybir.ActivationFunctionType.Copy
+MULT = mybir.AluOpType.mult
+
+P = 128
+PACK = 4
+QUADS = 4
+CHUNK = 256
+CHUNKS = J // CHUNK
+HALF = CHUNK // 2
+BANK = 512
+QUARTER = T // 4
+ALIGN = 64
+
+
+def tile_list_modp_gelu_noneP_kernel(
+    tc, tab_words, tab_scales, wu_words, wu_scales, sm, wd_words, wd_scales, wgo, offs, out_0, out_1, out_2
+):
+    nc = tc.nc
+    with ExitStack() as ctx:
+        sb = ctx.enter_context(tc.tile_pool(name="sb", bufs=1))
+        ps = ctx.enter_context(tc.psum_pool(name="ps", bufs=1))
+
+        def tile(shape, dtype, name, tag=None):
+            return sb.tile(shape, dtype, name=name, tag=tag or name, align_bytes=ALIGN)
+
+        def scale_rows(plane, rows, q, queue):
+            queue.dma_start(
+                out=plane[32 * q : 32 * q + 4, :].bitcast(I32), in_=rows[0, 4 * q : 4 * q + 4, :].bitcast(I32)
+            )
+
+        offsets = sb.tile([P, J // 16], U16, name="offsets")
+        nc.sync.dma_start(offsets[:], offs)
+
+        tab_s = tile([P, T], U8, "tab_s")
+        wu_s_raw = tile([P, R], U8, "wu_s_raw")
+        wd_s_raw = tile([P, N], U8, "wd_s_raw")
+        for plane in (tab_s, wu_s_raw, wd_s_raw):
+            nc.vector.memset(plane[:].bitcast(I32), 0)
+
+        tab_w = tile([P, T], I32, "tab_w")
+        wu_raw = tile([P, 2 * R], U8, "wu_raw")
+        wd_raw = tile([P, N], I32, "wd_raw")
+        sm_t = tile([P, PACK], F32, "sm_t")
+        wgo_t = tile([P, J], F32, "wgo_t")
+        for q in range(QUADS):
+            scale_rows(tab_s, tab_scales, q, nc.sync)
+        scale_rows(wu_s_raw, wu_scales, 0, nc.sync)
+        nc.sync.dma_start(out=tab_w[:], in_=tab_words[0].rearrange("p t i -> p (t i)").bitcast(I32))
+        nc.sync.dma_start(out=wu_raw[:].bitcast(I32), in_=wu_words[0].bitcast(I32))
+        for q in range(1, QUADS):
+            scale_rows(wu_s_raw, wu_scales, q, nc.scalar)
+        nc.sync.dma_start(out=sm_t[:], in_=sm.rearrange("(p t) -> p t", t=PACK))
+        nc.sync.dma_start(out=wd_raw[:], in_=wd_words[0].rearrange("p n i -> p (n i)").bitcast(I32))
+        nc.sync.dma_start(out=wgo_t[:], in_=wgo)
+        for q in range(QUADS):
+            scale_rows(wd_s_raw, wd_scales, q, nc.sync)
+
+        def listed(first, count):
+            return offsets[:, first // 16 : (first + count) // 16]
+
+        def gather(c, words_tag=None, scales_tag=None):
+            words = tile([P, CHUNK], U32, "gw%d" % c, words_tag)
+            scales = tile([P, CHUNK], U8, "gs%d" % c, scales_tag)
+            nc.vector.tensor_copy(words[:], tab_w[:].bitcast(U32).indirect(listed(c * CHUNK, CHUNK)))
+            nc.vector.tensor_copy(scales[:], tab_s[:].indirect(listed(c * CHUNK, CHUNK)))
+            return words, scales
+
+        gathered = {0: gather(0)}
+        wu_p = tile([P, 2 * R], U8, "wu_p")
+        wu_s = tile([P, R], U8, "wu_s")
+        nc.vector.tensor_copy(
+            wu_p[:].rearrange("p (t m b) -> p t m b", t=PACK, b=2),
+            wu_raw[:].rearrange("p (m t b) -> p t m b", t=PACK, b=2),
+        )
+        nc.vector.tensor_copy(
+            wu_s[:].rearrange("p (t m) -> p t m", t=PACK), wu_s_raw[:].rearrange("p (m t) -> p t m", t=PACK)
+        )
+
+        def up(out, c, t, first, count):
+            words, scales = gathered[c]
+            nc.tensor.matmul_mx(
+                out=out,
+                lhsT=wu_p[:, 2 * P * t : 2 * P * (t + 1)].bitcast(FP4X4),
+                lhsT_scale=wu_s[:, P * t : P * (t + 1)],
+                rhs=words[:, first : first + count].bitcast(FP8X4),
+                rhs_scale=scales[:, first : first + count],
+                start=True,
+                stop=True,
+            )
+
+        h_w = tile([P, J], U32, "h_w")
+        h_s = tile([P, J], U8, "h_s")
+
+        def quantize_h(grouped, first, count):
+            nc.vector.quantize_mx(
+                out=h_w[:, first : first + count].bitcast(FP8X4), scales=h_s[:, first : first + count], in_=grouped
+            )
+
+        first_h = []
+        for half in range(2):
+            acc = ps.tile([P, PACK, HALF], F32, name="a0_%d" % half, tag="a%d" % half)
+            for t in range(PACK):
+                up(acc[:, t, :], 0, t, half * HALF, HALF)
+            act = tile([P, HALF, PACK], F32, "act0_%d" % half)
+            nc.scalar.activation(act[:], acc[:].rearrange("p t n -> p n t"), GELU)
+            grouped = tile([P, HALF, PACK], BF16, "h0_%d" % half)
+            nc.vector.tensor_tensor(grouped[:], act[:], sm_t[:].unsqueeze(1).to_broadcast([P, HALF, PACK]), MULT)
+            first_h.append(grouped)
+        for half in range(2):
+            quantize_h(first_h[half][:].rearrange("p n t -> p (n t)"), half * HALF, HALF)
+
+        wd_p = tile([P, N], I32, "wd_p")
+        wd_s = tile([P, N], U8, "wd_s")
+        nc.vector.tensor_copy(
+            wd_p[:].rearrange("p (t m) -> p t m", t=PACK), wd_raw[:].rearrange("p (m t) -> p t m", t=PACK)
+        )
+        nc.vector.tensor_copy(
+            wd_s[:].rearrange("p (t m) -> p t m", t=PACK), wd_s_raw[:].rearrange("p (m t) -> p t m", t=PACK)
+        )
+        gathered[1] = gather(1)
+        gathered[2] = gather(2)
+        gathered[3] = gather(3, "act0_0", "act0_1")
+
+        def hidden(c):
+            pairs = tile([P, 2, CHUNK, 2], BF16, "pairs%d" % c)
+            for u in range(2):
+                acc = ps.tile([P, 2, CHUNK], F32, name="a%d_%d" % (c, u), tag="ab"[c % 2] + str(u))
+                for e in range(2):
+                    up(acc[:, e, :], c, 2 * u + e, 0, CHUNK)
+                act = tile([P, 2, CHUNK], F32, "act%d_%d" % (c, u))
+                nc.scalar.activation(act[:], acc[:], GELU)
+                for e in range(2):
+                    t = 2 * u + e
+                    nc.scalar.activation(pairs[:, u, :, e], act[:, e, :], COPY, scale=sm_t[:, t : t + 1])
+            grouped = tile([P, CHUNK * PACK], BF16, "h%d" % c)
+            nc.scalar.copy(
+                grouped[:].bitcast(F32).rearrange("p (n u) -> p n u", u=2),
+                pairs[:].rearrange("p u n e -> p (u n e)").bitcast(F32).rearrange("p (u n) -> p n u", u=2),
+            )
+            quantize_h(grouped[:], c * CHUNK, CHUNK)
+
+        def down(y, t, first, count, bank):
+            acc = ps.tile([P, count], F32, name="y%d_%d" % (t, first), tag=bank)
+            nc.tensor.matmul_mx(
+                out=acc[:],
+                lhsT=wd_p[:, P * t : P * (t + 1)].bitcast(FP8X4),
+                lhsT_scale=wd_s[:, P * t : P * (t + 1)],
+                rhs=h_w[:, first : first + count].bitcast(FP8X4),
+                rhs_scale=h_s[:, first : first + count],
+                start=True,
+                stop=True,
+            )
+            nc.scalar.copy(y, acc[:])
+
+        def scatter(page, y, first, count):
+            nc.vector.tensor_tensor(page[:].indirect(listed(first, count)), y, wgo_t[:, first : first + count], MULT)
+
+        pages = [tile([P, T], F32, "page%d" % t) for t in range(2)]
+        for page in pages:
+            nc.vector.memset(page[:], 0.0)
+
+        for c in range(CHUNKS):
+            y = tile([P, CHUNK], F32, "y0_%d" % c)
+            down(y[:], 0, c * CHUNK, CHUNK, "y%d" % (c % 2))
+            scatter(pages[0], y[:], c * CHUNK, CHUNK)
+            if c + 1 < CHUNKS:
+                hidden(c + 1)
+            y = tile([P, CHUNK], F32, "y1_%d" % c, "pairs%d" % (c + 1))
+            down(y[:], 1, c * CHUNK, CHUNK, "y%d" % (2 + c % 2))
+            scatter(pages[1], y[:], c * CHUNK, CHUNK)
+
+        for t, tag, banks in ((2, "h3", ("a0", "a1")), (3, "pairs3", ("y1", "y3"))):
+            page = tile([P, T], F32, "page%d" % t, tag)
+            nc.gpsimd.memset(page[:], 0.0)
+            pages.append(page)
+            y = tile([P, J], F32, "y%d" % t)
+            for half in range(2):
+                down(y[:, half * BANK : (half + 1) * BANK], t, half * BANK, BANK, banks[half])
+            scatter(page, y[:], 0, J)
+
+        out_rows = out_0.rearrange("(p t) n -> p t n", t=PACK)
+        out_pairs = [tile([P, 2, QUARTER, 2], BF16, "out_pairs%d" % c) for c in range(4)]
+        for t in range(3):
+            nc.sync.dma_start(out=out_rows[:, t, :], in_=pages[t][:])
+            for c in range(4):
+                cols = pages[t][:, c * QUARTER : (c + 1) * QUARTER]
+                if t == 2 and c < 2:
+                    nc.scalar.copy(out_pairs[c][:, 1, :, :], cols.unsqueeze(2).to_broadcast([P, QUARTER, 2]))
+                else:
+                    nc.scalar.copy(out_pairs[c][:, t // 2, :, t % 2], cols)
+        nc.sync.dma_start(out=out_rows[:, 3, :], in_=pages[3][:])
+
+        out_s = tile([P, QUARTER], U8, "out_s")
+        out_words = out_1[0].rearrange("p t i -> p (t i)")
+        groups = [tile([P, QUARTER * PACK], BF16, "out_grouped%d" % c) for c in range(4)]
+
+        def interleave(copy, c):
+            copy(
+                groups[c][:].bitcast(F32).rearrange("p (n u) -> p n u", u=2),
+                out_pairs[c][:].rearrange("p u n e -> p (u n e)").bitcast(F32).rearrange("p (u n) -> p n u", u=2),
+            )
+
+        for c in range(2):
+            nc.vector.tensor_copy(out_pairs[c][:, 1, :, 1], pages[3][:, c * QUARTER : (c + 1) * QUARTER])
+        for c in range(2):
+            interleave(nc.vector.tensor_copy, c)
+        for c in range(2, 4):
+            nc.scalar.copy(out_pairs[c][:, 1, :, 1], pages[3][:, c * QUARTER : (c + 1) * QUARTER])
+            interleave(nc.scalar.copy, c)
+        for c in range(4):
+            codes = tile([P, QUARTER], U32, "out_w%d" % c)
+            nc.vector.quantize_mx(out=codes[:].bitcast(FP8X4), scales=out_s[4 * c : P, :], in_=groups[c][:])
+            nc.sync.dma_start(
+                out=out_words[:, PACK * QUARTER * c : PACK * QUARTER * (c + 1)].bitcast(I32), in_=codes[:].bitcast(I32)
+            )
+        for q in range(QUADS):
+            queue = nc.scalar if q % 2 else nc.sync
+            queue.dma_start(
+                out=out_2[0, 4 * q : 4 * q + 4, :].rearrange("r (c n) -> c r n", c=4).bitcast(I32),
+                in_=out_s[32 * q : 32 * q + 16, :].bitcast(I32),
+            )

@@ -50,24 +50,19 @@ def tile_list_modp_gelu_noneP_kernel(
         tab_s = tile([P, T], U8, "tab_s")
         wu_s_raw = tile([P, R], U8, "wu_s_raw")
         wd_s_raw = tile([P, N], U8, "wd_s_raw")
-        for plane in (tab_s, wu_s_raw, wd_s_raw):
+        for plane in (wu_s_raw, tab_s, wd_s_raw):
             nc.vector.memset(plane[:].bitcast(I32), 0)
 
         tab_w = tile([P, T], I32, "tab_w")
         wu_raw = tile([P, 2 * R], U8, "wu_raw")
-        wd_raw = tile([P, N], I32, "wd_raw")
         sm_t = tile([P, PACK], F32, "sm_t")
-        wgo_t = tile([P, J], F32, "wgo_t")
-        for q in range(QUADS):
-            scale_rows(tab_s, tab_scales, q, nc.sync)
-        scale_rows(wu_s_raw, wu_scales, 0, nc.sync)
-        nc.sync.dma_start(out=tab_w[:], in_=tab_words[0].rearrange("p t i -> p (t i)").bitcast(I32))
         nc.sync.dma_start(out=wu_raw[:].bitcast(I32), in_=wu_words[0].bitcast(I32))
-        for q in range(1, QUADS):
-            scale_rows(wu_s_raw, wu_scales, q, nc.scalar)
-        nc.sync.dma_start(out=sm_t[:], in_=sm.rearrange("(p t) -> p t", t=PACK))
-        nc.sync.dma_start(out=wd_raw[:], in_=wd_words[0].rearrange("p n i -> p (n i)").bitcast(I32))
-        nc.sync.dma_start(out=wgo_t[:], in_=wgo)
+        nc.sync.dma_start(out=tab_w[:], in_=tab_words[0].rearrange("p t i -> p (t i)").bitcast(I32))
+        for q in range(QUADS):
+            scale_rows(wu_s_raw, wu_scales, q, nc.gpsimd if q == QUADS - 1 else nc.scalar)
+        for q in range(QUADS):
+            scale_rows(tab_s, tab_scales, q, nc.scalar)
+        nc.gpsimd.dma_start(out=sm_t[:], in_=sm.rearrange("(p t) -> p t", t=PACK))
         for q in range(QUADS):
             scale_rows(wd_s_raw, wd_scales, q, nc.sync)
 
@@ -85,12 +80,17 @@ def tile_list_modp_gelu_noneP_kernel(
         wu_p = tile([P, 2 * R], U8, "wu_p")
         wu_s = tile([P, R], U8, "wu_s")
         nc.vector.tensor_copy(
-            wu_p[:].rearrange("p (t m b) -> p t m b", t=PACK, b=2),
-            wu_raw[:].rearrange("p (m t b) -> p t m b", t=PACK, b=2),
+            wu_p[:].rearrange("p (t m b) -> p m t b", t=PACK, b=2),
+            wu_raw[:].rearrange("p (m t b) -> p m t b", t=PACK, b=2),
         )
         nc.vector.tensor_copy(
-            wu_s[:].rearrange("p (t m) -> p t m", t=PACK), wu_s_raw[:].rearrange("p (m t) -> p t m", t=PACK)
+            wu_s[:].rearrange("p (t m) -> p m t", t=PACK), wu_s_raw[:].rearrange("p (m t) -> p m t", t=PACK)
         )
+
+        wd_raw = tile([P, N], I32, "wd_raw", "wu_raw")
+        nc.sync.dma_start(out=wd_raw[:], in_=wd_words[0].rearrange("p n i -> p (n i)").bitcast(I32))
+        wgo_t = tile([P, J], F32, "wgo_t", "wu_s_raw")
+        nc.sync.dma_start(out=wgo_t[:], in_=wgo)
 
         def up(out, c, t, first, count):
             words, scales = gathered[c]
@@ -128,13 +128,13 @@ def tile_list_modp_gelu_noneP_kernel(
         wd_p = tile([P, N], I32, "wd_p")
         wd_s = tile([P, N], U8, "wd_s")
         nc.vector.tensor_copy(
-            wd_p[:].rearrange("p (t m) -> p t m", t=PACK), wd_raw[:].rearrange("p (m t) -> p t m", t=PACK)
+            wd_p[:].rearrange("p (t m) -> p m t", t=PACK), wd_raw[:].rearrange("p (m t) -> p m t", t=PACK)
         )
         nc.vector.tensor_copy(
-            wd_s[:].rearrange("p (t m) -> p t m", t=PACK), wd_s_raw[:].rearrange("p (m t) -> p t m", t=PACK)
+            wd_s[:].rearrange("p (t m) -> p m t", t=PACK), wd_s_raw[:].rearrange("p (m t) -> p m t", t=PACK)
         )
         gathered[1] = gather(1)
-        gathered[2] = gather(2)
+        gathered[2] = gather(2, "gw0", "gs0")
         gathered[3] = gather(3, "act0_0", "act0_1")
 
         def hidden(c):
@@ -173,7 +173,8 @@ def tile_list_modp_gelu_noneP_kernel(
 
         pages = [tile([P, T], F32, "page%d" % t) for t in range(2)]
         for page in pages:
-            nc.vector.memset(page[:], 0.0)
+            nc.vector.memset(page[:, : T // 2], 0.0)
+            nc.vector.memset(page[:, T // 2 :], 0.0)
 
         for c in range(CHUNKS):
             y = tile([P, CHUNK], F32, "y0_%d" % c)

@@ -57,12 +57,12 @@ def tile_list_modp_gelu_noneP_kernel(
         wu_raw = tile([P, 2 * R], U8, "wu_raw")
         sm_t = tile([P, PACK], F32, "sm_t")
         nc.sync.dma_start(out=wu_raw[:].bitcast(I32), in_=wu_words[0].bitcast(I32))
+        nc.sync.dma_start(out=sm_t[:], in_=sm.rearrange("(p t) -> p t", t=PACK))
         nc.sync.dma_start(out=tab_w[:], in_=tab_words[0].rearrange("p t i -> p (t i)").bitcast(I32))
         for q in range(QUADS):
-            scale_rows(wu_s_raw, wu_scales, q, nc.gpsimd if q == QUADS - 1 else nc.scalar)
+            scale_rows(wu_s_raw, wu_scales, q, nc.scalar)
         for q in range(QUADS):
             scale_rows(tab_s, tab_scales, q, nc.scalar)
-        nc.gpsimd.dma_start(out=sm_t[:], in_=sm.rearrange("(p t) -> p t", t=PACK))
         for q in range(QUADS):
             scale_rows(wd_s_raw, wd_scales, q, nc.sync)
 
@@ -80,11 +80,11 @@ def tile_list_modp_gelu_noneP_kernel(
         wu_p = tile([P, 2 * R], U8, "wu_p")
         wu_s = tile([P, R], U8, "wu_s")
         nc.vector.tensor_copy(
-            wu_p[:].rearrange("p (t m b) -> p m t b", t=PACK, b=2),
-            wu_raw[:].rearrange("p (m t b) -> p m t b", t=PACK, b=2),
+            wu_p[:].rearrange("p (t m b) -> p t m b", t=PACK, b=2),
+            wu_raw[:].rearrange("p (m t b) -> p t m b", t=PACK, b=2),
         )
         nc.vector.tensor_copy(
-            wu_s[:].rearrange("p (t m) -> p m t", t=PACK), wu_s_raw[:].rearrange("p (m t) -> p m t", t=PACK)
+            wu_s[:].rearrange("p (t m) -> p t m", t=PACK), wu_s_raw[:].rearrange("p (m t) -> p t m", t=PACK)
         )
 
         wd_raw = tile([P, N], I32, "wd_raw", "wu_raw")
@@ -112,31 +112,6 @@ def tile_list_modp_gelu_noneP_kernel(
                 out=h_w[:, first : first + count].bitcast(FP8X4), scales=h_s[:, first : first + count], in_=grouped
             )
 
-        first_h = []
-        for half in range(2):
-            acc = ps.tile([P, PACK, HALF], F32, name="a0_%d" % half, tag="a%d" % half)
-            for t in range(PACK):
-                up(acc[:, t, :], 0, t, half * HALF, HALF)
-            act = tile([P, HALF, PACK], F32, "act0_%d" % half)
-            nc.scalar.activation(act[:], acc[:].rearrange("p t n -> p n t"), GELU)
-            grouped = tile([P, HALF, PACK], BF16, "h0_%d" % half)
-            nc.vector.tensor_tensor(grouped[:], act[:], sm_t[:].unsqueeze(1).to_broadcast([P, HALF, PACK]), MULT)
-            first_h.append(grouped)
-        for half in range(2):
-            quantize_h(first_h[half][:].rearrange("p n t -> p (n t)"), half * HALF, HALF)
-
-        wd_p = tile([P, N], I32, "wd_p")
-        wd_s = tile([P, N], U8, "wd_s")
-        nc.vector.tensor_copy(
-            wd_p[:].rearrange("p (t m) -> p m t", t=PACK), wd_raw[:].rearrange("p (m t) -> p m t", t=PACK)
-        )
-        nc.vector.tensor_copy(
-            wd_s[:].rearrange("p (t m) -> p m t", t=PACK), wd_s_raw[:].rearrange("p (m t) -> p m t", t=PACK)
-        )
-        gathered[1] = gather(1)
-        gathered[2] = gather(2, "gw0", "gs0")
-        gathered[3] = gather(3, "act0_0", "act0_1")
-
         def hidden(c):
             pairs = tile([P, 2, CHUNK, 2], BF16, "pairs%d" % c)
             for u in range(2):
@@ -155,6 +130,15 @@ def tile_list_modp_gelu_noneP_kernel(
             )
             quantize_h(grouped[:], c * CHUNK, CHUNK)
 
+        wd_p = tile([P, N], I32, "wd_p")
+        wd_s = tile([P, N], U8, "wd_s")
+        nc.vector.tensor_copy(
+            wd_p[:].rearrange("p (t m i) -> p m t i", t=PACK, i=4), wd_raw[:].rearrange("p (m i t) -> p m t i", t=PACK, i=4)
+        )
+        nc.vector.tensor_copy(
+            wd_s[:].rearrange("p (t m) -> p t m", t=PACK), wd_s_raw[:].rearrange("p (m t) -> p t m", t=PACK)
+        )
+
         def down(y, t, first, count, bank):
             acc = ps.tile([P, count], F32, name="y%d_%d" % (t, first), tag=bank)
             nc.tensor.matmul_mx(
@@ -171,64 +155,77 @@ def tile_list_modp_gelu_noneP_kernel(
         def scatter(page, y, first, count):
             nc.vector.tensor_tensor(page[:].indirect(listed(first, count)), y, wgo_t[:, first : first + count], MULT)
 
-        pages = [tile([P, T], F32, "page%d" % t) for t in range(2)]
+        pages = [tile([P, T], F32, "page%d" % t) for t in range(PACK)]
+        gathered[1] = gather(1)
+        hidden(0)
+        gathered[2] = gather(2, "gw0", "gs0")
+        gathered[3] = gather(3, "h0", "pairs0")
         for page in pages:
             nc.vector.memset(page[:, : T // 2], 0.0)
             nc.vector.memset(page[:, T // 2 :], 0.0)
 
+        def place(t, c, bank, after=None):
+            y = tile([P, CHUNK], F32, "y%d_%d" % (t, c), after)
+            down(y[:], t, c * CHUNK, CHUNK, bank)
+            scatter(pages[t], y[:], c * CHUNK, CHUNK)
+
         for c in range(CHUNKS):
-            y = tile([P, CHUNK], F32, "y0_%d" % c)
-            down(y[:], 0, c * CHUNK, CHUNK, "y%d" % (c % 2))
-            scatter(pages[0], y[:], c * CHUNK, CHUNK)
+            early = range(3 if c < 2 else 2)
+            for t in early[:-1]:
+                place(t, c, "y%d" % t)
             if c + 1 < CHUNKS:
                 hidden(c + 1)
-            y = tile([P, CHUNK], F32, "y1_%d" % c, "pairs%d" % (c + 1))
-            down(y[:], 1, c * CHUNK, CHUNK, "y%d" % (2 + c % 2))
-            scatter(pages[1], y[:], c * CHUNK, CHUNK)
+            place(early[-1], c, "y2", "pairs%d" % (c + 1))
 
-        for t, tag, banks in ((2, "h3", ("a0", "a1")), (3, "pairs3", ("y1", "y3"))):
-            page = tile([P, T], F32, "page%d" % t, tag)
-            nc.gpsimd.memset(page[:], 0.0)
-            pages.append(page)
-            y = tile([P, J], F32, "y%d" % t)
-            for half in range(2):
-                down(y[:, half * BANK : (half + 1) * BANK], t, half * BANK, BANK, banks[half])
-            scatter(page, y[:], 0, J)
+        y = tile([P, BANK], F32, "y2_rest")
+        down(y[:], 2, BANK, BANK, "y1")
+        scatter(pages[2], y[:], BANK, BANK)
+        y = tile([P, J], F32, "y3")
+        for half, bank in enumerate(("y2", "y1")):
+            down(y[:, half * BANK : (half + 1) * BANK], 3, half * BANK, BANK, bank)
+        scatter(pages[3], y[:], 0, J)
 
         out_rows = out_0.rearrange("(p t) n -> p t n", t=PACK)
-        out_pairs = [tile([P, 2, QUARTER, 2], BF16, "out_pairs%d" % c) for c in range(4)]
+        out_words = out_1[0].rearrange("p t i -> p (t i)")
+        pieces = [(0, QUARTER), (QUARTER, QUARTER), (2 * QUARTER, QUARTER), (3 * QUARTER, CHUNK), (T - CHUNK, CHUNK)]
+        out_pairs = [tile([P, 2, count, 2], BF16, "out_pairs%d" % first) for first, count in pieces]
+        groups = [tile([P, count * PACK], BF16, "out_grouped%d" % first) for first, count in pieces]
         for t in range(3):
             nc.sync.dma_start(out=out_rows[:, t, :], in_=pages[t][:])
-            for c in range(4):
-                cols = pages[t][:, c * QUARTER : (c + 1) * QUARTER]
-                if t == 2 and c < 2:
-                    nc.scalar.copy(out_pairs[c][:, 1, :, :], cols.unsqueeze(2).to_broadcast([P, QUARTER, 2]))
+            for i, (first, count) in enumerate(pieces):
+                cols = pages[t][:, first : first + count]
+                if t == 2 and i < 2:
+                    nc.scalar.copy(out_pairs[i][:, 1, :, :], cols.unsqueeze(2).to_broadcast([P, count, 2]))
                 else:
-                    nc.scalar.copy(out_pairs[c][:, t // 2, :, t % 2], cols)
+                    nc.scalar.copy(out_pairs[i][:, t // 2, :, t % 2], cols)
         nc.sync.dma_start(out=out_rows[:, 3, :], in_=pages[3][:])
 
-        out_s = tile([P, QUARTER], U8, "out_s")
-        out_words = out_1[0].rearrange("p t i -> p (t i)")
-        groups = [tile([P, QUARTER * PACK], BF16, "out_grouped%d" % c) for c in range(4)]
+        def last_plane(copy, i):
+            first, count = pieces[i]
+            copy(out_pairs[i][:, 1, :, 1], pages[3][:, first : first + count])
 
-        def interleave(copy, c):
+        def interleave(copy, i):
             copy(
-                groups[c][:].bitcast(F32).rearrange("p (n u) -> p n u", u=2),
-                out_pairs[c][:].rearrange("p u n e -> p (u n e)").bitcast(F32).rearrange("p (u n) -> p n u", u=2),
+                groups[i][:].bitcast(F32).rearrange("p (n u) -> p n u", u=2),
+                out_pairs[i][:].rearrange("p u n e -> p (u n e)").bitcast(F32).rearrange("p (u n) -> p n u", u=2),
             )
 
-        for c in range(2):
-            nc.vector.tensor_copy(out_pairs[c][:, 1, :, 1], pages[3][:, c * QUARTER : (c + 1) * QUARTER])
-        for c in range(2):
-            interleave(nc.vector.tensor_copy, c)
-        for c in range(2, 4):
-            nc.scalar.copy(out_pairs[c][:, 1, :, 1], pages[3][:, c * QUARTER : (c + 1) * QUARTER])
-            interleave(nc.scalar.copy, c)
-        for c in range(4):
-            codes = tile([P, QUARTER], U32, "out_w%d" % c)
-            nc.vector.quantize_mx(out=codes[:].bitcast(FP8X4), scales=out_s[4 * c : P, :], in_=groups[c][:])
+        for i in range(2):
+            last_plane(nc.vector.tensor_copy, i)
+        for i in range(2):
+            interleave(nc.vector.tensor_copy, i)
+        for i in range(2, len(pieces)):
+            last_plane(nc.scalar.copy, i)
+            interleave(nc.scalar.copy, i)
+        out_s = tile([P, QUARTER], U8, "out_s")
+        for i, (first, count) in enumerate(pieces):
+            codes = tile([P, count], U32, "out_w%d" % first)
+            quarter, col = divmod(first, QUARTER)
+            nc.vector.quantize_mx(
+                out=codes[:].bitcast(FP8X4), scales=out_s[4 * quarter : P, col : col + count], in_=groups[i][:]
+            )
             nc.sync.dma_start(
-                out=out_words[:, PACK * QUARTER * c : PACK * QUARTER * (c + 1)].bitcast(I32), in_=codes[:].bitcast(I32)
+                out=out_words[:, PACK * first : PACK * (first + count)].bitcast(I32), in_=codes[:].bitcast(I32)
             )
         for q in range(QUADS):
             queue = nc.scalar if q % 2 else nc.sync

@@ -48,35 +48,34 @@ def tile_list_modp_gelu_noneP_kernel(
         nc.sync.dma_start(offsets[:], offs)
 
         tab_s = tile([P, T], U8, "tab_s")
+        nc.gpsimd.memset(tab_s[:].bitcast(I32), 0)
+        zeros = tile([P, R // 4], I32, "zeros")
+        nc.gpsimd.memset(zeros[:], 0)
         wu_s_raw = tile([P, R], U8, "wu_s_raw")
-        wd_s_raw = tile([P, N], U8, "wd_s_raw")
-        for plane in (wu_s_raw, tab_s, wd_s_raw):
-            nc.vector.memset(plane[:].bitcast(I32), 0)
+        nc.gpsimd.tensor_copy(wu_s_raw[:].bitcast(I32), zeros[:])
 
-        tab_w = tile([P, T], I32, "tab_w")
         wu_raw = tile([P, 2 * R], U8, "wu_raw")
         sm_t = tile([P, PACK], F32, "sm_t")
         nc.sync.dma_start(out=wu_raw[:].bitcast(I32), in_=wu_words[0].bitcast(I32))
         nc.sync.dma_start(out=sm_t[:], in_=sm.rearrange("(p t) -> p t", t=PACK))
-        nc.sync.dma_start(out=tab_w[:], in_=tab_words[0].rearrange("p t i -> p (t i)").bitcast(I32))
+        for q in range(QUADS):
+            scale_rows(tab_s, tab_scales, q, nc.sync)
+        tab_w = tile([P, T], I32, "tab_w", "zeros")
+        nc.scalar.dma_start(out=tab_w[:], in_=tab_words[0].rearrange("p t i -> p (t i)").bitcast(I32))
         for q in range(QUADS):
             scale_rows(wu_s_raw, wu_scales, q, nc.scalar)
-        for q in range(QUADS):
-            scale_rows(tab_s, tab_scales, q, nc.scalar)
-        for q in range(QUADS):
-            scale_rows(wd_s_raw, wd_scales, q, nc.sync)
 
         def listed(first, count):
             return offsets[:, first // 16 : (first + count) // 16]
 
-        def gather(c, words_tag=None, scales_tag=None):
+        def gather(c, words_tag=None):
             words = tile([P, CHUNK], U32, "gw%d" % c, words_tag)
-            scales = tile([P, CHUNK], U8, "gs%d" % c, scales_tag)
             nc.vector.tensor_copy(words[:], tab_w[:].bitcast(U32).indirect(listed(c * CHUNK, CHUNK)))
-            nc.vector.tensor_copy(scales[:], tab_s[:].indirect(listed(c * CHUNK, CHUNK)))
-            return words, scales
+            return words
 
         gathered = {0: gather(0)}
+        gathered_s = tile([P, J], U8, "gs")
+        nc.vector.tensor_copy(gathered_s[:], tab_s[:].indirect(offsets[:]))
         wu_p = tile([P, 2 * R], U8, "wu_p")
         wu_s = tile([P, R], U8, "wu_s")
         nc.vector.tensor_copy(
@@ -87,19 +86,19 @@ def tile_list_modp_gelu_noneP_kernel(
             wu_s[:].rearrange("p (t m) -> p t m", t=PACK), wu_s_raw[:].rearrange("p (m t) -> p t m", t=PACK)
         )
 
-        wd_raw = tile([P, N], I32, "wd_raw", "wu_raw")
-        nc.sync.dma_start(out=wd_raw[:], in_=wd_words[0].rearrange("p n i -> p (n i)").bitcast(I32))
-        wgo_t = tile([P, J], F32, "wgo_t", "wu_s_raw")
-        nc.sync.dma_start(out=wgo_t[:], in_=wgo)
+        wd_s_raw = tile([P, N], U8, "wd_s_raw", "wu_raw")
+        nc.gpsimd.memset(wd_s_raw[:].bitcast(I32), 0)
+        for q in range(QUADS):
+            scale_rows(wd_s_raw, wd_scales, q, nc.sync)
 
         def up(out, c, t, first, count):
-            words, scales = gathered[c]
+            words = gathered[c]
             nc.tensor.matmul_mx(
                 out=out,
                 lhsT=wu_p[:, 2 * P * t : 2 * P * (t + 1)].bitcast(FP4X4),
                 lhsT_scale=wu_s[:, P * t : P * (t + 1)],
                 rhs=words[:, first : first + count].bitcast(FP8X4),
-                rhs_scale=scales[:, first : first + count],
+                rhs_scale=gathered_s[:, c * CHUNK + first : c * CHUNK + first + count],
                 start=True,
                 stop=True,
             )
@@ -130,15 +129,6 @@ def tile_list_modp_gelu_noneP_kernel(
             )
             quantize_h(grouped[:], c * CHUNK, CHUNK)
 
-        wd_p = tile([P, N], I32, "wd_p")
-        wd_s = tile([P, N], U8, "wd_s")
-        nc.vector.tensor_copy(
-            wd_p[:].rearrange("p (t m i) -> p m t i", t=PACK, i=4), wd_raw[:].rearrange("p (m i t) -> p m t i", t=PACK, i=4)
-        )
-        nc.vector.tensor_copy(
-            wd_s[:].rearrange("p (t m) -> p t m", t=PACK), wd_s_raw[:].rearrange("p (m t) -> p t m", t=PACK)
-        )
-
         def down(y, t, first, count, bank):
             acc = ps.tile([P, count], F32, name="y%d_%d" % (t, first), tag=bank)
             nc.tensor.matmul_mx(
@@ -155,14 +145,47 @@ def tile_list_modp_gelu_noneP_kernel(
         def scatter(page, y, first, count):
             nc.vector.tensor_tensor(page[:].indirect(listed(first, count)), y, wgo_t[:, first : first + count], MULT)
 
-        pages = [tile([P, T], F32, "page%d" % t) for t in range(PACK)]
-        gathered[1] = gather(1)
-        hidden(0)
-        gathered[2] = gather(2, "gw0", "gs0")
-        gathered[3] = gather(3, "h0", "pairs0")
-        for page in pages:
-            nc.vector.memset(page[:, : T // 2], 0.0)
-            nc.vector.memset(page[:, T // 2 :], 0.0)
+        first_h = []
+        for half in range(2):
+            acc = ps.tile([P, PACK, HALF], F32, name="a0_%d" % half, tag="a%d" % half)
+            for t in range(PACK):
+                up(acc[:, t, :], 0, t, half * HALF, HALF)
+            act = tile([P, HALF, PACK], F32, "act0_%d" % half)
+            nc.scalar.activation(act[:], acc[:].rearrange("p t n -> p n t"), GELU)
+            grouped = tile([P, HALF, PACK], BF16, "h0_%d" % half)
+            nc.vector.tensor_tensor(grouped[:], act[:], sm_t[:].unsqueeze(1).to_broadcast([P, HALF, PACK]), MULT)
+            first_h.append(grouped)
+        for half in range(2):
+            quantize_h(first_h[half][:].rearrange("p n t -> p (n t)"), half * HALF, HALF)
+
+        wd_raw = tile([P, N], I32, "wd_raw", "tab_s")
+        nc.sync.dma_start(out=wd_raw[:], in_=wd_words[0].rearrange("p n i -> p (n i)").bitcast(I32))
+        wd_p = tile([P, N], I32, "wd_p")
+        wd_s = tile([P, N], U8, "wd_s")
+        nc.vector.tensor_copy(
+            wd_p[:].rearrange("p (t m i) -> p m t i", t=PACK, i=4), wd_raw[:].rearrange("p (m i t) -> p m t i", t=PACK, i=4)
+        )
+        nc.vector.tensor_copy(
+            wd_s[:].rearrange("p (t m) -> p t m", t=PACK), wd_s_raw[:].rearrange("p (m t) -> p t m", t=PACK)
+        )
+
+        wgo_t = tile([P, J], F32, "wgo_t", "gw0")
+        nc.sync.dma_start(out=wgo_t[:], in_=wgo)
+        gathered[1] = gather(1, "wu_s_raw")
+        gathered[2] = gather(2, "act0_1")
+        gathered[3] = gather(3, "h0_0")
+
+        pages = []
+
+        def new_page(after=None):
+            page = tile([P, T], F32, "page%d" % len(pages), after)
+            nc.gpsimd.memset(page[:, : T // 2], 0.0)
+            nc.gpsimd.memset(page[:, T // 2 :], 0.0)
+            pages.append(page)
+
+        new_page()
+        new_page()
+        new_page("zeros")
 
         def place(t, c, bank, after=None):
             y = tile([P, CHUNK], F32, "y%d_%d" % (t, c), after)
@@ -170,16 +193,18 @@ def tile_list_modp_gelu_noneP_kernel(
             scatter(pages[t], y[:], c * CHUNK, CHUNK)
 
         for c in range(CHUNKS):
-            early = range(3 if c < 2 else 2)
+            early = range(3 if c == 0 else 2)
             for t in early[:-1]:
                 place(t, c, "y%d" % t)
             if c + 1 < CHUNKS:
                 hidden(c + 1)
             place(early[-1], c, "y2", "pairs%d" % (c + 1))
 
-        y = tile([P, BANK], F32, "y2_rest")
-        down(y[:], 2, BANK, BANK, "y1")
-        scatter(pages[2], y[:], BANK, BANK)
+        y = tile([P, J - CHUNK], F32, "y2_rest")
+        down(y[:, :CHUNK], 2, CHUNK, CHUNK, "b0")
+        down(y[:, CHUNK:], 2, BANK, BANK, "y1")
+        scatter(pages[2], y[:], CHUNK, J - CHUNK)
+        new_page("h1")
         y = tile([P, J], F32, "y3")
         for half, bank in enumerate(("y2", "y1")):
             down(y[:, half * BANK : (half + 1) * BANK], 3, half * BANK, BANK, bank)

@@ -47,10 +47,10 @@ def tile_list_modp_gelu_noneP_kernel(
         offsets = sb.tile([P, J // 16], U16, name="offsets")
         nc.sync.dma_start(offsets[:], offs)
 
-        tab_s = tile([P, T], U8, "tab_s")
-        nc.gpsimd.memset(tab_s[:].bitcast(I32), 0)
         zeros = tile([P, R // 4], I32, "zeros")
         nc.gpsimd.memset(zeros[:], 0)
+        tab_s = tile([P, T], U8, "tab_s")
+        nc.gpsimd.memset(tab_s[:].bitcast(I32), 0)
         wu_s_raw = tile([P, R], U8, "wu_s_raw")
         nc.gpsimd.tensor_copy(wu_s_raw[:].bitcast(I32), zeros[:])
 
@@ -59,7 +59,7 @@ def tile_list_modp_gelu_noneP_kernel(
         nc.sync.dma_start(out=wu_raw[:].bitcast(I32), in_=wu_words[0].bitcast(I32))
         nc.sync.dma_start(out=sm_t[:], in_=sm.rearrange("(p t) -> p t", t=PACK))
         for q in range(QUADS):
-            scale_rows(tab_s, tab_scales, q, nc.sync)
+            scale_rows(tab_s, tab_scales, q, nc.scalar if q % 2 else nc.sync)
         tab_w = tile([P, T], I32, "tab_w", "zeros")
         nc.scalar.dma_start(out=tab_w[:], in_=tab_words[0].rearrange("p t i -> p (t i)").bitcast(I32))
         for q in range(QUADS):
@@ -111,22 +111,25 @@ def tile_list_modp_gelu_noneP_kernel(
                 out=h_w[:, first : first + count].bitcast(FP8X4), scales=h_s[:, first : first + count], in_=grouped
             )
 
-        def hidden(c):
-            pairs = tile([P, 2, CHUNK, 2], BF16, "pairs%d" % c)
+        def up_chunk(c):
+            sums = []
             for u in range(2):
                 acc = ps.tile([P, 2, CHUNK], F32, name="a%d_%d" % (c, u), tag="ab"[c % 2] + str(u))
                 for e in range(2):
                     up(acc[:, e, :], c, 2 * u + e, 0, CHUNK)
+                sums.append(acc)
+            return sums
+
+        def hidden(c, sums):
+            pairs = tile([P, PACK, CHUNK], BF16, "pairs%d" % c)
+            for u, acc in enumerate(sums):
                 act = tile([P, 2, CHUNK], F32, "act%d_%d" % (c, u))
                 nc.scalar.activation(act[:], acc[:], GELU)
                 for e in range(2):
                     t = 2 * u + e
-                    nc.scalar.activation(pairs[:, u, :, e], act[:, e, :], COPY, scale=sm_t[:, t : t + 1])
+                    nc.scalar.activation(pairs[:, t, :], act[:, e, :], COPY, scale=sm_t[:, t : t + 1])
             grouped = tile([P, CHUNK * PACK], BF16, "h%d" % c)
-            nc.scalar.copy(
-                grouped[:].bitcast(F32).rearrange("p (n u) -> p n u", u=2),
-                pairs[:].rearrange("p u n e -> p (u n e)").bitcast(F32).rearrange("p (u n) -> p n u", u=2),
-            )
+            nc.scalar.copy(grouped[:].rearrange("p (n t) -> p n t", t=PACK), pairs[:].rearrange("p t n -> p n t"))
             quantize_h(grouped[:], c * CHUNK, CHUNK)
 
         def down(y, t, first, count, bank):
@@ -160,8 +163,8 @@ def tile_list_modp_gelu_noneP_kernel(
 
         wd_raw = tile([P, N], I32, "wd_raw", "tab_s")
         nc.sync.dma_start(out=wd_raw[:], in_=wd_words[0].rearrange("p n i -> p (n i)").bitcast(I32))
-        wd_p = tile([P, N], I32, "wd_p")
-        wd_s = tile([P, N], U8, "wd_s")
+        wd_p = tile([P, N], I32, "wd_p", "gw0")
+        wd_s = tile([P, N], U8, "wd_s", "act0_0")
         nc.vector.tensor_copy(
             wd_p[:].rearrange("p (t m i) -> p m t i", t=PACK, i=4), wd_raw[:].rearrange("p (m i t) -> p m t i", t=PACK, i=4)
         )
@@ -169,46 +172,41 @@ def tile_list_modp_gelu_noneP_kernel(
             wd_s[:].rearrange("p (t m) -> p t m", t=PACK), wd_s_raw[:].rearrange("p (m t) -> p t m", t=PACK)
         )
 
-        wgo_t = tile([P, J], F32, "wgo_t", "gw0")
-        nc.sync.dma_start(out=wgo_t[:], in_=wgo)
         gathered[1] = gather(1, "wu_s_raw")
         gathered[2] = gather(2, "act0_1")
         gathered[3] = gather(3, "h0_0")
 
-        pages = []
-
-        def new_page(after=None):
-            page = tile([P, T], F32, "page%d" % len(pages), after)
-            nc.gpsimd.memset(page[:, : T // 2], 0.0)
-            nc.gpsimd.memset(page[:, T // 2 :], 0.0)
-            pages.append(page)
-
-        new_page()
-        new_page()
-        new_page("zeros")
+        pages = [tile([P, T], F32, "page%d" % t) for t in range(2)]
+        nc.vector.memset(pages[0][:, : T // 2 - 1], 0.0)
+        nc.vector.memset(pages[0][:, T // 2 - 1 :], 0.0)
+        nc.gpsimd.memset(pages[1][:, :QUARTER], 0.0)
+        nc.gpsimd.memset(pages[1][:, QUARTER : T // 2], 0.0)
+        nc.vector.memset(pages[1][:, T // 2 :], 0.0)
 
         def place(t, c, bank, after=None):
             y = tile([P, CHUNK], F32, "y%d_%d" % (t, c), after)
             down(y[:], t, c * CHUNK, CHUNK, bank)
             scatter(pages[t], y[:], c * CHUNK, CHUNK)
 
+        sums = up_chunk(1)
+        wgo_t = tile([P, J], F32, "wgo_t", "wu_s_raw")
+        nc.sync.dma_start(out=wgo_t[:], in_=wgo)
         for c in range(CHUNKS):
-            early = range(3 if c == 0 else 2)
-            for t in early[:-1]:
-                place(t, c, "y%d" % t)
+            place(0, c, "y0")
             if c + 1 < CHUNKS:
-                hidden(c + 1)
-            place(early[-1], c, "y2", "pairs%d" % (c + 1))
+                hidden(c + 1, sums)
+            if c + 2 < CHUNKS:
+                sums = up_chunk(c + 2)
+            place(1, c, "y1", "pairs%d" % (c + 1))
 
-        y = tile([P, J - CHUNK], F32, "y2_rest")
-        down(y[:, :CHUNK], 2, CHUNK, CHUNK, "b0")
-        down(y[:, CHUNK:], 2, BANK, BANK, "y1")
-        scatter(pages[2], y[:], CHUNK, J - CHUNK)
-        new_page("h1")
-        y = tile([P, J], F32, "y3")
-        for half, bank in enumerate(("y2", "y1")):
-            down(y[:, half * BANK : (half + 1) * BANK], 3, half * BANK, BANK, bank)
-        scatter(pages[3], y[:], 0, J)
+        for t, banks in ((2, ("b0", "y3")), (3, ("y1", "y3"))):
+            page = tile([P, T], F32, "page%d" % t, "h%d" % (t - 1))
+            nc.gpsimd.memset(page[:], 0.0)
+            pages.append(page)
+            y = tile([P, J], F32, "y%d" % t)
+            for half in range(2):
+                down(y[:, half * BANK : (half + 1) * BANK], t, half * BANK, BANK, banks[half])
+            scatter(page, y[:], 0, J)
 
         out_rows = out_0.rearrange("(p t) n -> p t n", t=PACK)
         out_words = out_1[0].rearrange("p t i -> p (t i)")

@@ -26,6 +26,8 @@ HALF = CHUNK // 2
 BANK = 512
 QUARTER = T // 4
 ALIGN = 64
+ZEROS = 32
+EARLY = 2
 
 
 def tile_list_modp_gelu_noneP_kernel(
@@ -35,61 +37,84 @@ def tile_list_modp_gelu_noneP_kernel(
     with ExitStack() as ctx:
         sb = ctx.enter_context(tc.tile_pool(name="sb", bufs=1))
         ps = ctx.enter_context(tc.psum_pool(name="ps", bufs=1))
+        head = ctx.enter_context(tc.tile_pool(name="head", bufs=1))
+
+        def placed(shape, dtype, name, offset):
+            return head.tile(shape, dtype, name=name, tag=name, align_bytes=ALIGN, offset=offset)
 
         def tile(shape, dtype, name, tag=None):
             return sb.tile(shape, dtype, name=name, tag=tag or name, align_bytes=ALIGN)
 
         def scale_rows(plane, rows, q, queue):
             queue.dma_start(
-                out=plane[32 * q : 32 * q + 4, :].bitcast(I32), in_=rows[0, 4 * q : 4 * q + 4, :].bitcast(I32)
+                out=plane[32 * q : 32 * q + 4].bitcast(I32), in_=rows[0, 4 * q : 4 * q + 4, :].bitcast(I32)
             )
 
         offsets = sb.tile([P, J // 16], U16, name="offsets")
         nc.sync.dma_start(offsets[:], offs)
 
-        zeros = tile([P, R // 4], I32, "zeros")
+        zeros = tile([P, ZEROS], I32, "zeros")
         nc.gpsimd.memset(zeros[:], 0)
         tab_s = tile([P, T], U8, "tab_s")
         nc.gpsimd.memset(tab_s[:].bitcast(I32), 0)
-        wu_s_raw = tile([P, R], U8, "wu_s_raw")
-        nc.gpsimd.tensor_copy(wu_s_raw[:].bitcast(I32), zeros[:])
+        wu_s_raw = placed([P, R], U8, "wu_s_raw", 2048)
+        nc.gpsimd.tensor_copy(
+            wu_s_raw[:].bitcast(I32).rearrange("p (a z) -> p a z", z=ZEROS),
+            zeros[:].unsqueeze(1).to_broadcast([P, R // 4 // ZEROS, ZEROS]),
+        )
 
-        wu_raw = tile([P, 2 * R], U8, "wu_raw")
-        sm_t = tile([P, PACK], F32, "sm_t")
+        wu_raw = placed([P, 2 * R], U8, "wu_raw", 0)
         nc.sync.dma_start(out=wu_raw[:].bitcast(I32), in_=wu_words[0].bitcast(I32))
-        nc.sync.dma_start(out=sm_t[:], in_=sm.rearrange("(p t) -> p t", t=PACK))
+        wd_raw = tile([P, N], I32, "wd_raw")
+        nc.sync.dma_start(out=wd_raw[:], in_=wd_words[0].rearrange("p n i -> p (n i)").bitcast(I32))
         for q in range(QUADS):
-            scale_rows(tab_s, tab_scales, q, nc.scalar if q % 2 else nc.sync)
+            scale_rows(tab_s[:], tab_scales, q, nc.scalar if q % 2 else nc.sync)
         tab_w = tile([P, T], I32, "tab_w", "zeros")
         nc.scalar.dma_start(out=tab_w[:], in_=tab_words[0].rearrange("p t i -> p (t i)").bitcast(I32))
         for q in range(QUADS):
-            scale_rows(wu_s_raw, wu_scales, q, nc.scalar)
+            scale_rows(wu_s_raw[:], wu_scales, q, nc.sync)
+
+        pages = [tile([P, T], F32, "page%d" % t) for t in range(2)]
+        nc.vector.memset(pages[0][:, : T // 2 - 1], 0.0)
+        nc.vector.memset(pages[0][:, T // 2 - 1 :], 0.0)
+        nc.gpsimd.memset(pages[1][:], 0.0)
+
+        wu_p = tile([P, 2 * R], U8, "wu_p")
+        nc.vector.tensor_copy(
+            wu_p[:].bitcast(U16).rearrange("p (t m) -> p t m", t=PACK),
+            wu_raw[:].bitcast(U16).rearrange("p (m t) -> p t m", t=PACK),
+        )
+        wd_p = tile([P, N], I32, "wd_p")
+        nc.vector.tensor_copy(
+            wd_p[:].rearrange("p (t m i) -> p m t i", t=PACK, i=4), wd_raw[:].rearrange("p (m i t) -> p m t i", t=PACK, i=4)
+        )
+        sm_t = placed([P, PACK], F32, "sm_t", 0)
+        nc.sync.dma_start(out=sm_t[:], in_=sm.rearrange("(p t) -> p t", t=PACK))
+        wd_s_raw = placed([P, N], U8, "wd_s_raw", 512)
+        nc.gpsimd.memset(wd_s_raw[:].bitcast(I32), 0)
+        for q in range(QUADS):
+            scale_rows(wd_s_raw[:], wd_scales, q, nc.sync)
+        pages.append(tile([P, T], F32, "page2", "wd_raw"))
+        nc.gpsimd.memset(pages[2][:], 0.0)
 
         def listed(first, count):
             return offsets[:, first // 16 : (first + count) // 16]
 
-        def gather(c, words_tag=None):
-            words = tile([P, CHUNK], U32, "gw%d" % c, words_tag)
+        def gather(c, words):
             nc.vector.tensor_copy(words[:], tab_w[:].bitcast(U32).indirect(listed(c * CHUNK, CHUNK)))
             return words
 
-        gathered = {0: gather(0)}
+        def deal_scales(raw, name):
+            dealt = tile([P, R], U8, name)
+            nc.vector.tensor_copy(dealt[:].rearrange("p (t m) -> p t m", t=PACK), raw.rearrange("p (m t) -> p t m", t=PACK))
+            return dealt
+
         gathered_s = tile([P, J], U8, "gs")
         nc.vector.tensor_copy(gathered_s[:], tab_s[:].indirect(offsets[:]))
-        wu_p = tile([P, 2 * R], U8, "wu_p")
-        wu_s = tile([P, R], U8, "wu_s")
-        nc.vector.tensor_copy(
-            wu_p[:].rearrange("p (t m b) -> p t m b", t=PACK, b=2),
-            wu_raw[:].rearrange("p (m t b) -> p t m b", t=PACK, b=2),
-        )
-        nc.vector.tensor_copy(
-            wu_s[:].rearrange("p (t m) -> p t m", t=PACK), wu_s_raw[:].rearrange("p (m t) -> p t m", t=PACK)
-        )
-
-        wd_s_raw = tile([P, N], U8, "wd_s_raw", "wu_raw")
-        nc.gpsimd.memset(wd_s_raw[:].bitcast(I32), 0)
-        for q in range(QUADS):
-            scale_rows(wd_s_raw, wd_scales, q, nc.sync)
+        wgo_t = tile([P, J], F32, "wgo_t", "tab_s")
+        nc.sync.dma_start(out=wgo_t[:], in_=wgo)
+        gathered = {0: gather(0, tile([P, CHUNK], U32, "gw0"))}
+        wu_s = deal_scales(wu_s_raw[:], "wu_s")
 
         def up(out, c, t, first, count):
             words = gathered[c]
@@ -121,15 +146,18 @@ def tile_list_modp_gelu_noneP_kernel(
             return sums
 
         def hidden(c, sums):
-            pairs = tile([P, PACK, CHUNK], BF16, "pairs%d" % c)
+            rows = tile([P, PACK, CHUNK], BF16, "rows%d" % c)
+            acts = []
             for u, acc in enumerate(sums):
                 act = tile([P, 2, CHUNK], F32, "act%d_%d" % (c, u))
                 nc.scalar.activation(act[:], acc[:], GELU)
-                for e in range(2):
-                    t = 2 * u + e
-                    nc.scalar.activation(pairs[:, t, :], act[:, e, :], COPY, scale=sm_t[:, t : t + 1])
+                acts.append(act)
+            for t in range(PACK):
+                nc.scalar.activation(rows[:, t, :], acts[t // 2][:, t % 2, :], COPY, scale=sm_t[:, t : t + 1])
             grouped = tile([P, CHUNK * PACK], BF16, "h%d" % c)
-            nc.scalar.copy(grouped[:].rearrange("p (n t) -> p n t", t=PACK), pairs[:].rearrange("p t n -> p n t"))
+            nc.scalar.copy(
+                grouped[:].rearrange("p (n i t) -> p n t i", t=PACK, i=4), rows[:].rearrange("p t (n i) -> p n t i", i=4)
+            )
             quantize_h(grouped[:], c * CHUNK, CHUNK)
 
         def down(y, t, first, count, bank):
@@ -148,6 +176,9 @@ def tile_list_modp_gelu_noneP_kernel(
         def scatter(page, y, first, count):
             nc.vector.tensor_tensor(page[:].indirect(listed(first, count)), y, wgo_t[:, first : first + count], MULT)
 
+        gathered[1] = gather(1, placed([P, CHUNK], U32, "gw1", 1280))
+        gathered[2] = gather(2, placed([P, CHUNK], U32, "gw2", 2304))
+
         first_h = []
         for half in range(2):
             acc = ps.tile([P, PACK, HALF], F32, name="a0_%d" % half, tag="a%d" % half)
@@ -158,55 +189,33 @@ def tile_list_modp_gelu_noneP_kernel(
             grouped = tile([P, HALF, PACK], BF16, "h0_%d" % half)
             nc.vector.tensor_tensor(grouped[:], act[:], sm_t[:].unsqueeze(1).to_broadcast([P, HALF, PACK]), MULT)
             first_h.append(grouped)
+        wd_s = deal_scales(wd_s_raw[:], "wd_s")
         for half in range(2):
             quantize_h(first_h[half][:].rearrange("p n t -> p (n t)"), half * HALF, HALF)
+        gathered[3] = gather(3, tile([P, CHUNK], U32, "gw3", "h0_0"))
+        pages.append(tile([P, T], F32, "page3", "h0_1"))
+        nc.gpsimd.memset(pages[3][:], 0.0)
 
-        wd_raw = tile([P, N], I32, "wd_raw", "tab_s")
-        nc.sync.dma_start(out=wd_raw[:], in_=wd_words[0].rearrange("p n i -> p (n i)").bitcast(I32))
-        wd_p = tile([P, N], I32, "wd_p", "gw0")
-        wd_s = tile([P, N], U8, "wd_s", "act0_0")
-        nc.vector.tensor_copy(
-            wd_p[:].rearrange("p (t m i) -> p m t i", t=PACK, i=4), wd_raw[:].rearrange("p (m i t) -> p m t i", t=PACK, i=4)
-        )
-        nc.vector.tensor_copy(
-            wd_s[:].rearrange("p (t m) -> p t m", t=PACK), wd_s_raw[:].rearrange("p (m t) -> p t m", t=PACK)
-        )
-
-        gathered[1] = gather(1, "wu_s_raw")
-        gathered[2] = gather(2, "act0_1")
-        gathered[3] = gather(3, "h0_0")
-
-        pages = [tile([P, T], F32, "page%d" % t) for t in range(2)]
-        nc.vector.memset(pages[0][:, : T // 2 - 1], 0.0)
-        nc.vector.memset(pages[0][:, T // 2 - 1 :], 0.0)
-        nc.gpsimd.memset(pages[1][:, :QUARTER], 0.0)
-        nc.gpsimd.memset(pages[1][:, QUARTER : T // 2], 0.0)
-        nc.vector.memset(pages[1][:, T // 2 :], 0.0)
-
-        def place(t, c, bank, after=None):
-            y = tile([P, CHUNK], F32, "y%d_%d" % (t, c), after)
-            down(y[:], t, c * CHUNK, CHUNK, bank)
-            scatter(pages[t], y[:], c * CHUNK, CHUNK)
+        def place(t, first, count, bank, after=None):
+            y = tile([P, count], F32, "y%d_%d" % (t, first), after)
+            down(y[:], t, first, count, bank)
+            scatter(pages[t], y[:], first, count)
 
         sums = up_chunk(1)
-        wgo_t = tile([P, J], F32, "wgo_t", "wu_s_raw")
-        nc.sync.dma_start(out=wgo_t[:], in_=wgo)
         for c in range(CHUNKS):
-            place(0, c, "y0")
+            place(0, c * CHUNK, CHUNK, "y0")
+            if c < EARLY:
+                place(2, c * CHUNK, CHUNK, "y2")
             if c + 1 < CHUNKS:
                 hidden(c + 1, sums)
             if c + 2 < CHUNKS:
                 sums = up_chunk(c + 2)
-            place(1, c, "y1", "pairs%d" % (c + 1))
-
-        for t, banks in ((2, ("b0", "y3")), (3, ("y1", "y3"))):
-            page = tile([P, T], F32, "page%d" % t, "h%d" % (t - 1))
-            nc.gpsimd.memset(page[:], 0.0)
-            pages.append(page)
-            y = tile([P, J], F32, "y%d" % t)
-            for half in range(2):
-                down(y[:, half * BANK : (half + 1) * BANK], t, half * BANK, BANK, banks[half])
-            scatter(page, y[:], 0, J)
+            place(1, c * CHUNK, CHUNK, "y1", "rows%d" % (c + 1))
+        place(2, EARLY * CHUNK, J - EARLY * CHUNK, "a0")
+        y = tile([P, J], F32, "y3")
+        for half, bank in enumerate(("b0", "a1")):
+            down(y[:, half * BANK : (half + 1) * BANK], 3, half * BANK, BANK, bank)
+        scatter(pages[3], y[:], 0, J)
 
         out_rows = out_0.rearrange("(p t) n -> p t n", t=PACK)
         out_words = out_1[0].rearrange("p t i -> p (t i)")

@@ -74,10 +74,13 @@ def tile_list_modp_gelu_noneP_kernel(
         for q in range(QUADS):
             scale_rows(wu_s_raw[:], wu_scales, q, nc.sync)
 
-        pages = [tile([P, T], F32, "page%d" % t) for t in range(2)]
-        nc.vector.memset(pages[0][:, : T // 2 - 1], 0.0)
-        nc.vector.memset(pages[0][:, T // 2 - 1 :], 0.0)
-        nc.gpsimd.memset(pages[1][:], 0.0)
+        pages = [tile([P, T], F32, "page0")]
+        nc.vector.memset(pages[0][:], 0.0)
+
+        def cleared_page(t, after):
+            page = tile([P, T], F32, "page%d" % t, after)
+            nc.gpsimd.memset(page[:], 0.0)
+            pages.append(page)
 
         wu_p = tile([P, 2 * R], U8, "wu_p")
         nc.vector.tensor_copy(
@@ -94,8 +97,7 @@ def tile_list_modp_gelu_noneP_kernel(
         nc.gpsimd.memset(wd_s_raw[:].bitcast(I32), 0)
         for q in range(QUADS):
             scale_rows(wd_s_raw[:], wd_scales, q, nc.sync)
-        pages.append(tile([P, T], F32, "page2", "wd_raw"))
-        nc.gpsimd.memset(pages[2][:], 0.0)
+        cleared_page(1, "wd_raw")
 
         def listed(first, count):
             return offsets[:, first // 16 : (first + count) // 16]
@@ -193,8 +195,7 @@ def tile_list_modp_gelu_noneP_kernel(
         for half in range(2):
             quantize_h(first_h[half][:].rearrange("p n t -> p (n t)"), half * HALF, HALF)
         gathered[3] = gather(3, tile([P, CHUNK], U32, "gw3", "h0_0"))
-        pages.append(tile([P, T], F32, "page3", "h0_1"))
-        nc.gpsimd.memset(pages[3][:], 0.0)
+        cleared_page(2, "h0_1")
 
         def place(t, first, count, bank, after=None):
             y = tile([P, count], F32, "y%d_%d" % (t, first), after)
@@ -205,12 +206,14 @@ def tile_list_modp_gelu_noneP_kernel(
         for c in range(CHUNKS):
             place(0, c * CHUNK, CHUNK, "y0")
             if c < EARLY:
-                place(2, c * CHUNK, CHUNK, "y2")
+                place(1, c * CHUNK, CHUNK, "y1")
             if c + 1 < CHUNKS:
                 hidden(c + 1, sums)
+            if c == 0:
+                cleared_page(3, "h1")
             if c + 2 < CHUNKS:
                 sums = up_chunk(c + 2)
-            place(1, c * CHUNK, CHUNK, "y1", "rows%d" % (c + 1))
+            place(2 if c < EARLY else 1, c * CHUNK, CHUNK, "y2", "rows%d" % (c + 1))
         place(2, EARLY * CHUNK, J - EARLY * CHUNK, "a0")
         y = tile([P, J], F32, "y3")
         for half, bank in enumerate(("b0", "a1")):

@@ -156,16 +156,18 @@ def tile_list_modp_gelu_noneP_kernel(
                 acts.append(act)
             for t in range(PACK):
                 nc.scalar.activation(rows[:, t, :], acts[t // 2][:, t % 2, :], COPY, scale=sm_t[:, t : t + 1])
+            return rows
+
+        def interleave_h(c, rows):
             grouped = tile([P, CHUNK * PACK], BF16, "h%d" % c)
             nc.scalar.copy(
                 grouped[:].rearrange("p (n i t) -> p n t i", t=PACK, i=4), rows[:].rearrange("p t (n i) -> p n t i", i=4)
             )
             quantize_h(grouped[:], c * CHUNK, CHUNK)
 
-        def down(y, t, first, count, bank):
-            acc = ps.tile([P, count], F32, name="y%d_%d" % (t, first), tag=bank)
+        def down_sums(out, t, first, count):
             nc.tensor.matmul_mx(
-                out=acc[:],
+                out=out,
                 lhsT=wd_p[:, P * t : P * (t + 1)].bitcast(FP8X4),
                 lhsT_scale=wd_s[:, P * t : P * (t + 1)],
                 rhs=h_w[:, first : first + count].bitcast(FP8X4),
@@ -173,6 +175,10 @@ def tile_list_modp_gelu_noneP_kernel(
                 start=True,
                 stop=True,
             )
+
+        def down(y, t, first, count, bank):
+            acc = ps.tile([P, count], F32, name="y%d_%d" % (t, first), tag=bank)
+            down_sums(acc[:], t, first, count)
             nc.scalar.copy(y, acc[:])
 
         def scatter(page, y, first, count):
@@ -202,13 +208,29 @@ def tile_list_modp_gelu_noneP_kernel(
             down(y[:], t, first, count, bank)
             scatter(pages[t], y[:], first, count)
 
+        def place_rows(ts, first, bank, after):
+            y = tile([P, len(ts), CHUNK], F32, "y_%d" % first, after)
+            acc = ps.tile([P, len(ts), CHUNK], F32, name="y_%d" % first, tag=bank)
+            for t in ts:
+                down_sums(acc[:, t, :], t, first, CHUNK)
+            nc.scalar.copy(y[:], acc[:])
+            for t in ts:
+                scatter(pages[t], y[:, t, :], first, CHUNK)
+
+        first_y = tile([P, CHUNK], F32, "y0_0")
+        for half in range(2):
+            down(first_y[:, half * HALF : (half + 1) * HALF], 0, half * HALF, HALF, "y%d" % (2 * half))
+        scatter(pages[0], first_y[:], 0, CHUNK)
         sums = up_chunk(1)
         for c in range(CHUNKS):
-            place(0, c * CHUNK, CHUNK, "y0")
-            if c < EARLY:
-                place(1, c * CHUNK, CHUNK, "y1")
             if c + 1 < CHUNKS:
-                hidden(c + 1, sums)
+                rows = hidden(c + 1, sums)
+            if c == 0:
+                place(1, 0, CHUNK, "y1")
+            else:
+                place_rows(range(2 if c < EARLY else 1), c * CHUNK, "y0", "act%d_1" % (c + 1))
+            if c + 1 < CHUNKS:
+                interleave_h(c + 1, rows)
             if c == 0:
                 cleared_page(3, "h1")
             if c + 2 < CHUNKS:
@@ -216,7 +238,7 @@ def tile_list_modp_gelu_noneP_kernel(
             place(2 if c < EARLY else 1, c * CHUNK, CHUNK, "y2", "rows%d" % (c + 1))
         place(2, EARLY * CHUNK, J - EARLY * CHUNK, "a0")
         y = tile([P, J], F32, "y3")
-        for half, bank in enumerate(("b0", "a1")):
+        for half, bank in enumerate(("y2", "a1")):
             down(y[:, half * BANK : (half + 1) * BANK], 3, half * BANK, BANK, bank)
         scatter(pages[3], y[:], 0, J)
 
@@ -252,12 +274,12 @@ def tile_list_modp_gelu_noneP_kernel(
         for i in range(2, len(pieces)):
             last_plane(nc.scalar.copy, i)
             interleave(nc.scalar.copy, i)
-        out_s = tile([P, QUARTER], U8, "out_s")
+        out_s = tile([P, T // 2], U8, "out_s")
         for i, (first, count) in enumerate(pieces):
             codes = tile([P, count], U32, "out_w%d" % first)
-            quarter, col = divmod(first, QUARTER)
+            side, col = divmod(first, T // 2)
             nc.vector.quantize_mx(
-                out=codes[:].bitcast(FP8X4), scales=out_s[4 * quarter : P, col : col + count], in_=groups[i][:]
+                out=codes[:].bitcast(FP8X4), scales=out_s[4 * side : P, col : col + count], in_=groups[i][:]
             )
             nc.sync.dma_start(
                 out=out_words[:, PACK * first : PACK * (first + count)].bitcast(I32), in_=codes[:].bitcast(I32)
@@ -265,6 +287,6 @@ def tile_list_modp_gelu_noneP_kernel(
         for q in range(QUADS):
             queue = nc.scalar if q % 2 else nc.sync
             queue.dma_start(
-                out=out_2[0, 4 * q : 4 * q + 4, :].rearrange("r (c n) -> c r n", c=4).bitcast(I32),
-                in_=out_s[32 * q : 32 * q + 16, :].bitcast(I32),
+                out=out_2[0, 4 * q : 4 * q + 4, :].rearrange("r (c n) -> c r n", c=2).bitcast(I32),
+                in_=out_s[32 * q : 32 * q + 8, :].bitcast(I32),
             )

@@ -245,26 +245,34 @@ def tile_list_modp_gelu_noneP_kernel(
         out_rows = out_0.rearrange("(p t) n -> p t n", t=PACK)
         out_words = out_1[0].rearrange("p t i -> p (t i)")
         pieces = [(0, QUARTER), (QUARTER, QUARTER), (2 * QUARTER, QUARTER), (3 * QUARTER, CHUNK), (T - CHUNK, CHUNK)]
-        out_pairs = [tile([P, 2, count, 2], BF16, "out_pairs%d" % first) for first, count in pieces]
         groups = [tile([P, count * PACK], BF16, "out_grouped%d" % first) for first, count in pieces]
+        sides = [tile([P, PACK, 2, CHUNK, 2], BF16, "out_pairs%d" % side) for side in range(2)]
+
+        def blocks(t, first, count):
+            return pages[t][:, first : first + count].rearrange("p (b n) -> p b n", n=CHUNK)
+
         for t in range(3):
             nc.sync.dma_start(out=out_rows[:, t, :], in_=pages[t][:])
-            for i, (first, count) in enumerate(pieces):
-                cols = pages[t][:, first : first + count]
-                if t == 2 and i < 2:
-                    nc.scalar.copy(out_pairs[i][:, 1, :, :], cols.unsqueeze(2).to_broadcast([P, count, 2]))
+            for side in range(2):
+                cols = blocks(t, side * (T // 2), T // 2)
+                if t == 2 and side == 0:
+                    nc.scalar.copy(sides[0][:, :, 1, :, :], cols.unsqueeze(3).to_broadcast([P, PACK, CHUNK, 2]))
                 else:
-                    nc.scalar.copy(out_pairs[i][:, t // 2, :, t % 2], cols)
+                    nc.scalar.copy(sides[side][:, :, t // 2, :, t % 2], cols)
         nc.sync.dma_start(out=out_rows[:, 3, :], in_=pages[3][:])
 
-        def last_plane(copy, i):
+        def pairs_of(i):
             first, count = pieces[i]
-            copy(out_pairs[i][:, 1, :, 1], pages[3][:, first : first + count])
+            side, col = divmod(first, T // 2)
+            return sides[side][:, col // CHUNK : (col + count) // CHUNK]
+
+        def last_plane(copy, i):
+            copy(pairs_of(i)[:, :, 1, :, 1], blocks(3, *pieces[i]))
 
         def interleave(copy, i):
             copy(
-                groups[i][:].bitcast(F32).rearrange("p (n u) -> p n u", u=2),
-                out_pairs[i][:].rearrange("p u n e -> p (u n e)").bitcast(F32).rearrange("p (u n) -> p n u", u=2),
+                groups[i][:].bitcast(F32).rearrange("p (b n u) -> p b n u", u=2, n=CHUNK),
+                pairs_of(i).rearrange("p b u n e -> p b (u n e)").bitcast(F32).rearrange("p b (u n) -> p b n u", u=2),
             )
 
         for i in range(2):

@@ -20,14 +20,22 @@ MULT = mybir.AluOpType.mult
 P = 128
 PACK = 4
 QUADS = 4
+LANES = 16
 CHUNK = 256
 CHUNKS = J // CHUNK
 HALF = CHUNK // 2
 BANK = 512
+SIDE = T // 2
 QUARTER = T // 4
+RUN = 4
 ALIGN = 64
 ZEROS = 32
 EARLY = 2
+AT_WU = 0
+AT_WD_SCALES = AT_WU + R
+AT_WU_SCALES = 4 * R
+AT_WORDS_1 = AT_WU_SCALES + R // 2 - 4 * CHUNK
+AT_WORDS_2 = AT_WU_SCALES + R // 2
 
 
 def tile_list_modp_gelu_noneP_kernel(
@@ -37,42 +45,42 @@ def tile_list_modp_gelu_noneP_kernel(
     with ExitStack() as ctx:
         sb = ctx.enter_context(tc.tile_pool(name="sb", bufs=1))
         ps = ctx.enter_context(tc.psum_pool(name="ps", bufs=1))
-        head = ctx.enter_context(tc.tile_pool(name="head", bufs=1))
+        by_hand = ctx.enter_context(tc.tile_pool(name="by_hand", bufs=1))
 
         def placed(shape, dtype, name, offset):
-            return head.tile(shape, dtype, name=name, tag=name, align_bytes=ALIGN, offset=offset)
+            return by_hand.tile(shape, dtype, name=name, tag=name, align_bytes=ALIGN, offset=offset)
 
-        def tile(shape, dtype, name, tag=None):
-            return sb.tile(shape, dtype, name=name, tag=tag or name, align_bytes=ALIGN)
+        def tile(shape, dtype, name, after=None):
+            return sb.tile(shape, dtype, name=name, tag=after or name, align_bytes=ALIGN)
 
-        def scale_rows(plane, rows, q, queue):
+        def load_scale_rows(plane, rows, q, queue):
             queue.dma_start(
                 out=plane[32 * q : 32 * q + 4].bitcast(I32), in_=rows[0, 4 * q : 4 * q + 4, :].bitcast(I32)
             )
 
-        offsets = sb.tile([P, J // 16], U16, name="offsets")
+        offsets = sb.tile([P, J // LANES], U16, name="offsets")
         nc.sync.dma_start(offsets[:], offs)
 
         zeros = tile([P, ZEROS], I32, "zeros")
         nc.gpsimd.memset(zeros[:], 0)
         tab_s = tile([P, T], U8, "tab_s")
         nc.gpsimd.memset(tab_s[:].bitcast(I32), 0)
-        wu_s_raw = placed([P, R], U8, "wu_s_raw", 2048)
+        wu_s_raw = placed([P, R], U8, "wu_s_raw", AT_WU_SCALES)
         nc.gpsimd.tensor_copy(
             wu_s_raw[:].bitcast(I32).rearrange("p (a z) -> p a z", z=ZEROS),
             zeros[:].unsqueeze(1).to_broadcast([P, R // 4 // ZEROS, ZEROS]),
         )
 
-        wu_raw = placed([P, 2 * R], U8, "wu_raw", 0)
+        wu_raw = placed([P, 2 * R], U8, "wu_raw", AT_WU)
         nc.sync.dma_start(out=wu_raw[:].bitcast(I32), in_=wu_words[0].bitcast(I32))
         wd_raw = tile([P, N], I32, "wd_raw")
         nc.sync.dma_start(out=wd_raw[:], in_=wd_words[0].rearrange("p n i -> p (n i)").bitcast(I32))
         for q in range(QUADS):
-            scale_rows(tab_s[:], tab_scales, q, nc.scalar if q % 2 else nc.sync)
+            load_scale_rows(tab_s[:], tab_scales, q, nc.scalar if q % 2 else nc.sync)
         tab_w = tile([P, T], I32, "tab_w", "zeros")
         nc.scalar.dma_start(out=tab_w[:], in_=tab_words[0].rearrange("p t i -> p (t i)").bitcast(I32))
         for q in range(QUADS):
-            scale_rows(wu_s_raw[:], wu_scales, q, nc.sync)
+            load_scale_rows(wu_s_raw[:], wu_scales, q, nc.sync)
 
         pages = [tile([P, T], F32, "page0")]
         nc.vector.memset(pages[0][:], 0.0)
@@ -82,50 +90,52 @@ def tile_list_modp_gelu_noneP_kernel(
             nc.gpsimd.memset(page[:], 0.0)
             pages.append(page)
 
-        wu_p = tile([P, 2 * R], U8, "wu_p")
+        wu_w = tile([P, 2 * R], U8, "wu_w")
         nc.vector.tensor_copy(
-            wu_p[:].bitcast(U16).rearrange("p (t m) -> p t m", t=PACK),
+            wu_w[:].bitcast(U16).rearrange("p (t m) -> p t m", t=PACK),
             wu_raw[:].bitcast(U16).rearrange("p (m t) -> p t m", t=PACK),
         )
-        wd_p = tile([P, N], I32, "wd_p")
+        wd_w = tile([P, N], I32, "wd_w")
         nc.vector.tensor_copy(
-            wd_p[:].rearrange("p (t m i) -> p m t i", t=PACK, i=4), wd_raw[:].rearrange("p (m i t) -> p m t i", t=PACK, i=4)
+            wd_w[:].rearrange("p (t m i) -> p m t i", t=PACK, i=RUN),
+            wd_raw[:].rearrange("p (m i t) -> p m t i", t=PACK, i=RUN),
         )
-        sm_t = placed([P, PACK], F32, "sm_t", 0)
+        sm_t = placed([P, PACK], F32, "sm_t", AT_WU)
         nc.sync.dma_start(out=sm_t[:], in_=sm.rearrange("(p t) -> p t", t=PACK))
-        wd_s_raw = placed([P, N], U8, "wd_s_raw", 512)
+        wd_s_raw = placed([P, N], U8, "wd_s_raw", AT_WD_SCALES)
         nc.gpsimd.memset(wd_s_raw[:].bitcast(I32), 0)
         for q in range(QUADS):
-            scale_rows(wd_s_raw[:], wd_scales, q, nc.sync)
+            load_scale_rows(wd_s_raw[:], wd_scales, q, nc.sync)
         cleared_page(1, "wd_raw")
 
         def listed(first, count):
-            return offsets[:, first // 16 : (first + count) // 16]
+            return offsets[:, first // LANES : (first + count) // LANES]
 
-        def gather(c, words):
+        def gather_words(c, words):
             nc.vector.tensor_copy(words[:], tab_w[:].bitcast(U32).indirect(listed(c * CHUNK, CHUNK)))
             return words
 
         def deal_scales(raw, name):
             dealt = tile([P, R], U8, name)
-            nc.vector.tensor_copy(dealt[:].rearrange("p (t m) -> p t m", t=PACK), raw.rearrange("p (m t) -> p t m", t=PACK))
+            nc.vector.tensor_copy(
+                dealt[:].rearrange("p (t m) -> p t m", t=PACK), raw.rearrange("p (m t) -> p t m", t=PACK)
+            )
             return dealt
 
-        gathered_s = tile([P, J], U8, "gs")
-        nc.vector.tensor_copy(gathered_s[:], tab_s[:].indirect(offsets[:]))
+        v_s = tile([P, J], U8, "v_s")
+        nc.vector.tensor_copy(v_s[:], tab_s[:].indirect(offsets[:]))
         wgo_t = tile([P, J], F32, "wgo_t", "tab_s")
         nc.sync.dma_start(out=wgo_t[:], in_=wgo)
-        gathered = {0: gather(0, tile([P, CHUNK], U32, "gw0"))}
+        v_w = {0: gather_words(0, tile([P, CHUNK], U32, "v_w0"))}
         wu_s = deal_scales(wu_s_raw[:], "wu_s")
 
-        def up(out, c, t, first, count):
-            words = gathered[c]
+        def up_sums(out, c, t, first, count):
             nc.tensor.matmul_mx(
                 out=out,
-                lhsT=wu_p[:, 2 * P * t : 2 * P * (t + 1)].bitcast(FP4X4),
+                lhsT=wu_w[:, 2 * P * t : 2 * P * (t + 1)].bitcast(FP4X4),
                 lhsT_scale=wu_s[:, P * t : P * (t + 1)],
-                rhs=words[:, first : first + count].bitcast(FP8X4),
-                rhs_scale=gathered_s[:, c * CHUNK + first : c * CHUNK + first + count],
+                rhs=v_w[c][:, first : first + count].bitcast(FP8X4),
+                rhs_scale=v_s[:, c * CHUNK + first : c * CHUNK + first + count],
                 start=True,
                 stop=True,
             )
@@ -143,11 +153,11 @@ def tile_list_modp_gelu_noneP_kernel(
             for u in range(2):
                 acc = ps.tile([P, 2, CHUNK], F32, name="a%d_%d" % (c, u), tag="ab"[c % 2] + str(u))
                 for e in range(2):
-                    up(acc[:, e, :], c, 2 * u + e, 0, CHUNK)
+                    up_sums(acc[:, e, :], c, 2 * u + e, 0, CHUNK)
                 sums.append(acc)
             return sums
 
-        def hidden(c, sums):
+        def hidden_rows(c, sums):
             rows = tile([P, PACK, CHUNK], BF16, "rows%d" % c)
             acts = []
             for u, acc in enumerate(sums):
@@ -158,40 +168,38 @@ def tile_list_modp_gelu_noneP_kernel(
                 nc.scalar.activation(rows[:, t, :], acts[t // 2][:, t % 2, :], COPY, scale=sm_t[:, t : t + 1])
             return rows
 
-        def interleave_h(c, rows):
+        def group_and_quantize_h(c, rows):
             grouped = tile([P, CHUNK * PACK], BF16, "h%d" % c)
             nc.scalar.copy(
-                grouped[:].rearrange("p (n i t) -> p n t i", t=PACK, i=4), rows[:].rearrange("p t (n i) -> p n t i", i=4)
+                grouped[:].rearrange("p (n i t) -> p n t i", t=PACK, i=RUN),
+                rows[:].rearrange("p t (n i) -> p n t i", i=RUN),
             )
             quantize_h(grouped[:], c * CHUNK, CHUNK)
 
-        def down_sums(out, t, first, count):
+        def down(y, t, first, count, bank):
+            acc = ps.tile([P, count], F32, name="y%d_%d" % (t, first), tag=bank)
             nc.tensor.matmul_mx(
-                out=out,
-                lhsT=wd_p[:, P * t : P * (t + 1)].bitcast(FP8X4),
+                out=acc[:],
+                lhsT=wd_w[:, P * t : P * (t + 1)].bitcast(FP8X4),
                 lhsT_scale=wd_s[:, P * t : P * (t + 1)],
                 rhs=h_w[:, first : first + count].bitcast(FP8X4),
                 rhs_scale=h_s[:, first : first + count],
                 start=True,
                 stop=True,
             )
-
-        def down(y, t, first, count, bank):
-            acc = ps.tile([P, count], F32, name="y%d_%d" % (t, first), tag=bank)
-            down_sums(acc[:], t, first, count)
             nc.scalar.copy(y, acc[:])
 
         def scatter(page, y, first, count):
             nc.vector.tensor_tensor(page[:].indirect(listed(first, count)), y, wgo_t[:, first : first + count], MULT)
 
-        gathered[1] = gather(1, placed([P, CHUNK], U32, "gw1", 1280))
-        gathered[2] = gather(2, placed([P, CHUNK], U32, "gw2", 2304))
+        v_w[1] = gather_words(1, placed([P, CHUNK], U32, "v_w1", AT_WORDS_1))
+        v_w[2] = gather_words(2, placed([P, CHUNK], U32, "v_w2", AT_WORDS_2))
 
         first_h = []
         for half in range(2):
             acc = ps.tile([P, PACK, HALF], F32, name="a0_%d" % half, tag="a%d" % half)
             for t in range(PACK):
-                up(acc[:, t, :], 0, t, half * HALF, HALF)
+                up_sums(acc[:, t, :], 0, t, half * HALF, HALF)
             act = tile([P, HALF, PACK], F32, "act0_%d" % half)
             nc.scalar.activation(act[:], acc[:].rearrange("p t n -> p n t"), GELU)
             grouped = tile([P, HALF, PACK], BF16, "h0_%d" % half)
@@ -200,7 +208,7 @@ def tile_list_modp_gelu_noneP_kernel(
         wd_s = deal_scales(wd_s_raw[:], "wd_s")
         for half in range(2):
             quantize_h(first_h[half][:].rearrange("p n t -> p (n t)"), half * HALF, HALF)
-        gathered[3] = gather(3, tile([P, CHUNK], U32, "gw3", "h0_0"))
+        v_w[3] = gather_words(3, tile([P, CHUNK], U32, "v_w3", "h0_0"))
         cleared_page(2, "h0_1")
 
         def place(t, first, count, bank, after=None):
@@ -208,84 +216,81 @@ def tile_list_modp_gelu_noneP_kernel(
             down(y[:], t, first, count, bank)
             scatter(pages[t], y[:], first, count)
 
-        def place_rows(ts, first, bank, after):
-            y = tile([P, len(ts), CHUNK], F32, "y_%d" % first, after)
-            acc = ps.tile([P, len(ts), CHUNK], F32, name="y_%d" % first, tag=bank)
-            for t in ts:
-                down_sums(acc[:, t, :], t, first, CHUNK)
-            nc.scalar.copy(y[:], acc[:])
-            for t in ts:
-                scatter(pages[t], y[:, t, :], first, CHUNK)
-
         first_y = tile([P, CHUNK], F32, "y0_0")
-        for half in range(2):
-            down(first_y[:, half * HALF : (half + 1) * HALF], 0, half * HALF, HALF, "y%d" % (2 * half))
+        for half, bank in enumerate(("y0", "y2")):
+            down(first_y[:, half * HALF : (half + 1) * HALF], 0, half * HALF, HALF, bank)
         scatter(pages[0], first_y[:], 0, CHUNK)
+
         sums = up_chunk(1)
         for c in range(CHUNKS):
             if c + 1 < CHUNKS:
-                rows = hidden(c + 1, sums)
+                rows = hidden_rows(c + 1, sums)
             if c == 0:
                 place(1, 0, CHUNK, "y1")
             else:
-                place_rows(range(2 if c < EARLY else 1), c * CHUNK, "y0", "act%d_1" % (c + 1))
+                place(0, c * CHUNK, CHUNK, "y0", "act%d_1" % (c + 1))
+                if c < EARLY:
+                    place(1, c * CHUNK, CHUNK, "y0")
             if c + 1 < CHUNKS:
-                interleave_h(c + 1, rows)
+                group_and_quantize_h(c + 1, rows)
             if c == 0:
                 cleared_page(3, "h1")
             if c + 2 < CHUNKS:
                 sums = up_chunk(c + 2)
             place(2 if c < EARLY else 1, c * CHUNK, CHUNK, "y2", "rows%d" % (c + 1))
+
         place(2, EARLY * CHUNK, J - EARLY * CHUNK, "a0")
-        y = tile([P, J], F32, "y3")
+        last_y = tile([P, J], F32, "y3")
         for half, bank in enumerate(("y2", "a1")):
-            down(y[:, half * BANK : (half + 1) * BANK], 3, half * BANK, BANK, bank)
-        scatter(pages[3], y[:], 0, J)
+            down(last_y[:, half * BANK : (half + 1) * BANK], 3, half * BANK, BANK, bank)
+        scatter(pages[3], last_y[:], 0, J)
 
         out_rows = out_0.rearrange("(p t) n -> p t n", t=PACK)
         out_words = out_1[0].rearrange("p t i -> p (t i)")
         pieces = [(0, QUARTER), (QUARTER, QUARTER), (2 * QUARTER, QUARTER), (3 * QUARTER, CHUNK), (T - CHUNK, CHUNK)]
+        vector_pieces = SIDE // QUARTER
         groups = [tile([P, count * PACK], BF16, "out_grouped%d" % first) for first, count in pieces]
-        sides = [tile([P, PACK, 2, CHUNK, 2], BF16, "out_pairs%d" % side) for side in range(2)]
+        pairs = [tile([P, SIDE // CHUNK, 2, CHUNK, 2], BF16, "out_pairs%d" % side) for side in range(2)]
 
-        def blocks(t, first, count):
+        def page_columns(t, first, count):
             return pages[t][:, first : first + count].rearrange("p (b n) -> p b n", n=CHUNK)
 
-        for t in range(3):
+        for t in range(PACK - 1):
             nc.sync.dma_start(out=out_rows[:, t, :], in_=pages[t][:])
             for side in range(2):
-                cols = blocks(t, side * (T // 2), T // 2)
+                cols = page_columns(t, side * SIDE, SIDE)
                 if t == 2 and side == 0:
-                    nc.scalar.copy(sides[0][:, :, 1, :, :], cols.unsqueeze(3).to_broadcast([P, PACK, CHUNK, 2]))
+                    nc.scalar.copy(pairs[0][:, :, 1, :, :], cols.unsqueeze(3).to_broadcast([P, SIDE // CHUNK, CHUNK, 2]))
                 else:
-                    nc.scalar.copy(sides[side][:, :, t // 2, :, t % 2], cols)
+                    nc.scalar.copy(pairs[side][:, :, t // 2, :, t % 2], cols)
         nc.sync.dma_start(out=out_rows[:, 3, :], in_=pages[3][:])
 
         def pairs_of(i):
             first, count = pieces[i]
-            side, col = divmod(first, T // 2)
-            return sides[side][:, col // CHUNK : (col + count) // CHUNK]
+            side, col = divmod(first, SIDE)
+            return pairs[side][:, col // CHUNK : (col + count) // CHUNK]
 
-        def last_plane(copy, i):
-            copy(pairs_of(i)[:, :, 1, :, 1], blocks(3, *pieces[i]))
+        def round_page_3(copy, i):
+            copy(pairs_of(i)[:, :, 1, :, 1], page_columns(3, *pieces[i]))
 
-        def interleave(copy, i):
+        def group_words(copy, i):
             copy(
                 groups[i][:].bitcast(F32).rearrange("p (b n u) -> p b n u", u=2, n=CHUNK),
                 pairs_of(i).rearrange("p b u n e -> p b (u n e)").bitcast(F32).rearrange("p b (u n) -> p b n u", u=2),
             )
 
-        for i in range(2):
-            last_plane(nc.vector.tensor_copy, i)
-        for i in range(2):
-            interleave(nc.vector.tensor_copy, i)
-        for i in range(2, len(pieces)):
-            last_plane(nc.scalar.copy, i)
-            interleave(nc.scalar.copy, i)
-        out_s = tile([P, T // 2], U8, "out_s")
+        for i in range(vector_pieces):
+            round_page_3(nc.vector.tensor_copy, i)
+        for i in range(vector_pieces):
+            group_words(nc.vector.tensor_copy, i)
+        for i in range(vector_pieces, len(pieces)):
+            round_page_3(nc.scalar.copy, i)
+            group_words(nc.scalar.copy, i)
+
+        out_s = tile([P, SIDE], U8, "out_s")
         for i, (first, count) in enumerate(pieces):
             codes = tile([P, count], U32, "out_w%d" % first)
-            side, col = divmod(first, T // 2)
+            side, col = divmod(first, SIDE)
             nc.vector.quantize_mx(
                 out=codes[:].bitcast(FP8X4), scales=out_s[4 * side : P, col : col + count], in_=groups[i][:]
             )
@@ -295,6 +300,6 @@ def tile_list_modp_gelu_noneP_kernel(
         for q in range(QUADS):
             queue = nc.scalar if q % 2 else nc.sync
             queue.dma_start(
-                out=out_2[0, 4 * q : 4 * q + 4, :].rearrange("r (c n) -> c r n", c=2).bitcast(I32),
+                out=out_2[0, 4 * q : 4 * q + 4, :].rearrange("r (side n) -> side r n", side=2).bitcast(I32),
                 in_=out_s[32 * q : 32 * q + 8, :].bitcast(I32),
             )

@@ -62,11 +62,11 @@ def tile_list_modp_gelu_noneP_kernel(
         nc.sync.dma_start(offsets[:], offs)
 
         zeros = tile([P, ZEROS], I32, "zeros")
-        nc.gpsimd.memset(zeros[:], 0)
+        nc.vector.memset(zeros[:], 0)
         tab_s = tile([P, T], U8, "tab_s")
-        nc.gpsimd.memset(tab_s[:].bitcast(I32), 0)
+        nc.vector.memset(tab_s[:].bitcast(I32), 0)
         wu_s_raw = placed([P, R], U8, "wu_s_raw", AT_WU_SCALES)
-        nc.gpsimd.tensor_copy(
+        nc.vector.tensor_copy(
             wu_s_raw[:].bitcast(I32).rearrange("p (a z) -> p a z", z=ZEROS),
             zeros[:].unsqueeze(1).to_broadcast([P, R // 4 // ZEROS, ZEROS]),
         )

@@ -31,11 +31,17 @@ RUN = 4
 ALIGN = 64
 ZEROS = 32
 EARLY = 2
-AT_WU = 0
-AT_WD_SCALES = AT_WU + R
-AT_WU_SCALES = 4 * R
-AT_WORDS_1 = AT_WU_SCALES + R // 2 - 4 * CHUNK
-AT_WORDS_2 = AT_WU_SCALES + R // 2
+AT_PAGE_1 = 0
+AT_SM = AT_PAGE_1 + 4 * T
+AT_WU = AT_SM - ALIGN
+AT_WD_SCALES = AT_SM + ALIGN
+AT_WD = AT_WD_SCALES + N
+AT_FIRST_H = AT_WD + 2 * CHUNK
+AT_WORDS_2 = AT_WD
+AT_WORDS_3 = AT_WD + 4 * CHUNK
+AT_WORDS_1 = AT_WD + 4 * N
+AT_LAST_SCALES = AT_WORDS_1 + 4 * CHUNK
+AT_SCALES = AT_LAST_SCALES - R // 2
 
 
 def tile_list_modp_gelu_noneP_kernel(
@@ -53,10 +59,9 @@ def tile_list_modp_gelu_noneP_kernel(
         def tile(shape, dtype, name, after=None):
             return sb.tile(shape, dtype, name=name, tag=after or name, align_bytes=ALIGN)
 
-        def load_scale_rows(plane, rows, q, queue):
-            queue.dma_start(
-                out=plane[32 * q : 32 * q + 4].bitcast(I32), in_=rows[0, 4 * q : 4 * q + 4, :].bitcast(I32)
-            )
+        def load_scale_rows(plane, below, rows, q, queue):
+            first = 32 * q + below
+            queue.dma_start(out=plane[first : first + 4].bitcast(I32), in_=rows[0, 4 * q : 4 * q + 4, :].bitcast(I32))
 
         offsets = sb.tile([P, J // LANES], U16, name="offsets")
         nc.sync.dma_start(offsets[:], offs)
@@ -65,28 +70,26 @@ def tile_list_modp_gelu_noneP_kernel(
         nc.vector.memset(zeros[:], 0)
         tab_s = tile([P, T], U8, "tab_s")
         nc.vector.memset(tab_s[:].bitcast(I32), 0)
-        wu_s_raw = placed([P, R], U8, "wu_s_raw", AT_WU_SCALES)
+        w_s_raw = placed([P, R], U8, "w_s_raw", AT_SCALES)
         nc.vector.tensor_copy(
-            wu_s_raw[:].bitcast(I32).rearrange("p (a z) -> p a z", z=ZEROS),
+            w_s_raw[:].bitcast(I32).rearrange("p (a z) -> p a z", z=ZEROS),
             zeros[:].unsqueeze(1).to_broadcast([P, R // 4 // ZEROS, ZEROS]),
         )
 
         wu_raw = placed([P, 2 * R], U8, "wu_raw", AT_WU)
         nc.sync.dma_start(out=wu_raw[:].bitcast(I32), in_=wu_words[0].bitcast(I32))
-        wd_raw = tile([P, N], I32, "wd_raw")
-        nc.sync.dma_start(out=wd_raw[:], in_=wd_words[0].rearrange("p n i -> p (n i)").bitcast(I32))
         for q in range(QUADS):
-            load_scale_rows(tab_s[:], tab_scales, q, nc.scalar if q % 2 else nc.sync)
+            load_scale_rows(tab_s[:], 0, tab_scales, q, nc.scalar if q % 2 else nc.sync)
+        load_scale_rows(w_s_raw[:], 0, wu_scales, 0, nc.sync)
         tab_w = tile([P, T], I32, "tab_w", "zeros")
         nc.scalar.dma_start(out=tab_w[:], in_=tab_words[0].rearrange("p t i -> p (t i)").bitcast(I32))
-        for q in range(QUADS):
-            load_scale_rows(wu_s_raw[:], wu_scales, q, nc.sync)
+        for q in range(1, QUADS):
+            load_scale_rows(w_s_raw[:], 0, wu_scales, q, nc.sync)
 
         pages = [tile([P, T], F32, "page0")]
         nc.vector.memset(pages[0][:], 0.0)
 
-        def cleared_page(t, after):
-            page = tile([P, T], F32, "page%d" % t, after)
+        def cleared_page(page):
             nc.gpsimd.memset(page[:], 0.0)
             pages.append(page)
 
@@ -95,18 +98,16 @@ def tile_list_modp_gelu_noneP_kernel(
             wu_w[:].bitcast(U16).rearrange("p (t m) -> p t m", t=PACK),
             wu_raw[:].bitcast(U16).rearrange("p (m t) -> p t m", t=PACK),
         )
-        wd_w = tile([P, N], I32, "wd_w")
-        nc.vector.tensor_copy(
-            wd_w[:].rearrange("p (t m i) -> p m t i", t=PACK, i=RUN),
-            wd_raw[:].rearrange("p (m i t) -> p m t i", t=PACK, i=RUN),
-        )
-        sm_t = placed([P, PACK], F32, "sm_t", AT_WU)
-        nc.sync.dma_start(out=sm_t[:], in_=sm.rearrange("(p t) -> p t", t=PACK))
+        wd_raw = placed([P, N], I32, "wd_raw", AT_WD)
+        nc.sync.dma_start(out=wd_raw[:], in_=wd_words[0].rearrange("p n i -> p (n i)").bitcast(I32))
         wd_s_raw = placed([P, N], U8, "wd_s_raw", AT_WD_SCALES)
         nc.gpsimd.memset(wd_s_raw[:].bitcast(I32), 0)
-        for q in range(QUADS):
-            load_scale_rows(wd_s_raw[:], wd_scales, q, nc.sync)
-        cleared_page(1, "wd_raw")
+        for q in range(QUADS - 1):
+            load_scale_rows(wd_s_raw[:], 0, wd_scales, q, nc.sync)
+        sm_t = placed([P, PACK], F32, "sm_t", AT_SM)
+        nc.sync.dma_start(out=sm_t[:], in_=sm.rearrange("(p t) -> p t", t=PACK))
+        load_scale_rows(wd_s_raw[:], 0, wd_scales, QUADS - 1, nc.sync)
+        cleared_page(placed([P, T], F32, "page1", AT_PAGE_1))
 
         def listed(first, count):
             return offsets[:, first // LANES : (first + count) // LANES]
@@ -115,27 +116,25 @@ def tile_list_modp_gelu_noneP_kernel(
             nc.vector.tensor_copy(words[:], tab_w[:].bitcast(U32).indirect(listed(c * CHUNK, CHUNK)))
             return words
 
-        def deal_scales(raw, name):
-            dealt = tile([P, R], U8, name)
-            nc.vector.tensor_copy(
-                dealt[:].rearrange("p (t m) -> p t m", t=PACK), raw.rearrange("p (m t) -> p t m", t=PACK)
-            )
-            return dealt
+        def gather_scales(first, count, scales):
+            nc.vector.tensor_copy(scales[:], tab_s[:].indirect(listed(first, count)))
+            return scales
 
-        v_s = tile([P, J], U8, "v_s")
-        nc.vector.tensor_copy(v_s[:], tab_s[:].indirect(offsets[:]))
-        wgo_t = tile([P, J], F32, "wgo_t", "tab_s")
-        nc.sync.dma_start(out=wgo_t[:], in_=wgo)
+        early_s = gather_scales(0, J - CHUNK, tile([P, J - CHUNK], U8, "early_s"))
+        v_s = {c: early_s[:, c * CHUNK : (c + 1) * CHUNK] for c in range(CHUNKS - 1)}
         v_w = {0: gather_words(0, tile([P, CHUNK], U32, "v_w0"))}
-        wu_s = deal_scales(wu_s_raw[:], "wu_s")
+        w_s = tile([P, R], U8, "w_s")
+        nc.vector.tensor_copy(
+            w_s[:].rearrange("p (t m) -> p t m", t=PACK), w_s_raw[:].rearrange("p (m t) -> p t m", t=PACK)
+        )
 
         def up_sums(out, c, t, first, count):
             nc.tensor.matmul_mx(
                 out=out,
                 lhsT=wu_w[:, 2 * P * t : 2 * P * (t + 1)].bitcast(FP4X4),
-                lhsT_scale=wu_s[:, P * t : P * (t + 1)],
+                lhsT_scale=w_s[:, P * t : P * (t + 1)],
                 rhs=v_w[c][:, first : first + count].bitcast(FP8X4),
-                rhs_scale=v_s[:, c * CHUNK + first : c * CHUNK + first + count],
+                rhs_scale=v_s[c][:, first : first + count],
                 start=True,
                 stop=True,
             )
@@ -193,7 +192,14 @@ def tile_list_modp_gelu_noneP_kernel(
             nc.vector.tensor_tensor(page[:].indirect(listed(first, count)), y, wgo_t[:, first : first + count], MULT)
 
         v_w[1] = gather_words(1, placed([P, CHUNK], U32, "v_w1", AT_WORDS_1))
-        v_w[2] = gather_words(2, placed([P, CHUNK], U32, "v_w2", AT_WORDS_2))
+        v_s[CHUNKS - 1] = gather_scales(J - CHUNK, CHUNK, placed([P, CHUNK], U8, "last_s", AT_LAST_SCALES))[:]
+        wgo_t = tile([P, J], F32, "wgo_t", "tab_s")
+        nc.sync.dma_start(out=wgo_t[:], in_=wgo)
+        wd_w = tile([P, N], I32, "wd_w")
+        nc.vector.tensor_copy(
+            wd_w[:].rearrange("p (t m i) -> p m t i", t=PACK, i=RUN),
+            wd_raw[:].rearrange("p (m i t) -> p m t i", t=PACK, i=RUN),
+        )
 
         first_h = []
         for half in range(2):
@@ -202,14 +208,19 @@ def tile_list_modp_gelu_noneP_kernel(
                 up_sums(acc[:, t, :], 0, t, half * HALF, HALF)
             act = tile([P, HALF, PACK], F32, "act0_%d" % half)
             nc.scalar.activation(act[:], acc[:].rearrange("p t n -> p n t"), GELU)
-            grouped = tile([P, HALF, PACK], BF16, "h0_%d" % half)
+            shape = [P, HALF, PACK]
+            grouped = tile(shape, BF16, "h0_1") if half else placed(shape, BF16, "h0_0", AT_FIRST_H)
             nc.vector.tensor_tensor(grouped[:], act[:], sm_t[:].unsqueeze(1).to_broadcast([P, HALF, PACK]), MULT)
             first_h.append(grouped)
-        wd_s = deal_scales(wd_s_raw[:], "wd_s")
+        wd_s = tile([P, N], U8, "wd_s")
+        nc.vector.tensor_copy(
+            wd_s[:].rearrange("p (t m) -> p t m", t=PACK), wd_s_raw[:].rearrange("p (m t) -> p t m", t=PACK)
+        )
         for half in range(2):
             quantize_h(first_h[half][:].rearrange("p n t -> p (n t)"), half * HALF, HALF)
-        v_w[3] = gather_words(3, tile([P, CHUNK], U32, "v_w3", "h0_0"))
-        cleared_page(2, "h0_1")
+        v_w[2] = gather_words(2, placed([P, CHUNK], U32, "v_w2", AT_WORDS_2))
+        v_w[3] = gather_words(3, placed([P, CHUNK], U32, "v_w3", AT_WORDS_3))
+        cleared_page(tile([P, T], F32, "page2", "h0_1"))
 
         def place(t, first, count, bank, after=None):
             y = tile([P, count], F32, "y%d_%d" % (t, first), after)
@@ -234,7 +245,7 @@ def tile_list_modp_gelu_noneP_kernel(
             if c + 1 < CHUNKS:
                 group_and_quantize_h(c + 1, rows)
             if c == 0:
-                cleared_page(3, "h1")
+                cleared_page(tile([P, T], F32, "page3", "h1"))
             if c + 2 < CHUNKS:
                 sums = up_chunk(c + 2)
             place(2 if c < EARLY else 1, c * CHUNK, CHUNK, "y2", "rows%d" % (c + 1))

@@ -59,9 +59,8 @@ def tile_list_modp_gelu_noneP_kernel(
         def tile(shape, dtype, name, after=None):
             return sb.tile(shape, dtype, name=name, tag=after or name, align_bytes=ALIGN)
 
-        def load_scale_rows(plane, below, rows, q, queue):
-            first = 32 * q + below
-            queue.dma_start(out=plane[first : first + 4].bitcast(I32), in_=rows[0, 4 * q : 4 * q + 4, :].bitcast(I32))
+        def load_scale_rows(plane, rows, r, queue):
+            queue.dma_start(out=plane[r:P:32].bitcast(I32), in_=rows[0, r : 4 * QUADS : 4, :].bitcast(I32))
 
         offsets = sb.tile([P, J // LANES], U16, name="offsets")
         nc.sync.dma_start(offsets[:], offs)
@@ -79,12 +78,12 @@ def tile_list_modp_gelu_noneP_kernel(
         wu_raw = placed([P, 2 * R], U8, "wu_raw", AT_WU)
         nc.sync.dma_start(out=wu_raw[:].bitcast(I32), in_=wu_words[0].bitcast(I32))
         for q in range(QUADS):
-            load_scale_rows(tab_s[:], 0, tab_scales, q, nc.scalar if q % 2 else nc.sync)
-        load_scale_rows(w_s_raw[:], 0, wu_scales, 0, nc.sync)
+            load_scale_rows(tab_s[:], tab_scales, q, nc.scalar if q >= QUADS // 2 else nc.sync)
+        load_scale_rows(w_s_raw[:], wu_scales, 0, nc.sync)
         tab_w = tile([P, T], I32, "tab_w", "zeros")
         nc.scalar.dma_start(out=tab_w[:], in_=tab_words[0].rearrange("p t i -> p (t i)").bitcast(I32))
         for q in range(1, QUADS):
-            load_scale_rows(w_s_raw[:], 0, wu_scales, q, nc.sync)
+            load_scale_rows(w_s_raw[:], wu_scales, q, nc.sync)
 
         pages = [tile([P, T], F32, "page0")]
         nc.vector.memset(pages[0][:], 0.0)
@@ -99,14 +98,14 @@ def tile_list_modp_gelu_noneP_kernel(
             wu_raw[:].bitcast(U16).rearrange("p (m t) -> p t m", t=PACK),
         )
         wd_raw = placed([P, N], I32, "wd_raw", AT_WD)
-        nc.sync.dma_start(out=wd_raw[:], in_=wd_words[0].rearrange("p n i -> p (n i)").bitcast(I32))
+        nc.scalar.dma_start(out=wd_raw[:], in_=wd_words[0].rearrange("p n i -> p (n i)").bitcast(I32))
         wd_s_raw = placed([P, N], U8, "wd_s_raw", AT_WD_SCALES)
         nc.gpsimd.memset(wd_s_raw[:].bitcast(I32), 0)
         for q in range(QUADS - 1):
-            load_scale_rows(wd_s_raw[:], 0, wd_scales, q, nc.sync)
+            load_scale_rows(wd_s_raw[:], wd_scales, q, nc.sync)
         sm_t = placed([P, PACK], F32, "sm_t", AT_SM)
         nc.sync.dma_start(out=sm_t[:], in_=sm.rearrange("(p t) -> p t", t=PACK))
-        load_scale_rows(wd_s_raw[:], 0, wd_scales, QUADS - 1, nc.sync)
+        load_scale_rows(wd_s_raw[:], wd_scales, QUADS - 1, nc.sync)
         cleared_page(placed([P, T], F32, "page1", AT_PAGE_1))
 
         def listed(first, count):
@@ -309,7 +308,7 @@ def tile_list_modp_gelu_noneP_kernel(
                 out=out_words[:, PACK * first : PACK * (first + count)].bitcast(I32), in_=codes[:].bitcast(I32)
             )
         for q in range(QUADS):
-            queue = nc.scalar if q % 2 else nc.sync
+            queue = nc.scalar if q >= QUADS // 2 else nc.sync
             queue.dma_start(
                 out=out_2[0, 4 * q : 4 * q + 4, :].rearrange("r (side n) -> side r n", side=2).bitcast(I32),
                 in_=out_s[32 * q : 32 * q + 8, :].bitcast(I32),

@@ -41,7 +41,8 @@ AT_WORDS_2 = AT_WD
 AT_WORDS_3 = AT_WD + 4 * CHUNK
 AT_WORDS_1 = AT_WD + 4 * N
 AT_LAST_SCALES = AT_WORDS_1 + 4 * CHUNK
-AT_SCALES = AT_LAST_SCALES - R // 2
+AT_WGO = AT_LAST_SCALES + CHUNK
+AT_SCALES = AT_WGO + ALIGN - R
 
 
 def tile_list_modp_gelu_noneP_kernel(
@@ -192,7 +193,7 @@ def tile_list_modp_gelu_noneP_kernel(
 
         v_w[1] = gather_words(1, placed([P, CHUNK], U32, "v_w1", AT_WORDS_1))
         v_s[CHUNKS - 1] = gather_scales(J - CHUNK, CHUNK, placed([P, CHUNK], U8, "last_s", AT_LAST_SCALES))[:]
-        wgo_t = tile([P, J], F32, "wgo_t", "tab_s")
+        wgo_t = placed([P, J], F32, "wgo_t", AT_WGO)
         nc.sync.dma_start(out=wgo_t[:], in_=wgo)
         wd_w = tile([P, N], I32, "wd_w")
         nc.vector.tensor_copy(

@@ -31,18 +31,16 @@ RUN = 4
 ALIGN = 64
 ZEROS = 32
 EARLY = 2
-AT_PAGE_1 = 0
-AT_SM = AT_PAGE_1 + 4 * T
-AT_WU = AT_SM - ALIGN
+AT_WU = 0
+AT_SM = AT_WU
 AT_WD_SCALES = AT_SM + ALIGN
 AT_WD = AT_WD_SCALES + N
-AT_FIRST_H = AT_WD + 2 * CHUNK
-AT_WORDS_2 = AT_WD
-AT_WORDS_3 = AT_WD + 4 * CHUNK
-AT_WORDS_1 = AT_WD + 4 * N
-AT_LAST_SCALES = AT_WORDS_1 + 4 * CHUNK
-AT_WGO = AT_LAST_SCALES + CHUNK
-AT_SCALES = AT_WGO + ALIGN - R
+AT_LAST_SCALES = AT_WD + 4 * N
+AT_SCALES = AT_LAST_SCALES
+AT_WGO = AT_SCALES + R - ALIGN
+AT_WORDS_3 = AT_WGO + 4 * J
+AT_FIRST_H = AT_WORDS_3 + ALIGN
+AT_PAGE_2 = AT_WORDS_3 + 4 * CHUNK
 
 
 def tile_list_modp_gelu_noneP_kernel(
@@ -86,7 +84,7 @@ def tile_list_modp_gelu_noneP_kernel(
         for q in range(1, QUADS):
             load_scale_rows(w_s_raw[:], wu_scales, q, nc.sync)
 
-        pages = [tile([P, T], F32, "page0")]
+        pages = [tile([P, T], F32, "page0"), tile([P, T], F32, "page1")]
         nc.vector.memset(pages[0][:], 0.0)
 
         def cleared_page(page):
@@ -98,6 +96,7 @@ def tile_list_modp_gelu_noneP_kernel(
             wu_w[:].bitcast(U16).rearrange("p (t m) -> p t m", t=PACK),
             wu_raw[:].bitcast(U16).rearrange("p (m t) -> p t m", t=PACK),
         )
+        nc.vector.memset(pages[1][:], 0.0)
         wd_raw = placed([P, N], I32, "wd_raw", AT_WD)
         nc.scalar.dma_start(out=wd_raw[:], in_=wd_words[0].rearrange("p n i -> p (n i)").bitcast(I32))
         wd_s_raw = placed([P, N], U8, "wd_s_raw", AT_WD_SCALES)
@@ -107,13 +106,12 @@ def tile_list_modp_gelu_noneP_kernel(
         sm_t = placed([P, PACK], F32, "sm_t", AT_SM)
         nc.sync.dma_start(out=sm_t[:], in_=sm.rearrange("(p t) -> p t", t=PACK))
         load_scale_rows(wd_s_raw[:], wd_scales, QUADS - 1, nc.sync)
-        cleared_page(placed([P, T], F32, "page1", AT_PAGE_1))
 
         def listed(first, count):
             return offsets[:, first // LANES : (first + count) // LANES]
 
-        def gather_words(c, words):
-            nc.vector.tensor_copy(words[:], tab_w[:].bitcast(U32).indirect(listed(c * CHUNK, CHUNK)))
+        def gather_words(first, count, words):
+            nc.vector.tensor_copy(words, tab_w[:].bitcast(U32).indirect(listed(first, count)))
             return words
 
         def gather_scales(first, count, scales):
@@ -122,9 +120,11 @@ def tile_list_modp_gelu_noneP_kernel(
 
         early_s = gather_scales(0, J - CHUNK, tile([P, J - CHUNK], U8, "early_s"))
         v_s = {c: early_s[:, c * CHUNK : (c + 1) * CHUNK] for c in range(CHUNKS - 1)}
-        v_w = {0: gather_words(0, tile([P, CHUNK], U32, "v_w0"))}
+        v_w = {0: tile([P, CHUNK], U32, "v_w0")[:]}
+        for half in range(2):
+            gather_words(half * HALF, HALF, v_w[0][:, half * HALF : (half + 1) * HALF])
         w_s = tile([P, R], U8, "w_s")
-        nc.vector.tensor_copy(
+        nc.gpsimd.tensor_copy(
             w_s[:].rearrange("p (t m) -> p t m", t=PACK), w_s_raw[:].rearrange("p (m t) -> p t m", t=PACK)
         )
 
@@ -191,14 +191,14 @@ def tile_list_modp_gelu_noneP_kernel(
         def scatter(page, y, first, count):
             nc.vector.tensor_tensor(page[:].indirect(listed(first, count)), y, wgo_t[:, first : first + count], MULT)
 
-        v_w[1] = gather_words(1, placed([P, CHUNK], U32, "v_w1", AT_WORDS_1))
+        for c in (1, 2):
+            v_w[c] = gather_words(c * CHUNK, CHUNK, tile([P, CHUNK], U32, "v_w%d" % c)[:])
         v_s[CHUNKS - 1] = gather_scales(J - CHUNK, CHUNK, placed([P, CHUNK], U8, "last_s", AT_LAST_SCALES))[:]
         wgo_t = placed([P, J], F32, "wgo_t", AT_WGO)
         nc.sync.dma_start(out=wgo_t[:], in_=wgo)
         wd_w = tile([P, N], I32, "wd_w")
-        nc.vector.tensor_copy(
-            wd_w[:].rearrange("p (t m i) -> p m t i", t=PACK, i=RUN),
-            wd_raw[:].rearrange("p (m i t) -> p m t i", t=PACK, i=RUN),
+        nc.gpsimd.tensor_copy(
+            wd_w[:].rearrange("p (t m) -> p t m", t=PACK), wd_raw[:].rearrange("p (m t) -> p t m", t=PACK)
         )
 
         first_h = []
@@ -209,7 +209,7 @@ def tile_list_modp_gelu_noneP_kernel(
             act = tile([P, HALF, PACK], F32, "act0_%d" % half)
             nc.scalar.activation(act[:], acc[:].rearrange("p t n -> p n t"), GELU)
             shape = [P, HALF, PACK]
-            grouped = tile(shape, BF16, "h0_1") if half else placed(shape, BF16, "h0_0", AT_FIRST_H)
+            grouped = placed(shape, BF16, "h0_1", AT_FIRST_H) if half else tile(shape, BF16, "h0_0")
             nc.vector.tensor_tensor(grouped[:], act[:], sm_t[:].unsqueeze(1).to_broadcast([P, HALF, PACK]), MULT)
             first_h.append(grouped)
         wd_s = tile([P, N], U8, "wd_s")
@@ -218,9 +218,8 @@ def tile_list_modp_gelu_noneP_kernel(
         )
         for half in range(2):
             quantize_h(first_h[half][:].rearrange("p n t -> p (n t)"), half * HALF, HALF)
-        v_w[2] = gather_words(2, placed([P, CHUNK], U32, "v_w2", AT_WORDS_2))
-        v_w[3] = gather_words(3, placed([P, CHUNK], U32, "v_w3", AT_WORDS_3))
-        cleared_page(tile([P, T], F32, "page2", "h0_1"))
+        v_w[3] = gather_words(3 * CHUNK, CHUNK, placed([P, CHUNK], U32, "v_w3", AT_WORDS_3)[:])
+        cleared_page(placed([P, T], F32, "page2", AT_PAGE_2))
 
         def place(t, first, count, bank, after=None):
             y = tile([P, count], F32, "y%d_%d" % (t, first), after)
@@ -261,7 +260,9 @@ def tile_list_modp_gelu_noneP_kernel(
         pieces = [(0, QUARTER), (QUARTER, QUARTER), (2 * QUARTER, QUARTER), (3 * QUARTER, CHUNK), (T - CHUNK, CHUNK)]
         vector_pieces = SIDE // QUARTER
         groups = [tile([P, count * PACK], BF16, "out_grouped%d" % first) for first, count in pieces]
-        pairs = [tile([P, SIDE // CHUNK, 2, CHUNK, 2], BF16, "out_pairs%d" % side) for side in range(2)]
+        pairs = [
+            tile([P, SIDE // CHUNK, 2, CHUNK, 2], BF16, "out_pairs%d" % side, ("h_w", "h_s")[side]) for side in range(2)
+        ]
 
         def page_columns(t, first, count):
             return pages[t][:, first : first + count].rearrange("p (b n) -> p b n", n=CHUNK)

@@ -29,18 +29,22 @@ SIDE = T // 2
 QUARTER = T // 4
 RUN = 4
 ALIGN = 64
+LOWER = 96
 ZEROS = 32
 EARLY = 2
-AT_WU = 0
-AT_SM = AT_WU
+AT_PAGE_1 = 0
+AT_SM = AT_PAGE_1 + 4 * T
+AT_WU = AT_SM - ALIGN
 AT_WD_SCALES = AT_SM + ALIGN
 AT_WD = AT_WD_SCALES + N
 AT_LAST_SCALES = AT_WD + 4 * N
 AT_SCALES = AT_LAST_SCALES
 AT_WGO = AT_SCALES + R - ALIGN
-AT_WORDS_3 = AT_WGO + 4 * J
-AT_FIRST_H = AT_WORDS_3 + ALIGN
-AT_PAGE_2 = AT_WORDS_3 + 4 * CHUNK
+AT_PAGE_3 = AT_WGO + 4 * J
+AT_SECOND_H = AT_PAGE_3 + 4 * T - ALIGN
+AT_FIRST_H = AT_SECOND_H + 2 * PACK * CHUNK - ALIGN
+AT_LATER_S = AT_FIRST_H + ALIGN
+AT_PAGE_2 = AT_FIRST_H + 2 * PACK * HALF - ALIGN
 
 
 def tile_list_modp_gelu_noneP_kernel(
@@ -61,6 +65,9 @@ def tile_list_modp_gelu_noneP_kernel(
         def load_scale_rows(plane, rows, r, queue):
             queue.dma_start(out=plane[r:P:32].bitcast(I32), in_=rows[0, r : 4 * QUADS : 4, :].bitcast(I32))
 
+        def load_quadrant(plane, rows, q, queue):
+            queue.dma_start(out=plane[32 * q : 32 * q + 4].bitcast(I32), in_=rows[0, 4 * q : 4 * q + 4, :].bitcast(I32))
+
         offsets = sb.tile([P, J // LANES], U16, name="offsets")
         nc.sync.dma_start(offsets[:], offs)
 
@@ -69,22 +76,23 @@ def tile_list_modp_gelu_noneP_kernel(
         tab_s = tile([P, T], U8, "tab_s")
         nc.vector.memset(tab_s[:].bitcast(I32), 0)
         w_s_raw = placed([P, R], U8, "w_s_raw", AT_SCALES)
+        nc.gpsimd.memset(w_s_raw[LOWER:P].bitcast(I32), 0)
         nc.vector.tensor_copy(
-            w_s_raw[:].bitcast(I32).rearrange("p (a z) -> p a z", z=ZEROS),
-            zeros[:].unsqueeze(1).to_broadcast([P, R // 4 // ZEROS, ZEROS]),
+            w_s_raw[:LOWER].bitcast(I32).rearrange("p (a z) -> p a z", z=ZEROS),
+            zeros[:LOWER].unsqueeze(1).to_broadcast([LOWER, R // 4 // ZEROS, ZEROS]),
         )
+        load_quadrant(w_s_raw[:], wu_scales, QUADS - 1, nc.scalar)
 
         wu_raw = placed([P, 2 * R], U8, "wu_raw", AT_WU)
         nc.sync.dma_start(out=wu_raw[:].bitcast(I32), in_=wu_words[0].bitcast(I32))
         for q in range(QUADS):
             load_scale_rows(tab_s[:], tab_scales, q, nc.scalar if q >= QUADS // 2 else nc.sync)
-        load_scale_rows(w_s_raw[:], wu_scales, 0, nc.sync)
         tab_w = tile([P, T], I32, "tab_w", "zeros")
         nc.scalar.dma_start(out=tab_w[:], in_=tab_words[0].rearrange("p t i -> p (t i)").bitcast(I32))
-        for q in range(1, QUADS):
-            load_scale_rows(w_s_raw[:], wu_scales, q, nc.sync)
+        for q in range(QUADS - 1):
+            load_quadrant(w_s_raw[:], wu_scales, q, nc.sync)
 
-        pages = [tile([P, T], F32, "page0"), tile([P, T], F32, "page1")]
+        pages = [tile([P, T], F32, "page0")]
         nc.vector.memset(pages[0][:], 0.0)
 
         def cleared_page(page):
@@ -96,7 +104,6 @@ def tile_list_modp_gelu_noneP_kernel(
             wu_w[:].bitcast(U16).rearrange("p (t m) -> p t m", t=PACK),
             wu_raw[:].bitcast(U16).rearrange("p (m t) -> p t m", t=PACK),
         )
-        nc.vector.memset(pages[1][:], 0.0)
         wd_raw = placed([P, N], I32, "wd_raw", AT_WD)
         nc.scalar.dma_start(out=wd_raw[:], in_=wd_words[0].rearrange("p n i -> p (n i)").bitcast(I32))
         wd_s_raw = placed([P, N], U8, "wd_s_raw", AT_WD_SCALES)
@@ -106,6 +113,7 @@ def tile_list_modp_gelu_noneP_kernel(
         sm_t = placed([P, PACK], F32, "sm_t", AT_SM)
         nc.sync.dma_start(out=sm_t[:], in_=sm.rearrange("(p t) -> p t", t=PACK))
         load_scale_rows(wd_s_raw[:], wd_scales, QUADS - 1, nc.sync)
+        cleared_page(placed([P, T], F32, "page1", AT_PAGE_1))
 
         def listed(first, count):
             return offsets[:, first // LANES : (first + count) // LANES]
@@ -118,8 +126,8 @@ def tile_list_modp_gelu_noneP_kernel(
             nc.vector.tensor_copy(scales[:], tab_s[:].indirect(listed(first, count)))
             return scales
 
-        early_s = gather_scales(0, J - CHUNK, tile([P, J - CHUNK], U8, "early_s"))
-        v_s = {c: early_s[:, c * CHUNK : (c + 1) * CHUNK] for c in range(CHUNKS - 1)}
+        all_s = gather_scales(0, J, tile([P, J], U8, "all_s"))
+        v_s = {c: all_s[:, c * CHUNK : (c + 1) * CHUNK] for c in range(CHUNKS)}
         v_w = {0: tile([P, CHUNK], U32, "v_w0")[:]}
         for half in range(2):
             gather_words(half * HALF, HALF, v_w[0][:, half * HALF : (half + 1) * HALF])
@@ -180,7 +188,7 @@ def tile_list_modp_gelu_noneP_kernel(
             nc.tensor.matmul_mx(
                 out=acc[:],
                 lhsT=wd_w[:, P * t : P * (t + 1)].bitcast(FP8X4),
-                lhsT_scale=wd_s[:, P * t : P * (t + 1)],
+                lhsT_scale=later_s[:, t - 1, :] if t else wd_s[:],
                 rhs=h_w[:, first : first + count].bitcast(FP8X4),
                 rhs_scale=h_s[:, first : first + count],
                 start=True,
@@ -191,9 +199,8 @@ def tile_list_modp_gelu_noneP_kernel(
         def scatter(page, y, first, count):
             nc.vector.tensor_tensor(page[:].indirect(listed(first, count)), y, wgo_t[:, first : first + count], MULT)
 
-        for c in (1, 2):
+        for c in range(1, CHUNKS):
             v_w[c] = gather_words(c * CHUNK, CHUNK, tile([P, CHUNK], U32, "v_w%d" % c)[:])
-        v_s[CHUNKS - 1] = gather_scales(J - CHUNK, CHUNK, placed([P, CHUNK], U8, "last_s", AT_LAST_SCALES))[:]
         wgo_t = placed([P, J], F32, "wgo_t", AT_WGO)
         nc.sync.dma_start(out=wgo_t[:], in_=wgo)
         wd_w = tile([P, N], I32, "wd_w")
@@ -201,24 +208,37 @@ def tile_list_modp_gelu_noneP_kernel(
             wd_w[:].rearrange("p (t m) -> p t m", t=PACK), wd_raw[:].rearrange("p (m t) -> p t m", t=PACK)
         )
 
+        def up_half(c, half):
+            acc = ps.tile([P, PACK, HALF], F32, name="a%d_%d" % (c, half), tag="ab"[c % 2] + str(half))
+            for t in range(PACK):
+                up_sums(acc[:, t, :], c, t, half * HALF, HALF)
+            return acc
+
+        def grouped_gelu(c, half):
+            act = tile([P, HALF, PACK], F32, "act%d_%d" % (c, half))
+            nc.scalar.activation(act[:], up_half(c, half)[:].rearrange("p t n -> p n t"), GELU)
+            return act
+
+        def times_sm(grouped, act):
+            nc.vector.tensor_tensor(grouped, act[:], sm_t[:].unsqueeze(1).to_broadcast([P, HALF, PACK]), MULT)
+
         first_h = []
         for half in range(2):
-            acc = ps.tile([P, PACK, HALF], F32, name="a0_%d" % half, tag="a%d" % half)
-            for t in range(PACK):
-                up_sums(acc[:, t, :], 0, t, half * HALF, HALF)
-            act = tile([P, HALF, PACK], F32, "act0_%d" % half)
-            nc.scalar.activation(act[:], acc[:].rearrange("p t n -> p n t"), GELU)
             shape = [P, HALF, PACK]
             grouped = placed(shape, BF16, "h0_1", AT_FIRST_H) if half else tile(shape, BF16, "h0_0")
-            nc.vector.tensor_tensor(grouped[:], act[:], sm_t[:].unsqueeze(1).to_broadcast([P, HALF, PACK]), MULT)
+            times_sm(grouped[:], grouped_gelu(0, half))
             first_h.append(grouped)
-        wd_s = tile([P, N], U8, "wd_s")
+        wd_s = tile([P, P], U8, "wd_s")
+        raw_s = wd_s_raw[:].rearrange("p (m t) -> p t m", t=PACK)
+        quantize_h(first_h[0][:].rearrange("p n t -> p (n t)"), 0, HALF)
+        nc.vector.tensor_copy(wd_s[:], raw_s[:, 0, :])
+        quantize_h(first_h[1][:].rearrange("p n t -> p (n t)"), HALF, HALF)
+        second_h = placed([P, CHUNK, PACK], BF16, "h1", AT_SECOND_H)
+        times_sm(second_h[:, :HALF, :], grouped_gelu(1, 0))
+        later_s = placed([P, PACK - 1, P], U8, "later_s", AT_LATER_S)
         nc.vector.tensor_copy(
-            wd_s[:].rearrange("p (t m) -> p t m", t=PACK), wd_s_raw[:].rearrange("p (m t) -> p t m", t=PACK)
+            later_s[:].rearrange("p t (a m) -> p a t m", a=2), raw_s[:, 1:, :].rearrange("p t (a m) -> p a t m", a=2)
         )
-        for half in range(2):
-            quantize_h(first_h[half][:].rearrange("p n t -> p (n t)"), half * HALF, HALF)
-        v_w[3] = gather_words(3 * CHUNK, CHUNK, placed([P, CHUNK], U32, "v_w3", AT_WORDS_3)[:])
         cleared_page(placed([P, T], F32, "page2", AT_PAGE_2))
 
         def place(t, first, count, bank, after=None):
@@ -227,24 +247,32 @@ def tile_list_modp_gelu_noneP_kernel(
             scatter(pages[t], y[:], first, count)
 
         first_y = tile([P, CHUNK], F32, "y0_0")
-        for half, bank in enumerate(("y0", "y2")):
+        for half, bank in enumerate(("a0", "a1")):
             down(first_y[:, half * HALF : (half + 1) * HALF], 0, half * HALF, HALF, bank)
         scatter(pages[0], first_y[:], 0, CHUNK)
 
-        sums = up_chunk(1)
-        for c in range(CHUNKS):
+        act = tile([P, PACK, HALF], F32, "act1_1")
+        nc.scalar.activation(act[:], up_half(1, 1)[:], GELU)
+        rows = tile([P, PACK, HALF], BF16, "rows1")
+        for t in range(PACK):
+            nc.scalar.activation(rows[:, t, :], act[:, t, :], COPY, scale=sm_t[:, t : t + 1])
+        place(1, 0, CHUNK, "b0")
+        nc.scalar.copy(
+            second_h[:, HALF:, :].rearrange("p (n i) t -> p n t i", i=RUN),
+            rows[:].rearrange("p t (n i) -> p n t i", i=RUN),
+        )
+        quantize_h(second_h[:].rearrange("p n t -> p (n t)"), CHUNK, CHUNK)
+        cleared_page(placed([P, T], F32, "page3", AT_PAGE_3))
+        sums = up_chunk(2)
+        place(2, 0, CHUNK, "b1", "rows1")
+        for c in range(1, CHUNKS):
             if c + 1 < CHUNKS:
                 rows = hidden_rows(c + 1, sums)
-            if c == 0:
-                place(1, 0, CHUNK, "y1")
-            else:
-                place(0, c * CHUNK, CHUNK, "y0", "act%d_1" % (c + 1))
-                if c < EARLY:
-                    place(1, c * CHUNK, CHUNK, "y0")
+            place(0, c * CHUNK, CHUNK, "y0", "act%d_1" % (c + 1))
+            if c < EARLY:
+                place(1, c * CHUNK, CHUNK, "y0")
             if c + 1 < CHUNKS:
                 group_and_quantize_h(c + 1, rows)
-            if c == 0:
-                cleared_page(tile([P, T], F32, "page3", "h1"))
             if c + 2 < CHUNKS:
                 sums = up_chunk(c + 2)
             place(2 if c < EARLY else 1, c * CHUNK, CHUNK, "y2", "rows%d" % (c + 1))

@@ -37,14 +37,13 @@ AT_SM = AT_PAGE_1 + 4 * T
 AT_WU = AT_SM - ALIGN
 AT_WD_SCALES = AT_SM + ALIGN
 AT_WD = AT_WD_SCALES + N
-AT_LAST_SCALES = AT_WD + 4 * N
-AT_SCALES = AT_LAST_SCALES
+AT_PAGE_2 = AT_WD - ALIGN
+AT_SCALES = AT_PAGE_2 + 4 * T
 AT_WGO = AT_SCALES + R - ALIGN
 AT_PAGE_3 = AT_WGO + 4 * J
 AT_SECOND_H = AT_PAGE_3 + 4 * T - ALIGN
 AT_FIRST_H = AT_SECOND_H + 2 * PACK * CHUNK - ALIGN
 AT_LATER_S = AT_FIRST_H + ALIGN
-AT_PAGE_2 = AT_FIRST_H + 2 * PACK * HALF - ALIGN
 
 
 def tile_list_modp_gelu_noneP_kernel(

@@ -30,14 +30,14 @@ QUARTER = T // 4
 RUN = 4
 ALIGN = 64
 LOWER = 96
-ZEROS = 32
+ZEROS = 64
 EARLY = 2
-AT_PAGE_1 = 0
-AT_SM = AT_PAGE_1 + 4 * T
-AT_WU = AT_SM - ALIGN
-AT_WD_SCALES = AT_SM + ALIGN
-AT_WD = AT_WD_SCALES + N
-AT_PAGE_2 = AT_WD - ALIGN
+AT_TABLE = 0
+AT_SM = AT_TABLE + 4 * T
+AT_ZEROS = AT_SM - ALIGN
+AT_WD = AT_ZEROS + 4 * ZEROS - ALIGN
+AT_WD_SCALES = AT_WD + 4 * N
+AT_PAGE_2 = AT_WD_SCALES + N - ALIGN
 AT_SCALES = AT_PAGE_2 + 4 * T
 AT_WGO = AT_SCALES + R - ALIGN
 AT_PAGE_3 = AT_WGO + 4 * J
@@ -70,7 +70,7 @@ def tile_list_modp_gelu_noneP_kernel(
         offsets = sb.tile([P, J // LANES], U16, name="offsets")
         nc.sync.dma_start(offsets[:], offs)
 
-        zeros = tile([P, ZEROS], I32, "zeros")
+        zeros = placed([P, ZEROS], I32, "zeros", AT_ZEROS)
         nc.vector.memset(zeros[:], 0)
         tab_s = tile([P, T], U8, "tab_s")
         nc.vector.memset(tab_s[:].bitcast(I32), 0)
@@ -81,18 +81,21 @@ def tile_list_modp_gelu_noneP_kernel(
             zeros[:LOWER].unsqueeze(1).to_broadcast([LOWER, R // 4 // ZEROS, ZEROS]),
         )
         load_quadrant(w_s_raw[:], wu_scales, QUADS - 1, nc.scalar)
+        wd_s_raw = placed([P, N], U8, "wd_s_raw", AT_WD_SCALES)
+        nc.vector.memset(wd_s_raw[:].bitcast(I32), 0)
 
-        wu_raw = placed([P, 2 * R], U8, "wu_raw", AT_WU)
+        wu_raw = tile([P, 2 * R], U8, "wu_raw")
         nc.sync.dma_start(out=wu_raw[:].bitcast(I32), in_=wu_words[0].bitcast(I32))
         for q in range(QUADS):
             load_scale_rows(tab_s[:], tab_scales, q, nc.scalar if q >= QUADS // 2 else nc.sync)
-        tab_w = tile([P, T], I32, "tab_w", "zeros")
+        tab_w = placed([P, T], I32, "tab_w", AT_TABLE)
         nc.scalar.dma_start(out=tab_w[:], in_=tab_words[0].rearrange("p t i -> p (t i)").bitcast(I32))
         for q in range(QUADS - 1):
             load_quadrant(w_s_raw[:], wu_scales, q, nc.sync)
 
-        pages = [tile([P, T], F32, "page0")]
-        nc.vector.memset(pages[0][:], 0.0)
+        pages = [tile([P, T], F32, "page0"), tile([P, T], F32, "page1")]
+        for page in pages:
+            nc.vector.memset(page[:], 0.0)
 
         def cleared_page(page):
             nc.gpsimd.memset(page[:], 0.0)
@@ -104,15 +107,12 @@ def tile_list_modp_gelu_noneP_kernel(
             wu_raw[:].bitcast(U16).rearrange("p (m t) -> p t m", t=PACK),
         )
         wd_raw = placed([P, N], I32, "wd_raw", AT_WD)
-        nc.scalar.dma_start(out=wd_raw[:], in_=wd_words[0].rearrange("p n i -> p (n i)").bitcast(I32))
-        wd_s_raw = placed([P, N], U8, "wd_s_raw", AT_WD_SCALES)
-        nc.gpsimd.memset(wd_s_raw[:].bitcast(I32), 0)
+        nc.sync.dma_start(out=wd_raw[:], in_=wd_words[0].rearrange("p n i -> p (n i)").bitcast(I32))
         for q in range(QUADS - 1):
             load_scale_rows(wd_s_raw[:], wd_scales, q, nc.sync)
         sm_t = placed([P, PACK], F32, "sm_t", AT_SM)
         nc.sync.dma_start(out=sm_t[:], in_=sm.rearrange("(p t) -> p t", t=PACK))
         load_scale_rows(wd_s_raw[:], wd_scales, QUADS - 1, nc.sync)
-        cleared_page(placed([P, T], F32, "page1", AT_PAGE_1))
 
         def listed(first, count):
             return offsets[:, first // LANES : (first + count) // LANES]

@@ -1,6 +1,7 @@
 from contextlib import ExitStack
 
 import concourse.mybir as mybir
+from concourse.masks import make_identity
 
 K, R, N, T, J = 512, 512, 512, 2048, 1024
 FLOPS = 2 * K * R * J + 2 * R * N * J
@@ -16,6 +17,7 @@ FP4X4 = mybir.dt.float4_e2m1fn_x4
 GELU = mybir.ActivationFunctionType.Gelu_apprx_tanh
 COPY = mybir.ActivationFunctionType.Copy
 MULT = mybir.AluOpType.mult
+ADD = mybir.AluOpType.add
 
 P = 128
 PACK = 4
@@ -31,7 +33,6 @@ RUN = 4
 ALIGN = 64
 LOWER = 96
 ZEROS = 64
-EARLY = 2
 AT_TABLE = 0
 AT_SM = AT_TABLE + 4 * T
 AT_ZEROS = AT_SM - ALIGN
@@ -42,8 +43,12 @@ AT_SCALES = AT_PAGE_2 + 4 * T
 AT_WGO = AT_SCALES + R - ALIGN
 AT_PAGE_3 = AT_WGO + 4 * J
 AT_SECOND_H = AT_PAGE_3 + 4 * T - ALIGN
-AT_FIRST_H = AT_SECOND_H + 2 * PACK * CHUNK - ALIGN
-AT_LATER_S = AT_FIRST_H + ALIGN
+AT_FIRST_H = AT_SECOND_H + 2 * PACK * CHUNK
+AT_LATER_S = AT_FIRST_H
+AT_LAST_WORDS = AT_FIRST_H + 2 * PACK * HALF - ALIGN
+AT_PAIRS_0 = AT_LAST_WORDS + 4 * CHUNK
+AT_TURNED = AT_PAIRS_0 + 2 * PACK * SIDE - ALIGN
+AT_PAIRS_1 = AT_TURNED + 4 * BANK - ALIGN
 
 
 def tile_list_modp_gelu_noneP_kernel(
@@ -106,6 +111,8 @@ def tile_list_modp_gelu_noneP_kernel(
             wu_w[:].bitcast(U16).rearrange("p (t m) -> p t m", t=PACK),
             wu_raw[:].bitcast(U16).rearrange("p (m t) -> p t m", t=PACK),
         )
+        identity = tile([P, P], F32, "identity", "wu_raw")
+        make_identity(nc, identity[:])
         wd_raw = placed([P, N], I32, "wd_raw", AT_WD)
         nc.sync.dma_start(out=wd_raw[:], in_=wd_words[0].rearrange("p n i -> p (n i)").bitcast(I32))
         for q in range(QUADS - 1):
@@ -175,7 +182,8 @@ def tile_list_modp_gelu_noneP_kernel(
             return rows
 
         def group_and_quantize_h(c, rows):
-            grouped = tile([P, CHUNK * PACK], BF16, "h%d" % c)
+            shape = [P, CHUNK * PACK]
+            grouped = placed(shape, BF16, "h1", AT_SECOND_H) if c == 1 else tile(shape, BF16, "h%d" % c)
             nc.scalar.copy(
                 grouped[:].rearrange("p (n i t) -> p n t i", t=PACK, i=RUN),
                 rows[:].rearrange("p t (n i) -> p n t i", i=RUN),
@@ -198,7 +206,7 @@ def tile_list_modp_gelu_noneP_kernel(
         def scatter(page, y, first, count):
             nc.vector.tensor_tensor(page[:].indirect(listed(first, count)), y, wgo_t[:, first : first + count], MULT)
 
-        for c in range(1, CHUNKS):
+        for c in range(1, CHUNKS - 1):
             v_w[c] = gather_words(c * CHUNK, CHUNK, tile([P, CHUNK], U32, "v_w%d" % c)[:])
         wgo_t = placed([P, J], F32, "wgo_t", AT_WGO)
         nc.sync.dma_start(out=wgo_t[:], in_=wgo)
@@ -232,13 +240,17 @@ def tile_list_modp_gelu_noneP_kernel(
         quantize_h(first_h[0][:].rearrange("p n t -> p (n t)"), 0, HALF)
         nc.vector.tensor_copy(wd_s[:], raw_s[:, 0, :])
         quantize_h(first_h[1][:].rearrange("p n t -> p (n t)"), HALF, HALF)
-        second_h = placed([P, CHUNK, PACK], BF16, "h1", AT_SECOND_H)
-        times_sm(second_h[:, :HALF, :], grouped_gelu(1, 0))
         later_s = placed([P, PACK - 1, P], U8, "later_s", AT_LATER_S)
         nc.vector.tensor_copy(
             later_s[:].rearrange("p t (a m) -> p a t m", a=2), raw_s[:, 1:, :].rearrange("p t (a m) -> p a t m", a=2)
         )
         cleared_page(placed([P, T], F32, "page2", AT_PAGE_2))
+        last = CHUNKS - 1
+        v_w[last] = gather_words(last * CHUNK, CHUNK, placed([P, CHUNK], U32, "v_w_last", AT_LAST_WORDS)[:])
+        wgo_by_token = tile([P, J // P], F32, "wgo_by_token", "act0_0")
+        with nc.allow_non_contiguous_dma(reason="one weight a partition"):
+            nc.sync.dma_start(out=wgo_by_token[:], in_=wgo[0].rearrange("(b p) -> p b", p=P))
+        sums = up_chunk(1)
 
         def place(t, first, count, bank, after=None):
             y = tile([P, count], F32, "y%d_%d" % (t, first), after)
@@ -250,37 +262,48 @@ def tile_list_modp_gelu_noneP_kernel(
             down(first_y[:, half * HALF : (half + 1) * HALF], 0, half * HALF, HALF, bank)
         scatter(pages[0], first_y[:], 0, CHUNK)
 
-        act = tile([P, PACK, HALF], F32, "act1_1")
-        nc.scalar.activation(act[:], up_half(1, 1)[:], GELU)
-        rows = tile([P, PACK, HALF], BF16, "rows1")
-        for t in range(PACK):
-            nc.scalar.activation(rows[:, t, :], act[:, t, :], COPY, scale=sm_t[:, t : t + 1])
-        place(1, 0, CHUNK, "b0")
-        nc.scalar.copy(
-            second_h[:, HALF:, :].rearrange("p (n i) t -> p n t i", i=RUN),
-            rows[:].rearrange("p t (n i) -> p n t i", i=RUN),
-        )
-        quantize_h(second_h[:].rearrange("p n t -> p (n t)"), CHUNK, CHUNK)
+        rows = hidden_rows(1, sums)
+        place(1, 0, CHUNK, "y0")
+        group_and_quantize_h(1, rows)
         cleared_page(placed([P, T], F32, "page3", AT_PAGE_3))
         sums = up_chunk(2)
-        place(2, 0, CHUNK, "b1", "rows1")
+        place(2, 0, CHUNK, "y2", "rows1")
         for c in range(1, CHUNKS):
             if c + 1 < CHUNKS:
                 rows = hidden_rows(c + 1, sums)
             place(0, c * CHUNK, CHUNK, "y0", "act%d_1" % (c + 1))
-            if c < EARLY:
-                place(1, c * CHUNK, CHUNK, "y0")
+            place(1, c * CHUNK, CHUNK, "y0")
             if c + 1 < CHUNKS:
                 group_and_quantize_h(c + 1, rows)
             if c + 2 < CHUNKS:
                 sums = up_chunk(c + 2)
-            place(2 if c < EARLY else 1, c * CHUNK, CHUNK, "y2", "rows%d" % (c + 1))
+            place(2, c * CHUNK, CHUNK, "y2", "rows%d" % (c + 1))
 
-        place(2, EARLY * CHUNK, J - EARLY * CHUNK, "a0")
         last_y = tile([P, J], F32, "y3")
-        for half, bank in enumerate(("y2", "a1")):
-            down(last_y[:, half * BANK : (half + 1) * BANK], 3, half * BANK, BANK, bank)
-        scatter(pages[3], last_y[:], 0, J)
+        blocks = BANK // P
+        for half in range(J // BANK):
+            acc = ps.tile([P, blocks, P], F32, name="turned_sums%d" % half, tag="b%d" % half)
+            for b in range(blocks):
+                first = half * BANK + b * P
+                nc.tensor.matmul_mx(
+                    out=acc[:, b, :],
+                    lhsT=h_w[:, first : first + P].bitcast(FP8X4),
+                    lhsT_scale=h_s[:, first : first + P],
+                    rhs=wd_w[:, P * (PACK - 1) :].bitcast(FP8X4),
+                    rhs_scale=later_s[:, PACK - 2, :],
+                    start=True,
+                    stop=True,
+                )
+            shape = [P, blocks, P]
+            turned = placed(shape, F32, "turned1", AT_TURNED) if half else tile(shape, F32, "turned0", "h%d" % last)
+            for b in range(blocks):
+                at = half * blocks + b
+                nc.scalar.activation(turned[:, b, :], acc[:, b, :], COPY, scale=wgo_by_token[:, at : at + 1])
+            back = ps.tile([P, blocks, P], F32, name="back%d" % half, tag="a%d" % half)
+            for b in range(blocks):
+                nc.tensor.transpose(back[:, b, :], turned[:, b, :], identity[:])
+            nc.scalar.copy(last_y[:, half * BANK : (half + 1) * BANK], back[:].rearrange("p b j -> p (b j)"))
+        nc.vector.tensor_copy(pages[3][:].indirect(offsets[:]), last_y[:])
 
         out_rows = out_0.rearrange("(p t) n -> p t n", t=PACK)
         out_words = out_1[0].rearrange("p t i -> p (t i)")
@@ -288,7 +311,8 @@ def tile_list_modp_gelu_noneP_kernel(
         vector_pieces = SIDE // QUARTER
         groups = [tile([P, count * PACK], BF16, "out_grouped%d" % first) for first, count in pieces]
         pairs = [
-            tile([P, SIDE // CHUNK, 2, CHUNK, 2], BF16, "out_pairs%d" % side, ("h_w", "h_s")[side]) for side in range(2)
+            placed([P, SIDE // CHUNK, 2, CHUNK, 2], BF16, "out_pairs%d" % side, (AT_PAIRS_0, AT_PAIRS_1)[side])
+            for side in range(2)
         ]
 
         def page_columns(t, first, count):
@@ -298,8 +322,9 @@ def tile_list_modp_gelu_noneP_kernel(
             nc.sync.dma_start(out=out_rows[:, t, :], in_=pages[t][:])
             for side in range(2):
                 cols = page_columns(t, side * SIDE, SIDE)
-                if t == 2 and side == 0:
-                    nc.scalar.copy(pairs[0][:, :, 1, :, :], cols.unsqueeze(3).to_broadcast([P, SIDE // CHUNK, CHUNK, 2]))
+                if t == 2:
+                    both = cols.unsqueeze(3).to_broadcast([P, SIDE // CHUNK, CHUNK, 2])
+                    nc.gpsimd.tensor_scalar(pairs[side][:, :, 1, :, :], both, 1.0, 0.0, MULT, ADD)
                 else:
                     nc.scalar.copy(pairs[side][:, :, t // 2, :, t % 2], cols)
         nc.sync.dma_start(out=out_rows[:, 3, :], in_=pages[3][:])

@@ -26,9 +26,12 @@ LANES = 16
 CHUNK = 256
 CHUNKS = J // CHUNK
 HALF = CHUNK // 2
+STEP = HALF // 2
 BANK = 512
 SIDE = T // 2
 QUARTER = T // 4
+BLOCK = 64
+SHARE = 896
 RUN = 4
 ALIGN = 64
 LOWER = 96
@@ -47,8 +50,8 @@ AT_FIRST_H = AT_SECOND_H + 2 * PACK * CHUNK
 AT_LATER_S = AT_FIRST_H
 AT_LAST_WORDS = AT_FIRST_H + 2 * PACK * HALF - ALIGN
 AT_PAIRS_0 = AT_LAST_WORDS + 4 * CHUNK
-AT_TURNED = AT_PAIRS_0 + 2 * PACK * SIDE - ALIGN
-AT_PAIRS_1 = AT_TURNED + 4 * BANK - ALIGN
+AT_TURNED = AT_PAIRS_0 + 2 * PACK * SHARE - ALIGN
+AT_PAIRS_1 = AT_TURNED + 4 * CHUNK - ALIGN
 
 
 def tile_list_modp_gelu_noneP_kernel(
@@ -221,19 +224,17 @@ def tile_list_modp_gelu_noneP_kernel(
                 up_sums(acc[:, t, :], c, t, half * HALF, HALF)
             return acc
 
-        def grouped_gelu(c, half):
-            act = tile([P, HALF, PACK], F32, "act%d_%d" % (c, half))
-            nc.scalar.activation(act[:], up_half(c, half)[:].rearrange("p t n -> p n t"), GELU)
-            return act
-
-        def times_sm(grouped, act):
-            nc.vector.tensor_tensor(grouped, act[:], sm_t[:].unsqueeze(1).to_broadcast([P, HALF, PACK]), MULT)
-
         first_h = []
         for half in range(2):
             shape = [P, HALF, PACK]
             grouped = placed(shape, BF16, "h0_1", AT_FIRST_H) if half else tile(shape, BF16, "h0_0")
-            times_sm(grouped[:], grouped_gelu(0, half))
+            acc = up_half(0, half)
+            for first in range(0, HALF, STEP):
+                act = tile([P, STEP, PACK], F32, "act0_%d" % (half * HALF + first))
+                nc.scalar.activation(act[:], acc[:, :, first : first + STEP].rearrange("p t n -> p n t"), GELU)
+                nc.vector.tensor_tensor(
+                    grouped[:, first : first + STEP, :], act[:], sm_t[:].unsqueeze(1).to_broadcast([P, STEP, PACK]), MULT
+                )
             first_h.append(grouped)
         wd_s = tile([P, P], U8, "wd_s")
         raw_s = wd_s_raw[:].rearrange("p (m t) -> p t m", t=PACK)
@@ -277,90 +278,95 @@ def tile_list_modp_gelu_noneP_kernel(
                 group_and_quantize_h(c + 1, rows)
             if c + 2 < CHUNKS:
                 sums = up_chunk(c + 2)
-            place(2, c * CHUNK, CHUNK, "y2", "rows%d" % (c + 1))
+            if c < last:
+                place(2, c * CHUNK, CHUNK, "y2", "rows%d" % (c + 1))
 
-        last_y = tile([P, J], F32, "y3")
-        blocks = BANK // P
-        for half in range(J // BANK):
-            acc = ps.tile([P, blocks, P], F32, name="turned_sums%d" % half, tag="b%d" % half)
+        def turned_back(first, count, t, turned, banks, outs):
+            blocks, wide = count // P, PACK - t
+            acc = ps.tile([P, blocks, wide * P], F32, name="turned_sums%d" % first, tag=banks[0])
             for b in range(blocks):
-                first = half * BANK + b * P
+                at = first + b * P
                 nc.tensor.matmul_mx(
                     out=acc[:, b, :],
-                    lhsT=h_w[:, first : first + P].bitcast(FP8X4),
-                    lhsT_scale=h_s[:, first : first + P],
-                    rhs=wd_w[:, P * (PACK - 1) :].bitcast(FP8X4),
-                    rhs_scale=later_s[:, PACK - 2, :],
+                    lhsT=h_w[:, at : at + P].bitcast(FP8X4),
+                    lhsT_scale=h_s[:, at : at + P],
+                    rhs=wd_w[:, P * t :].bitcast(FP8X4),
+                    rhs_scale=later_s[:, t - 1 :, :].rearrange("p t m -> p (t m)"),
                     start=True,
                     stop=True,
                 )
-            shape = [P, blocks, P]
-            turned = placed(shape, F32, "turned1", AT_TURNED) if half else tile(shape, F32, "turned0", "h%d" % last)
             for b in range(blocks):
-                at = half * blocks + b
+                at = first // P + b
                 nc.scalar.activation(turned[:, b, :], acc[:, b, :], COPY, scale=wgo_by_token[:, at : at + 1])
-            back = ps.tile([P, blocks, P], F32, name="back%d" % half, tag="a%d" % half)
-            for b in range(blocks):
-                nc.tensor.transpose(back[:, b, :], turned[:, b, :], identity[:])
-            nc.scalar.copy(last_y[:, half * BANK : (half + 1) * BANK], back[:].rearrange("p b j -> p (b j)"))
+            back = ps.tile([P, wide, count], F32, name="back%d" % first, tag=banks[1])
+            for e in range(wide):
+                for b in range(blocks):
+                    nc.tensor.transpose(back[:, e, b * P : (b + 1) * P], turned[:, b, e * P : (e + 1) * P], identity[:])
+            for e in range(wide):
+                nc.scalar.copy(outs[e], back[:, e, :])
+
+        last_y = tile([P, J], F32, "y3")
+        y2_last = tile([P, CHUNK], F32, "y2_last")
+        tail = last * CHUNK
+        turned_back(tail, CHUNK, 2, tile([P, 2, 2 * P], F32, "turned_c"), ("b0", "a0"), [y2_last[:], last_y[:, tail:]])
+        nc.vector.tensor_copy(pages[2][:].indirect(listed(tail, CHUNK)), y2_last[:])
+        turned_back(0, BANK, 3, tile([P, BANK // P, P], F32, "turned_a", "h2"), ("n0", "n1"), [last_y[:, :BANK]])
+        turned_back(BANK, CHUNK, 3, placed([P, 2, P], F32, "turned_b", AT_TURNED), ("b1", "a1"), [last_y[:, BANK:tail]])
         nc.vector.tensor_copy(pages[3][:].indirect(offsets[:]), last_y[:])
 
         out_rows = out_0.rearrange("(p t) n -> p t n", t=PACK)
         out_words = out_1[0].rearrange("p t i -> p (t i)")
-        pieces = [(0, QUARTER), (QUARTER, QUARTER), (2 * QUARTER, QUARTER), (3 * QUARTER, CHUNK), (T - CHUNK, CHUNK)]
-        vector_pieces = SIDE // QUARTER
-        groups = [tile([P, count * PACK], BF16, "out_grouped%d" % first) for first, count in pieces]
+        shares = [(0, SHARE), (SHARE, T - SHARE)]
         pairs = [
-            placed([P, SIDE // CHUNK, 2, CHUNK, 2], BF16, "out_pairs%d" % side, (AT_PAIRS_0, AT_PAIRS_1)[side])
-            for side in range(2)
+            placed([P, count // BLOCK, 2, BLOCK, 2], BF16, "out_pairs%d" % first, at)
+            for (first, count), at in zip(shares, (AT_PAIRS_0, AT_PAIRS_1))
         ]
+        grouped = tile([P, T * PACK], BF16, "out_grouped")
 
         def page_columns(t, first, count):
-            return pages[t][:, first : first + count].rearrange("p (b n) -> p b n", n=CHUNK)
+            return pages[t][:, first : first + count].rearrange("p (b n) -> p b n", n=BLOCK)
+
+        def gpsimd_copy(out, in_):
+            nc.gpsimd.tensor_scalar(out, in_, 1.0, 0.0, MULT, ADD)
 
         for t in range(PACK - 1):
             nc.sync.dma_start(out=out_rows[:, t, :], in_=pages[t][:])
-            for side in range(2):
-                cols = page_columns(t, side * SIDE, SIDE)
+            for (first, count), rounded, copy in zip(shares, pairs, (gpsimd_copy, nc.scalar.copy)):
+                cols = page_columns(t, first, count)
                 if t == 2:
-                    both = cols.unsqueeze(3).to_broadcast([P, SIDE // CHUNK, CHUNK, 2])
-                    nc.gpsimd.tensor_scalar(pairs[side][:, :, 1, :, :], both, 1.0, 0.0, MULT, ADD)
+                    copy(rounded[:, :, 1, :, :], cols.unsqueeze(3).to_broadcast([P, count // BLOCK, BLOCK, 2]))
                 else:
-                    nc.scalar.copy(pairs[side][:, :, t // 2, :, t % 2], cols)
+                    copy(rounded[:, :, 0, :, t], cols)
         nc.sync.dma_start(out=out_rows[:, 3, :], in_=pages[3][:])
 
-        def pairs_of(i):
-            first, count = pieces[i]
-            side, col = divmod(first, SIDE)
-            return pairs[side][:, col // CHUNK : (col + count) // CHUNK]
-
-        def round_page_3(copy, i):
-            copy(pairs_of(i)[:, :, 1, :, 1], page_columns(3, *pieces[i]))
-
-        def group_words(copy, i):
+        def group_words(copy, rounded, first, count):
             copy(
-                groups[i][:].bitcast(F32).rearrange("p (b n u) -> p b n u", u=2, n=CHUNK),
-                pairs_of(i).rearrange("p b u n e -> p b (u n e)").bitcast(F32).rearrange("p b (u n) -> p b n u", u=2),
+                grouped[:, PACK * first : PACK * (first + count)].bitcast(F32).rearrange("p (b n u) -> p b n u", u=2, n=BLOCK),
+                rounded.rearrange("p b u n e -> p b (u n e)").bitcast(F32).rearrange("p b (u n) -> p b n u", u=2),
             )
 
-        for i in range(vector_pieces):
-            round_page_3(nc.vector.tensor_copy, i)
-        for i in range(vector_pieces):
-            group_words(nc.vector.tensor_copy, i)
-        for i in range(vector_pieces, len(pieces)):
-            round_page_3(nc.scalar.copy, i)
-            group_words(nc.scalar.copy, i)
+        group_words(nc.scalar.copy, pairs[1][:], *shares[1])
+        vector_parts = [(0, QUARTER), (QUARTER, SHARE - QUARTER)]
+        for first, count in vector_parts:
+            nc.vector.tensor_copy(
+                pairs[0][:, first // BLOCK : (first + count) // BLOCK, 1, :, 1], page_columns(3, first, count)
+            )
+        for first, count in vector_parts:
+            group_words(nc.vector.tensor_copy, pairs[0][:, first // BLOCK : (first + count) // BLOCK], first, count)
+        for first, end in ((SHARE, 3 * QUARTER), (3 * QUARTER, T - CHUNK), (T - CHUNK, T)):
+            nc.scalar.copy(grouped[:].rearrange("p (n t) -> p n t", t=PACK)[:, first:end, PACK - 1], pages[3][:, first:end])
 
         out_s = tile([P, SIDE], U8, "out_s")
-        for i, (first, count) in enumerate(pieces):
-            codes = tile([P, count], U32, "out_w%d" % first)
-            side, col = divmod(first, SIDE)
-            nc.vector.quantize_mx(
-                out=codes[:].bitcast(FP8X4), scales=out_s[4 * side : P, col : col + count], in_=groups[i][:]
-            )
-            nc.sync.dma_start(
-                out=out_words[:, PACK * first : PACK * (first + count)].bitcast(I32), in_=codes[:].bitcast(I32)
-            )
+        for cuts in ((0, QUARTER), (QUARTER, SHARE, SIDE), (SIDE, 3 * QUARTER), (3 * QUARTER, T - CHUNK), (T - CHUNK, T)):
+            codes = tile([P, cuts[-1] - cuts[0]], U32, "out_w%d" % cuts[0])
+            for first, end in zip(cuts, cuts[1:]):
+                side, col = divmod(first, SIDE)
+                nc.vector.quantize_mx(
+                    out=codes[:, first - cuts[0] : end - cuts[0]].bitcast(FP8X4),
+                    scales=out_s[4 * side : P, col : col + end - first],
+                    in_=grouped[:, PACK * first : PACK * end],
+                )
+            nc.sync.dma_start(out=out_words[:, PACK * cuts[0] : PACK * cuts[-1]].bitcast(I32), in_=codes[:].bitcast(I32))
         for q in range(QUADS):
             queue = nc.scalar if q >= QUADS // 2 else nc.sync
             queue.dma_start(

@@ -30,8 +30,8 @@ STEP = HALF // 2
 BANK = 512
 SIDE = T // 2
 QUARTER = T // 4
-BLOCK = 64
-SHARE = 896
+BLOCK = 32
+SHARE = 960
 RUN = 4
 ALIGN = 64
 LOWER = 96
@@ -316,48 +316,43 @@ def tile_list_modp_gelu_noneP_kernel(
 
         out_rows = out_0.rearrange("(p t) n -> p t n", t=PACK)
         out_words = out_1[0].rearrange("p t i -> p (t i)")
-        shares = [(0, SHARE), (SHARE, T - SHARE)]
-        pairs = [
-            placed([P, count // BLOCK, 2, BLOCK, 2], BF16, "out_pairs%d" % first, at)
-            for (first, count), at in zip(shares, (AT_PAIRS_0, AT_PAIRS_1))
-        ]
         grouped = tile([P, T * PACK], BF16, "out_grouped")
-
-        def page_columns(t, first, count):
-            return pages[t][:, first : first + count].rearrange("p (b n) -> p b n", n=BLOCK)
+        by_column = grouped[:].rearrange("p (n t) -> p n t", t=PACK)
 
         def gpsimd_copy(out, in_):
             nc.gpsimd.tensor_scalar(out, in_, 1.0, 0.0, MULT, ADD)
 
-        for t in range(PACK - 1):
+        def blocks_of(columns, part):
+            first, count, step = part
+            names = "p (b n) u -> p b n u" if columns.ndim == 3 else "p (b n) -> p b n"
+            return columns.rearrange(names, n=BLOCK)[:, first : first + (count - 1) * step + 1 : step]
+
+        odd = (T - SHARE) // BLOCK // 2
+        parts = [(0, SHARE // BLOCK, 1), (SHARE // BLOCK, odd, 2), (SHARE // BLOCK + 1, odd, 2)]
+        pairs = [
+            placed([P, parts[0][1], 2, BLOCK, 2], BF16, "out_pairs0", AT_PAIRS_0),
+            placed([P, odd, 2, BLOCK, 2], BF16, "out_pairs1", AT_PAIRS_1),
+            tile([P, odd, 2, BLOCK, 2], BF16, "out_pairs2", "y2_last"),
+        ]
+        for t in range(PACK):
             nc.sync.dma_start(out=out_rows[:, t, :], in_=pages[t][:])
-            for (first, count), rounded, copy in zip(shares, pairs, (gpsimd_copy, nc.scalar.copy)):
-                cols = page_columns(t, first, count)
-                if t == 2:
-                    copy(rounded[:, :, 1, :, :], cols.unsqueeze(3).to_broadcast([P, count // BLOCK, BLOCK, 2]))
-                else:
-                    copy(rounded[:, :, 0, :, t], cols)
-        nc.sync.dma_start(out=out_rows[:, 3, :], in_=pages[3][:])
-
-        def group_words(copy, rounded, first, count):
-            copy(
-                grouped[:, PACK * first : PACK * (first + count)].bitcast(F32).rearrange("p (b n u) -> p b n u", u=2, n=BLOCK),
-                rounded.rearrange("p b u n e -> p b (u n e)").bitcast(F32).rearrange("p b (u n) -> p b n u", u=2),
+        for part, rounded, copy in zip(parts, pairs, (nc.scalar.copy, gpsimd_copy, gpsimd_copy)):
+            for t in range(2):
+                copy(rounded[:, :, 0, :, t], blocks_of(pages[t][:], part))
+            copy(rounded[:, :, 1, :, :], blocks_of(pages[2][:], part).unsqueeze(3).to_broadcast([P, part[1], BLOCK, 2]))
+        words = grouped[:].bitcast(F32).rearrange("p (n u) -> p n u", u=2)
+        for part, rounded in zip(parts, pairs):
+            nc.scalar.copy(
+                blocks_of(words, part),
+                rounded[:].rearrange("p b u n e -> p b (u n e)").bitcast(F32).rearrange("p b (u n) -> p b n u", u=2),
             )
-
-        group_words(nc.scalar.copy, pairs[1][:], *shares[1])
-        vector_parts = [(0, QUARTER), (QUARTER, SHARE - QUARTER)]
-        for first, count in vector_parts:
-            nc.vector.tensor_copy(
-                pairs[0][:, first // BLOCK : (first + count) // BLOCK, 1, :, 1], page_columns(3, first, count)
-            )
-        for first, count in vector_parts:
-            group_words(nc.vector.tensor_copy, pairs[0][:, first // BLOCK : (first + count) // BLOCK], first, count)
+        for first, end in ((0, QUARTER), (QUARTER, SHARE)):
+            nc.vector.tensor_copy(by_column[:, first:end, PACK - 1], pages[3][:, first:end])
         for first, end in ((SHARE, 3 * QUARTER), (3 * QUARTER, T - CHUNK), (T - CHUNK, T)):
-            nc.scalar.copy(grouped[:].rearrange("p (n t) -> p n t", t=PACK)[:, first:end, PACK - 1], pages[3][:, first:end])
+            nc.scalar.copy(by_column[:, first:end, PACK - 1], pages[3][:, first:end])
 
         out_s = tile([P, SIDE], U8, "out_s")
-        for cuts in ((0, QUARTER), (QUARTER, SHARE, SIDE), (SIDE, 3 * QUARTER), (3 * QUARTER, T - CHUNK), (T - CHUNK, T)):
+        for cuts in ((0, QUARTER), (QUARTER, SIDE), (SIDE, 3 * QUARTER), (3 * QUARTER, T - CHUNK), (T - CHUNK, T)):
             codes = tile([P, cuts[-1] - cuts[0]], U32, "out_w%d" % cuts[0])
             for first, end in zip(cuts, cuts[1:]):
                 side, col = divmod(first, SIDE)

@@ -43,15 +43,18 @@ AT_WD = AT_ZEROS + 4 * ZEROS - ALIGN
 AT_WD_SCALES = AT_WD + 4 * N
 AT_PAGE_2 = AT_WD_SCALES + N - ALIGN
 AT_SCALES = AT_PAGE_2 + 4 * T
-AT_WGO = AT_SCALES + R - ALIGN
-AT_PAGE_3 = AT_WGO + 4 * J
+AT_PAGE_3 = AT_SCALES + R
 AT_SECOND_H = AT_PAGE_3 + 4 * T - ALIGN
 AT_FIRST_H = AT_SECOND_H + 2 * PACK * CHUNK
 AT_LATER_S = AT_FIRST_H
+AT_LAST_SCALES = AT_LATER_S + (PACK - 1) * P
 AT_LAST_WORDS = AT_FIRST_H + 2 * PACK * HALF - ALIGN
 AT_PAIRS_0 = AT_LAST_WORDS + 4 * CHUNK
 AT_TURNED = AT_PAIRS_0 + 2 * PACK * SHARE - ALIGN
 AT_PAIRS_1 = AT_TURNED + 4 * CHUNK - ALIGN
+AT_IDENTITY = AT_PAIRS_1 + 2 * PACK * SIDE
+AT_WU = AT_IDENTITY + 4 * P - ALIGN
+AT_WGO = AT_WU + 2 * R - ALIGN
 
 
 def tile_list_modp_gelu_noneP_kernel(
@@ -92,7 +95,7 @@ def tile_list_modp_gelu_noneP_kernel(
         wd_s_raw = placed([P, N], U8, "wd_s_raw", AT_WD_SCALES)
         nc.vector.memset(wd_s_raw[:].bitcast(I32), 0)
 
-        wu_raw = tile([P, 2 * R], U8, "wu_raw")
+        wu_raw = placed([P, 2 * R], U8, "wu_raw", AT_WU)
         nc.sync.dma_start(out=wu_raw[:].bitcast(I32), in_=wu_words[0].bitcast(I32))
         for q in range(QUADS):
             load_scale_rows(tab_s[:], tab_scales, q, nc.scalar if q >= QUADS // 2 else nc.sync)
@@ -114,7 +117,7 @@ def tile_list_modp_gelu_noneP_kernel(
             wu_w[:].bitcast(U16).rearrange("p (t m) -> p t m", t=PACK),
             wu_raw[:].bitcast(U16).rearrange("p (m t) -> p t m", t=PACK),
         )
-        identity = tile([P, P], F32, "identity", "wu_raw")
+        identity = placed([P, P], F32, "identity", AT_IDENTITY)
         make_identity(nc, identity[:])
         wd_raw = placed([P, N], I32, "wd_raw", AT_WD)
         nc.sync.dma_start(out=wd_raw[:], in_=wd_words[0].rearrange("p n i -> p (n i)").bitcast(I32))
@@ -135,15 +138,17 @@ def tile_list_modp_gelu_noneP_kernel(
             nc.vector.tensor_copy(scales[:], tab_s[:].indirect(listed(first, count)))
             return scales
 
-        all_s = gather_scales(0, J, tile([P, J], U8, "all_s"))
-        v_s = {c: all_s[:, c * CHUNK : (c + 1) * CHUNK] for c in range(CHUNKS)}
+        early_s = gather_scales(0, J - CHUNK, tile([P, J - CHUNK], U8, "early_s"))
+        v_s = {c: early_s[:, c * CHUNK : (c + 1) * CHUNK] for c in range(CHUNKS - 1)}
         v_w = {0: tile([P, CHUNK], U32, "v_w0")[:]}
         for half in range(2):
             gather_words(half * HALF, HALF, v_w[0][:, half * HALF : (half + 1) * HALF])
         w_s = tile([P, R], U8, "w_s")
-        nc.gpsimd.tensor_copy(
-            w_s[:].rearrange("p (t m) -> p t m", t=PACK), w_s_raw[:].rearrange("p (m t) -> p t m", t=PACK)
-        )
+        for u in range(2):
+            nc.gpsimd.tensor_copy(
+                w_s[:].rearrange("p (t m) -> p t m", t=PACK)[:, 2 * u : 2 * u + 2, :],
+                w_s_raw[:].rearrange("p (m t) -> p t m", t=PACK)[:, 2 * u : 2 * u + 2, :],
+            )
 
         def up_sums(out, c, t, first, count):
             nc.tensor.matmul_mx(
@@ -242,12 +247,13 @@ def tile_list_modp_gelu_noneP_kernel(
         nc.vector.tensor_copy(wd_s[:], raw_s[:, 0, :])
         quantize_h(first_h[1][:].rearrange("p n t -> p (n t)"), HALF, HALF)
         later_s = placed([P, PACK - 1, P], U8, "later_s", AT_LATER_S)
-        nc.vector.tensor_copy(
-            later_s[:].rearrange("p t (a m) -> p a t m", a=2), raw_s[:, 1:, :].rearrange("p t (a m) -> p a t m", a=2)
+        nc.gpsimd.tensor_copy(
+            later_s[:], raw_s[:, 1:, :]
         )
         cleared_page(placed([P, T], F32, "page2", AT_PAGE_2))
         last = CHUNKS - 1
         v_w[last] = gather_words(last * CHUNK, CHUNK, placed([P, CHUNK], U32, "v_w_last", AT_LAST_WORDS)[:])
+        v_s[last] = gather_scales(last * CHUNK, CHUNK, placed([P, CHUNK], U8, "last_s", AT_LAST_SCALES))[:]
         wgo_by_token = tile([P, J // P], F32, "wgo_by_token", "act0_0")
         with nc.allow_non_contiguous_dma(reason="one weight a partition"):
             nc.sync.dma_start(out=wgo_by_token[:], in_=wgo[0].rearrange("(b p) -> p b", p=P))

@@ -113,9 +113,8 @@ def tile_list_modp_gelu_noneP_kernel(
             pages.append(page)
 
         wu_w = tile([P, 2 * R], U8, "wu_w")
-        nc.vector.tensor_copy(
-            wu_w[:].bitcast(U16).rearrange("p (t m) -> p t m", t=PACK),
-            wu_raw[:].bitcast(U16).rearrange("p (m t) -> p t m", t=PACK),
+        nc.gpsimd.tensor_copy(
+            wu_w[:].rearrange("p (t m b) -> p t m b", t=PACK, b=2), wu_raw[:].rearrange("p (m t b) -> p t m b", t=PACK, b=2)
         )
         identity = placed([P, P], F32, "identity", AT_IDENTITY)
         make_identity(nc, identity[:])
@@ -144,11 +143,9 @@ def tile_list_modp_gelu_noneP_kernel(
         for half in range(2):
             gather_words(half * HALF, HALF, v_w[0][:, half * HALF : (half + 1) * HALF])
         w_s = tile([P, R], U8, "w_s")
-        for u in range(2):
-            nc.gpsimd.tensor_copy(
-                w_s[:].rearrange("p (t m) -> p t m", t=PACK)[:, 2 * u : 2 * u + 2, :],
-                w_s_raw[:].rearrange("p (m t) -> p t m", t=PACK)[:, 2 * u : 2 * u + 2, :],
-            )
+        nc.gpsimd.tensor_copy(
+            w_s[:].rearrange("p (t m) -> p t m", t=PACK), w_s_raw[:].rearrange("p (m t) -> p t m", t=PACK)
+        )
 
         def up_sums(out, c, t, first, count):
             nc.tensor.matmul_mx(
@@ -182,7 +179,7 @@ def tile_list_modp_gelu_noneP_kernel(
             rows = tile([P, PACK, CHUNK], BF16, "rows%d" % c)
             acts = []
             for u, acc in enumerate(sums):
-                act = tile([P, 2, CHUNK], F32, "act%d_%d" % (c, u))
+                act = tile([P, 2, CHUNK], F32, "act%d_%d" % (c, u), "act0_0" if (c, u) == (1, 0) else None)
                 nc.scalar.activation(act[:], acc[:], GELU)
                 acts.append(act)
             for t in range(PACK):
@@ -203,7 +200,7 @@ def tile_list_modp_gelu_noneP_kernel(
             nc.tensor.matmul_mx(
                 out=acc[:],
                 lhsT=wd_w[:, P * t : P * (t + 1)].bitcast(FP8X4),
-                lhsT_scale=later_s[:, t - 1, :] if t else wd_s[:],
+                lhsT_scale=(wd_s, later_s)[t // 2][:, t % 2, :],
                 rhs=h_w[:, first : first + count].bitcast(FP8X4),
                 rhs_scale=h_s[:, first : first + count],
                 start=True,
@@ -229,32 +226,39 @@ def tile_list_modp_gelu_noneP_kernel(
                 up_sums(acc[:, t, :], c, t, half * HALF, HALF)
             return acc
 
-        first_h = []
-        for half in range(2):
-            shape = [P, HALF, PACK]
-            grouped = placed(shape, BF16, "h0_1", AT_FIRST_H) if half else tile(shape, BF16, "h0_0")
-            acc = up_half(0, half)
-            for first in range(0, HALF, STEP):
-                act = tile([P, STEP, PACK], F32, "act0_%d" % (half * HALF + first))
-                nc.scalar.activation(act[:], acc[:, :, first : first + STEP].rearrange("p t n -> p n t"), GELU)
-                nc.vector.tensor_tensor(
-                    grouped[:, first : first + STEP, :], act[:], sm_t[:].unsqueeze(1).to_broadcast([P, STEP, PACK]), MULT
-                )
-            first_h.append(grouped)
-        wd_s = tile([P, P], U8, "wd_s")
+        def times_sm(grouped, act):
+            by_pair = sm_t[:].rearrange("p (u e) -> p u e", e=2)
+            nc.vector.tensor_tensor(grouped, act, by_pair.unsqueeze(1).to_broadcast([P, STEP, 2, 2]), MULT)
+
+        first_h = [tile([P, HALF, 2, 2], BF16, "h0_0"), placed([P, HALF, 2, 2], BF16, "h0_1", AT_FIRST_H)]
+        act = tile([P, 2, HALF, 2], F32, "act0_0")
+        for u, bank in enumerate(("a0", "n0")):
+            acc = ps.tile([P, 2, HALF], F32, name="first_sums%d" % u, tag=bank)
+            for e in range(2):
+                up_sums(acc[:, e, :], 0, 2 * u + e, 0, HALF)
+            for first in range(0, HALF, STEP if u else HALF):
+                end = first + (STEP if u else HALF)
+                nc.scalar.activation(act[:, u, first:end, :], acc[:, :, first:end].rearrange("p e n -> p n e"), GELU)
+        for first in range(0, HALF, STEP):
+            part = slice(first, first + STEP)
+            times_sm(first_h[0][:, part], act[:, :, part, :].rearrange("p u n e -> p n u e"))
+        acc = up_half(0, 1)
+        for first in range(0, HALF, STEP):
+            act = tile([P, STEP, PACK], F32, "act0_%d" % (HALF + first))
+            nc.scalar.activation(act[:], acc[:, :, first : first + STEP].rearrange("p t n -> p n t"), GELU)
+            times_sm(first_h[1][:, first : first + STEP], act[:].rearrange("p n (u e) -> p n u e", e=2))
+        wd_s = tile([P, 2, P], U8, "wd_s")
         raw_s = wd_s_raw[:].rearrange("p (m t) -> p t m", t=PACK)
-        quantize_h(first_h[0][:].rearrange("p n t -> p (n t)"), 0, HALF)
-        nc.vector.tensor_copy(wd_s[:], raw_s[:, 0, :])
-        quantize_h(first_h[1][:].rearrange("p n t -> p (n t)"), HALF, HALF)
-        later_s = placed([P, PACK - 1, P], U8, "later_s", AT_LATER_S)
-        nc.gpsimd.tensor_copy(
-            later_s[:], raw_s[:, 1:, :]
-        )
+        quantize_h(first_h[0][:].rearrange("p n u e -> p (n u e)"), 0, HALF)
+        nc.vector.tensor_copy(wd_s[:], raw_s[:, :2, :])
+        quantize_h(first_h[1][:].rearrange("p n u e -> p (n u e)"), HALF, HALF)
+        later_s = placed([P, 2, P], U8, "later_s", AT_LATER_S)
+        nc.gpsimd.tensor_copy(later_s[:], raw_s[:, 2:, :])
         cleared_page(placed([P, T], F32, "page2", AT_PAGE_2))
         last = CHUNKS - 1
         v_w[last] = gather_words(last * CHUNK, CHUNK, placed([P, CHUNK], U32, "v_w_last", AT_LAST_WORDS)[:])
         v_s[last] = gather_scales(last * CHUNK, CHUNK, placed([P, CHUNK], U8, "last_s", AT_LAST_SCALES))[:]
-        wgo_by_token = tile([P, J // P], F32, "wgo_by_token", "act0_0")
+        wgo_by_token = tile([P, J // P], F32, "wgo_by_token", "act0_%d" % HALF)
         with nc.allow_non_contiguous_dma(reason="one weight a partition"):
             nc.sync.dma_start(out=wgo_by_token[:], in_=wgo[0].rearrange("(b p) -> p b", p=P))
         sums = up_chunk(1)
@@ -297,7 +301,7 @@ def tile_list_modp_gelu_noneP_kernel(
                     lhsT=h_w[:, at : at + P].bitcast(FP8X4),
                     lhsT_scale=h_s[:, at : at + P],
                     rhs=wd_w[:, P * t :].bitcast(FP8X4),
-                    rhs_scale=later_s[:, t - 1 :, :].rearrange("p t m -> p (t m)"),
+                    rhs_scale=later_s[:, t - 2 :, :].rearrange("p t m -> p (t m)"),
                     start=True,
                     stop=True,
                 )

@@ -113,8 +113,9 @@ def tile_list_modp_gelu_noneP_kernel(
             pages.append(page)
 
         wu_w = tile([P, 2 * R], U8, "wu_w")
-        nc.gpsimd.tensor_copy(
-            wu_w[:].rearrange("p (t m b) -> p t m b", t=PACK, b=2), wu_raw[:].rearrange("p (m t b) -> p t m b", t=PACK, b=2)
+        nc.vector.tensor_copy(
+            wu_w[:].bitcast(U16).rearrange("p (t m) -> p t m", t=PACK),
+            wu_raw[:].bitcast(U16).rearrange("p (m t) -> p t m", t=PACK),
         )
         identity = placed([P, P], F32, "identity", AT_IDENTITY)
         make_identity(nc, identity[:])

@@ -121,11 +121,10 @@ def tile_list_modp_gelu_noneP_kernel(
         make_identity(nc, identity[:])
         wd_raw = placed([P, N], I32, "wd_raw", AT_WD)
         nc.sync.dma_start(out=wd_raw[:], in_=wd_words[0].rearrange("p n i -> p (n i)").bitcast(I32))
-        for q in range(QUADS - 1):
-            load_scale_rows(wd_s_raw[:], wd_scales, q, nc.sync)
         sm_t = placed([P, PACK], F32, "sm_t", AT_SM)
         nc.sync.dma_start(out=sm_t[:], in_=sm.rearrange("(p t) -> p t", t=PACK))
-        load_scale_rows(wd_s_raw[:], wd_scales, QUADS - 1, nc.sync)
+        for q in range(QUADS):
+            load_scale_rows(wd_s_raw[:], wd_scales, q, nc.sync)
 
         def listed(first, count):
             return offsets[:, first // LANES : (first + count) // LANES]
@@ -144,9 +143,11 @@ def tile_list_modp_gelu_noneP_kernel(
         for half in range(2):
             gather_words(half * HALF, HALF, v_w[0][:, half * HALF : (half + 1) * HALF])
         w_s = tile([P, R], U8, "w_s")
-        nc.gpsimd.tensor_copy(
-            w_s[:].rearrange("p (t m) -> p t m", t=PACK), w_s_raw[:].rearrange("p (m t) -> p t m", t=PACK)
-        )
+        for u in range(2):
+            nc.gpsimd.tensor_copy(
+                w_s[:].rearrange("p (t m) -> p t m", t=PACK)[:, 2 * u : 2 * u + 2, :],
+                w_s_raw[:].rearrange("p (m t) -> p t m", t=PACK)[:, 2 * u : 2 * u + 2, :],
+            )
 
         def up_sums(out, c, t, first, count):
             nc.tensor.matmul_mx(
@@ -172,7 +173,7 @@ def tile_list_modp_gelu_noneP_kernel(
             for u in range(2):
                 acc = ps.tile([P, 2, CHUNK], F32, name="a%d_%d" % (c, u), tag="ab"[c % 2] + str(u))
                 for e in range(2):
-                    up_sums(acc[:, e, :], c, 2 * u + e, 0, CHUNK)
+                    up_sums(acc[:, e, :], c, u + 2 * (1 - e), 0, CHUNK)
                 sums.append(acc)
             return sums
 
@@ -180,11 +181,11 @@ def tile_list_modp_gelu_noneP_kernel(
             rows = tile([P, PACK, CHUNK], BF16, "rows%d" % c)
             acts = []
             for u, acc in enumerate(sums):
-                act = tile([P, 2, CHUNK], F32, "act%d_%d" % (c, u), "act0_0" if (c, u) == (1, 0) else None)
+                act = tile([P, 2, CHUNK], F32, "act%d_%d" % (c, u))
                 nc.scalar.activation(act[:], acc[:], GELU)
                 acts.append(act)
             for t in range(PACK):
-                nc.scalar.activation(rows[:, t, :], acts[t // 2][:, t % 2, :], COPY, scale=sm_t[:, t : t + 1])
+                nc.scalar.activation(rows[:, t, :], acts[t % 2][:, 1 - t // 2, :], COPY, scale=sm_t[:, t : t + 1])
             return rows
 
         def group_and_quantize_h(c, rows):
@@ -223,7 +224,7 @@ def tile_list_modp_gelu_noneP_kernel(
 
         def up_half(c, half):
             acc = ps.tile([P, PACK, HALF], F32, name="a%d_%d" % (c, half), tag="ab"[c % 2] + str(half))
-            for t in range(PACK):
+            for t in reversed(range(PACK)):
                 up_sums(acc[:, t, :], c, t, half * HALF, HALF)
             return acc
 

@@ -1,7 +1,6 @@
 from contextlib import ExitStack
 
 import concourse.mybir as mybir
-from concourse.masks import make_identity
 
 K, R, N, T, J = 512, 512, 512, 2048, 1024
 FLOPS = 2 * K * R * J + 2 * R * N * J
@@ -16,6 +15,8 @@ FP8X4 = mybir.dt.float8_e4m3fn_x4
 FP4X4 = mybir.dt.float4_e2m1fn_x4
 GELU = mybir.ActivationFunctionType.Gelu_apprx_tanh
 COPY = mybir.ActivationFunctionType.Copy
+ABS = mybir.ActivationFunctionType.Abs
+RELU = mybir.ActivationFunctionType.Relu
 MULT = mybir.AluOpType.mult
 ADD = mybir.AluOpType.add
 
@@ -40,21 +41,23 @@ AT_TABLE = 0
 AT_SM = AT_TABLE + 4 * T
 AT_ZEROS = AT_SM - ALIGN
 AT_WD = AT_ZEROS + 4 * ZEROS - ALIGN
-AT_WD_SCALES = AT_WD + 4 * N
+ACT_BYTES = 2 * 4 * CHUNK
+ROWS_BYTES = 2 * PACK * CHUNK
+AT_ROWS = AT_WD + 4 * N - ALIGN
+AT_LATER_ROWS = AT_ROWS + ROWS_BYTES + 2 * (ACT_BYTES - ALIGN)
+AT_WD_SCALES = AT_LATER_ROWS + ROWS_BYTES + ACT_BYTES - ALIGN
 AT_PAGE_2 = AT_WD_SCALES + N - ALIGN
 AT_SCALES = AT_PAGE_2 + 4 * T
 AT_PAGE_3 = AT_SCALES + R
 AT_SECOND_H = AT_PAGE_3 + 4 * T - ALIGN
 AT_FIRST_H = AT_SECOND_H + 2 * PACK * CHUNK
 AT_LATER_S = AT_FIRST_H
-AT_LAST_SCALES = AT_LATER_S + (PACK - 1) * P
 AT_LAST_WORDS = AT_FIRST_H + 2 * PACK * HALF - ALIGN
 AT_PAIRS_0 = AT_LAST_WORDS + 4 * CHUNK
 AT_TURNED = AT_PAIRS_0 + 2 * PACK * SHARE - ALIGN
 AT_PAIRS_1 = AT_TURNED + 4 * CHUNK - ALIGN
-AT_IDENTITY = AT_PAIRS_1 + 2 * PACK * SIDE
-AT_WU = AT_IDENTITY + 4 * P - ALIGN
-AT_WGO = AT_WU + 2 * R - ALIGN
+AT_MORE_ZEROS = AT_PAIRS_1 + 2 * PACK * SIDE
+AT_WGO = AT_MORE_ZEROS + 4 * ZEROS - ALIGN
 
 
 def tile_list_modp_gelu_noneP_kernel(
@@ -93,9 +96,16 @@ def tile_list_modp_gelu_noneP_kernel(
         )
         load_quadrant(w_s_raw[:], wu_scales, QUADS - 1, nc.scalar)
         wd_s_raw = placed([P, N], U8, "wd_s_raw", AT_WD_SCALES)
-        nc.vector.memset(wd_s_raw[:].bitcast(I32), 0)
+        more_zeros = placed([P, ZEROS], I32, "more_zeros", AT_MORE_ZEROS)
+        nc.vector.memset(more_zeros[:], 0)
+        nc.vector.tensor_copy(
+            wd_s_raw[:].bitcast(I32).rearrange("p (a z) -> p a z", z=ZEROS),
+            more_zeros[:].unsqueeze(1).to_broadcast([P, N // 4 // ZEROS, ZEROS]),
+        )
+        apart = tile([P, P], F32, "apart")
+        nc.gpsimd.iota(apart[:], [[1, P]], base=0, channel_multiplier=-1, allow_small_or_imprecise_dtypes=True)
 
-        wu_raw = placed([P, 2 * R], U8, "wu_raw", AT_WU)
+        wu_raw = tile([P, 2 * R], U8, "wu_raw")
         nc.sync.dma_start(out=wu_raw[:].bitcast(I32), in_=wu_words[0].bitcast(I32))
         for q in range(QUADS):
             load_scale_rows(tab_s[:], tab_scales, q, nc.scalar if q >= QUADS // 2 else nc.sync)
@@ -113,12 +123,10 @@ def tile_list_modp_gelu_noneP_kernel(
             pages.append(page)
 
         wu_w = tile([P, 2 * R], U8, "wu_w")
-        nc.vector.tensor_copy(
+        nc.scalar.copy(
             wu_w[:].bitcast(U16).rearrange("p (t m) -> p t m", t=PACK),
             wu_raw[:].bitcast(U16).rearrange("p (m t) -> p t m", t=PACK),
         )
-        identity = placed([P, P], F32, "identity", AT_IDENTITY)
-        make_identity(nc, identity[:])
         wd_raw = placed([P, N], I32, "wd_raw", AT_WD)
         nc.sync.dma_start(out=wd_raw[:], in_=wd_words[0].rearrange("p n i -> p (n i)").bitcast(I32))
         sm_t = placed([P, PACK], F32, "sm_t", AT_SM)
@@ -137,8 +145,8 @@ def tile_list_modp_gelu_noneP_kernel(
             nc.vector.tensor_copy(scales[:], tab_s[:].indirect(listed(first, count)))
             return scales
 
-        early_s = gather_scales(0, J - CHUNK, tile([P, J - CHUNK], U8, "early_s"))
-        v_s = {c: early_s[:, c * CHUNK : (c + 1) * CHUNK] for c in range(CHUNKS - 1)}
+        all_s = gather_scales(0, J, tile([P, J], U8, "all_s"))
+        v_s = {c: all_s[:, c * CHUNK : (c + 1) * CHUNK] for c in range(CHUNKS)}
         v_w = {0: tile([P, CHUNK], U32, "v_w0")[:]}
         for half in range(2):
             gather_words(half * HALF, HALF, v_w[0][:, half * HALF : (half + 1) * HALF])
@@ -177,11 +185,18 @@ def tile_list_modp_gelu_noneP_kernel(
                 sums.append(acc)
             return sums
 
+        at_rows = {1: AT_ROWS, 2: AT_LATER_ROWS}
+
+        def at_act(c, u):
+            return at_rows[c - 1] + (ALIGN - ACT_BYTES if u else ROWS_BYTES - ALIGN)
+
         def hidden_rows(c, sums):
-            rows = tile([P, PACK, CHUNK], BF16, "rows%d" % c)
+            shape = [P, PACK, CHUNK]
+            rows = placed(shape, BF16, "rows%d" % c, at_rows[c]) if c in at_rows else tile(shape, BF16, "rows%d" % c)
             acts = []
             for u, acc in enumerate(sums):
-                act = tile([P, 2, CHUNK], F32, "act%d_%d" % (c, u))
+                name = "act%d_%d" % (c, u)
+                act = placed([P, 2, CHUNK], F32, name, at_act(c, u)) if c > 1 else tile([P, 2, CHUNK], F32, name)
                 nc.scalar.activation(act[:], acc[:], GELU)
                 acts.append(act)
             for t in range(PACK):
@@ -253,26 +268,27 @@ def tile_list_modp_gelu_noneP_kernel(
         raw_s = wd_s_raw[:].rearrange("p (m t) -> p t m", t=PACK)
         quantize_h(first_h[0][:].rearrange("p n u e -> p (n u e)"), 0, HALF)
         nc.vector.tensor_copy(wd_s[:], raw_s[:, :2, :])
-        quantize_h(first_h[1][:].rearrange("p n u e -> p (n u e)"), HALF, HALF)
+        for first in range(0, HALF, STEP):
+            quantize_h(first_h[1][:, first : first + STEP].rearrange("p n u e -> p (n u e)"), HALF + first, STEP)
         later_s = placed([P, 2, P], U8, "later_s", AT_LATER_S)
         nc.gpsimd.tensor_copy(later_s[:], raw_s[:, 2:, :])
         cleared_page(placed([P, T], F32, "page2", AT_PAGE_2))
         last = CHUNKS - 1
         v_w[last] = gather_words(last * CHUNK, CHUNK, placed([P, CHUNK], U32, "v_w_last", AT_LAST_WORDS)[:])
-        v_s[last] = gather_scales(last * CHUNK, CHUNK, placed([P, CHUNK], U8, "last_s", AT_LAST_SCALES))[:]
         wgo_by_token = tile([P, J // P], F32, "wgo_by_token", "act0_%d" % HALF)
         with nc.allow_non_contiguous_dma(reason="one weight a partition"):
             nc.sync.dma_start(out=wgo_by_token[:], in_=wgo[0].rearrange("(b p) -> p b", p=P))
         sums = up_chunk(1)
 
         def place(t, first, count, bank, after=None):
-            y = tile([P, count], F32, "y%d_%d" % (t, first), after)
+            name = "y%d_%d" % (t, first)
+            y = placed([P, count], F32, name, after) if isinstance(after, int) else tile([P, count], F32, name, after)
             down(y[:], t, first, count, bank)
             scatter(pages[t], y[:], first, count)
 
         first_y = tile([P, CHUNK], F32, "y0_0")
-        for half, bank in enumerate(("a0", "a1")):
-            down(first_y[:, half * HALF : (half + 1) * HALF], 0, half * HALF, HALF, bank)
+        for first, end, bank in ((0, HALF, "a0"), (HALF, HALF + STEP, "n0"), (HALF + STEP, CHUNK, "a1")):
+            down(first_y[:, first:end], 0, first, end - first, bank)
         scatter(pages[0], first_y[:], 0, CHUNK)
 
         rows = hidden_rows(1, sums)
@@ -280,18 +296,23 @@ def tile_list_modp_gelu_noneP_kernel(
         group_and_quantize_h(1, rows)
         cleared_page(placed([P, T], F32, "page3", AT_PAGE_3))
         sums = up_chunk(2)
-        place(2, 0, CHUNK, "y2", "rows1")
+        place(2, 0, CHUNK, "y2", at_rows[1] + ALIGN)
         for c in range(1, CHUNKS):
             if c + 1 < CHUNKS:
                 rows = hidden_rows(c + 1, sums)
-            place(0, c * CHUNK, CHUNK, "y0", "act%d_1" % (c + 1))
+            place(0, c * CHUNK, CHUNK, "y0", at_act(c + 1, 1) if c < last else None)
             place(1, c * CHUNK, CHUNK, "y0")
             if c + 1 < CHUNKS:
                 group_and_quantize_h(c + 1, rows)
             if c + 2 < CHUNKS:
                 sums = up_chunk(c + 2)
             if c < last:
-                place(2, c * CHUNK, CHUNK, "y2", "rows%d" % (c + 1))
+                place(2, c * CHUNK, CHUNK, "y2", at_rows[2] + ALIGN if c == 1 else "rows3")
+
+        distance = placed([P, P], F32, "distance", at_act(2, 0) + ALIGN)
+        nc.scalar.activation(distance[:], apart[:], ABS)
+        identity = tile([P, P], F32, "identity")
+        nc.scalar.activation(identity[:], distance[:], RELU, bias=1.0, scale=-1.0)
 
         def turned_back(first, count, t, turned, banks, outs):
             blocks, wide = count // P, PACK - t

@@ -41,17 +41,17 @@ AT_TABLE = 0
 AT_SM = AT_TABLE + 4 * T
 AT_ZEROS = AT_SM - ALIGN
 AT_WD = AT_ZEROS + 4 * ZEROS - ALIGN
-ACT_BYTES = 2 * 4 * CHUNK
-ROWS_BYTES = 2 * PACK * CHUNK
+ACT_BYTES = 4 * PACK * CHUNK
 AT_ROWS = AT_WD + 4 * N - ALIGN
-AT_LATER_ROWS = AT_ROWS + ROWS_BYTES + 2 * (ACT_BYTES - ALIGN)
-AT_WD_SCALES = AT_LATER_ROWS + ROWS_BYTES + ACT_BYTES - ALIGN
+AT_LATER_ROWS = AT_ROWS + 2 * PACK * HALF + ACT_BYTES
+AT_ACT = {2: AT_ROWS + 2 * PACK * HALF - ALIGN, 3: AT_LATER_ROWS + 2 * PACK * CHUNK - ALIGN}
+AT_WD_SCALES = AT_ACT[3] + ACT_BYTES
 AT_PAGE_2 = AT_WD_SCALES + N - ALIGN
 AT_SCALES = AT_PAGE_2 + 4 * T
 AT_PAGE_3 = AT_SCALES + R
 AT_SECOND_H = AT_PAGE_3 + 4 * T - ALIGN
-AT_FIRST_H = AT_SECOND_H + 2 * PACK * CHUNK
-AT_LATER_S = AT_FIRST_H
+AT_FIRST_H = AT_SECOND_H + 2 * PACK * CHUNK - ALIGN
+AT_LATER_S = AT_FIRST_H + ALIGN
 AT_LAST_WORDS = AT_FIRST_H + 2 * PACK * HALF - ALIGN
 AT_PAIRS_0 = AT_LAST_WORDS + 4 * CHUNK
 AT_TURNED = AT_PAIRS_0 + 2 * PACK * SHARE - ALIGN
@@ -185,31 +185,28 @@ def tile_list_modp_gelu_noneP_kernel(
                 sums.append(acc)
             return sums
 
-        at_rows = {1: AT_ROWS, 2: AT_LATER_ROWS}
-
-        def at_act(c, u):
-            return at_rows[c - 1] + (ALIGN - ACT_BYTES if u else ROWS_BYTES - ALIGN)
+        def scaled_rows(rows, act_of):
+            for t in range(PACK):
+                nc.scalar.activation(rows[:, t, :], act_of(t), COPY, scale=sm_t[:, t : t + 1])
 
         def hidden_rows(c, sums):
             shape = [P, PACK, CHUNK]
-            rows = placed(shape, BF16, "rows%d" % c, at_rows[c]) if c in at_rows else tile(shape, BF16, "rows%d" % c)
-            acts = []
+            rows = placed(shape, BF16, "rows2", AT_LATER_ROWS) if c == 2 else tile(shape, BF16, "rows%d" % c)
+            act = placed([P, 2, 2, CHUNK], F32, "act%d" % c, AT_ACT[c])
             for u, acc in enumerate(sums):
-                name = "act%d_%d" % (c, u)
-                act = placed([P, 2, CHUNK], F32, name, at_act(c, u)) if c > 1 else tile([P, 2, CHUNK], F32, name)
-                nc.scalar.activation(act[:], acc[:], GELU)
-                acts.append(act)
-            for t in range(PACK):
-                nc.scalar.activation(rows[:, t, :], acts[t % 2][:, 1 - t // 2, :], COPY, scale=sm_t[:, t : t + 1])
+                nc.scalar.activation(act[:, u], acc[:], GELU)
+            scaled_rows(rows, lambda t: act[:, t % 2, 1 - t // 2, :])
             return rows
 
-        def group_and_quantize_h(c, rows):
-            shape = [P, CHUNK * PACK]
-            grouped = placed(shape, BF16, "h1", AT_SECOND_H) if c == 1 else tile(shape, BF16, "h%d" % c)
+        def group(grouped, rows):
             nc.scalar.copy(
-                grouped[:].rearrange("p (n i t) -> p n t i", t=PACK, i=RUN),
+                grouped.rearrange("p (n i t) -> p n t i", t=PACK, i=RUN),
                 rows[:].rearrange("p t (n i) -> p n t i", i=RUN),
             )
+
+        def group_and_quantize_h(c, rows):
+            grouped = tile([P, CHUNK * PACK], BF16, "h%d" % c)
+            group(grouped[:], rows)
             quantize_h(grouped[:], c * CHUNK, CHUNK)
 
         def down(y, t, first, count, bank):
@@ -245,7 +242,7 @@ def tile_list_modp_gelu_noneP_kernel(
 
         def times_sm(grouped, act):
             by_pair = sm_t[:].rearrange("p (u e) -> p u e", e=2)
-            nc.vector.tensor_tensor(grouped, act, by_pair.unsqueeze(1).to_broadcast([P, STEP, 2, 2]), MULT)
+            nc.vector.tensor_tensor(grouped, act, by_pair.unsqueeze(1).to_broadcast(list(act.shape)), MULT)
 
         first_h = [tile([P, HALF, 2, 2], BF16, "h0_0"), placed([P, HALF, 2, 2], BF16, "h0_1", AT_FIRST_H)]
         act = tile([P, 2, HALF, 2], F32, "act0_0")
@@ -278,7 +275,15 @@ def tile_list_modp_gelu_noneP_kernel(
         wgo_by_token = tile([P, J // P], F32, "wgo_by_token", "act0_%d" % HALF)
         with nc.allow_non_contiguous_dma(reason="one weight a partition"):
             nc.sync.dma_start(out=wgo_by_token[:], in_=wgo[0].rearrange("(b p) -> p b", p=P))
-        sums = up_chunk(1)
+        second_h = placed([P, CHUNK * PACK], BF16, "h1", AT_SECOND_H)
+        act = tile([P, HALF, PACK], F32, "act1_0")
+        nc.scalar.activation(act[:], up_half(1, 0)[:].rearrange("p t n -> p n t"), GELU)
+        times_sm(
+            second_h[:, : HALF * PACK].rearrange("p (n u e) -> p n u e", u=2, e=2),
+            act[:].rearrange("p n (u e) -> p n u e", e=2),
+        )
+        act = tile([P, PACK, HALF], F32, "act1_1")
+        nc.scalar.activation(act[:], up_half(1, 1)[:], GELU)
 
         def place(t, first, count, bank, after=None):
             name = "y%d_%d" % (t, first)
@@ -291,25 +296,27 @@ def tile_list_modp_gelu_noneP_kernel(
             down(first_y[:, first:end], 0, first, end - first, bank)
         scatter(pages[0], first_y[:], 0, CHUNK)
 
-        rows = hidden_rows(1, sums)
+        rows = placed([P, PACK, HALF], BF16, "rows1", AT_ROWS)
+        scaled_rows(rows, lambda t: act[:, t, :])
         place(1, 0, CHUNK, "y0")
-        group_and_quantize_h(1, rows)
+        group(second_h[:, HALF * PACK :], rows)
+        quantize_h(second_h[:], CHUNK, CHUNK)
         cleared_page(placed([P, T], F32, "page3", AT_PAGE_3))
         sums = up_chunk(2)
-        place(2, 0, CHUNK, "y2", at_rows[1] + ALIGN)
+        place(2, 0, CHUNK, "y2", AT_ROWS + ALIGN - 4 * CHUNK)
         for c in range(1, CHUNKS):
             if c + 1 < CHUNKS:
                 rows = hidden_rows(c + 1, sums)
-            place(0, c * CHUNK, CHUNK, "y0", at_act(c + 1, 1) if c < last else None)
+            place(0, c * CHUNK, CHUNK, "y0", AT_ACT[c + 1] + ALIGN if c < last else None)
             place(1, c * CHUNK, CHUNK, "y0")
             if c + 1 < CHUNKS:
                 group_and_quantize_h(c + 1, rows)
             if c + 2 < CHUNKS:
                 sums = up_chunk(c + 2)
             if c < last:
-                place(2, c * CHUNK, CHUNK, "y2", at_rows[2] + ALIGN if c == 1 else "rows3")
+                place(2, c * CHUNK, CHUNK, "y2", AT_LATER_ROWS + ALIGN if c == 1 else "rows3")
 
-        distance = placed([P, P], F32, "distance", at_act(2, 0) + ALIGN)
+        distance = placed([P, P], F32, "distance", AT_ACT[2] + 2 * 4 * CHUNK)
         nc.scalar.activation(distance[:], apart[:], ABS)
         identity = tile([P, P], F32, "identity")
         nc.scalar.activation(identity[:], distance[:], RELU, bias=1.0, scale=-1.0)

@@ -46,14 +46,13 @@ AT_ROWS = AT_WD + 4 * N - ALIGN
 AT_LATER_ROWS = AT_ROWS + 2 * PACK * HALF + ACT_BYTES
 AT_ACT = {2: AT_ROWS + 2 * PACK * HALF - ALIGN, 3: AT_LATER_ROWS + 2 * PACK * CHUNK - ALIGN}
 AT_WD_SCALES = AT_ACT[3] + ACT_BYTES
-AT_PAGE_2 = AT_WD_SCALES + N - ALIGN
-AT_SCALES = AT_PAGE_2 + 4 * T
+AT_SCALES = AT_WD_SCALES + N
 AT_PAGE_3 = AT_SCALES + R
 AT_SECOND_H = AT_PAGE_3 + 4 * T - ALIGN
 AT_FIRST_H = AT_SECOND_H + 2 * PACK * CHUNK - ALIGN
-AT_LATER_S = AT_FIRST_H + ALIGN
-AT_LAST_WORDS = AT_FIRST_H + 2 * PACK * HALF - ALIGN
-AT_PAIRS_0 = AT_LAST_WORDS + 4 * CHUNK
+AT_LAST_WORDS = AT_FIRST_H + ALIGN
+AT_PAGE_2 = AT_FIRST_H + 2 * PACK * CHUNK - ALIGN
+AT_PAIRS_0 = AT_PAGE_2 + 4 * T
 AT_TURNED = AT_PAIRS_0 + 2 * PACK * SHARE - ALIGN
 AT_PAIRS_1 = AT_TURNED + 4 * CHUNK - ALIGN
 AT_MORE_ZEROS = AT_PAIRS_1 + 2 * PACK * SIDE
@@ -214,7 +213,7 @@ def tile_list_modp_gelu_noneP_kernel(
             nc.tensor.matmul_mx(
                 out=acc[:],
                 lhsT=wd_w[:, P * t : P * (t + 1)].bitcast(FP8X4),
-                lhsT_scale=(wd_s, later_s)[t // 2][:, t % 2, :],
+                lhsT_scale=wd_s[:, t, :],
                 rhs=h_w[:, first : first + count].bitcast(FP8X4),
                 rhs_scale=h_s[:, first : first + count],
                 start=True,
@@ -244,7 +243,8 @@ def tile_list_modp_gelu_noneP_kernel(
             by_pair = sm_t[:].rearrange("p (u e) -> p u e", e=2)
             nc.vector.tensor_tensor(grouped, act, by_pair.unsqueeze(1).to_broadcast(list(act.shape)), MULT)
 
-        first_h = [tile([P, HALF, 2, 2], BF16, "h0_0"), placed([P, HALF, 2, 2], BF16, "h0_1", AT_FIRST_H)]
+        whole_h = placed([P, 2, HALF, 2, 2], BF16, "h0", AT_FIRST_H)
+        first_h = [whole_h[:, half] for half in range(2)]
         act = tile([P, 2, HALF, 2], F32, "act0_0")
         for u, bank in enumerate(("a0", "n0")):
             acc = ps.tile([P, 2, HALF], F32, name="first_sums%d" % u, tag=bank)
@@ -261,18 +261,16 @@ def tile_list_modp_gelu_noneP_kernel(
             act = tile([P, STEP, PACK], F32, "act0_%d" % (HALF + first))
             nc.scalar.activation(act[:], acc[:, :, first : first + STEP].rearrange("p t n -> p n t"), GELU)
             times_sm(first_h[1][:, first : first + STEP], act[:].rearrange("p n (u e) -> p n u e", e=2))
-        wd_s = tile([P, 2, P], U8, "wd_s")
+        wd_s = tile([P, PACK, P], U8, "wd_s")
         raw_s = wd_s_raw[:].rearrange("p (m t) -> p t m", t=PACK)
-        quantize_h(first_h[0][:].rearrange("p n u e -> p (n u e)"), 0, HALF)
-        nc.vector.tensor_copy(wd_s[:], raw_s[:, :2, :])
-        for first in range(0, HALF, STEP):
-            quantize_h(first_h[1][:, first : first + STEP].rearrange("p n u e -> p (n u e)"), HALF + first, STEP)
-        later_s = placed([P, 2, P], U8, "later_s", AT_LATER_S)
-        nc.gpsimd.tensor_copy(later_s[:], raw_s[:, 2:, :])
+        quantize_h(first_h[0].rearrange("p n u e -> p (n u e)"), 0, HALF)
+        nc.vector.tensor_copy(wd_s[:], raw_s)
+        quantize_h(first_h[1][:, :STEP].rearrange("p n u e -> p (n u e)"), HALF, STEP)
+        quantize_h(first_h[1][:, STEP:].rearrange("p n u e -> p (n u e)"), HALF + STEP, STEP)
         cleared_page(placed([P, T], F32, "page2", AT_PAGE_2))
         last = CHUNKS - 1
         v_w[last] = gather_words(last * CHUNK, CHUNK, placed([P, CHUNK], U32, "v_w_last", AT_LAST_WORDS)[:])
-        wgo_by_token = tile([P, J // P], F32, "wgo_by_token", "act0_%d" % HALF)
+        wgo_by_token = tile([P, J // P], F32, "wgo_by_token", "act0_%d" % (HALF + STEP))
         with nc.allow_non_contiguous_dma(reason="one weight a partition"):
             nc.sync.dma_start(out=wgo_by_token[:], in_=wgo[0].rearrange("(b p) -> p b", p=P))
         second_h = placed([P, CHUNK * PACK], BF16, "h1", AT_SECOND_H)
@@ -331,7 +329,7 @@ def tile_list_modp_gelu_noneP_kernel(
                     lhsT=h_w[:, at : at + P].bitcast(FP8X4),
                     lhsT_scale=h_s[:, at : at + P],
                     rhs=wd_w[:, P * t :].bitcast(FP8X4),
-                    rhs_scale=later_s[:, t - 2 :, :].rearrange("p t m -> p (t m)"),
+                    rhs_scale=wd_s[:, t:, :].rearrange("p t m -> p (t m)"),
                     start=True,
                     stop=True,
                 )

@@ -43,8 +43,8 @@ AT_ZEROS = AT_SM - ALIGN
 AT_WD = AT_ZEROS + 4 * ZEROS - ALIGN
 ACT_BYTES = 4 * PACK * CHUNK
 AT_ROWS = AT_WD + 4 * N - ALIGN
-AT_LATER_ROWS = AT_ROWS + 2 * PACK * HALF + ACT_BYTES
-AT_ACT = {2: AT_ROWS + 2 * PACK * HALF - ALIGN, 3: AT_LATER_ROWS + 2 * PACK * CHUNK - ALIGN}
+AT_LATER_ROWS = AT_ROWS + 2 * PACK * (CHUNK - STEP) + ACT_BYTES
+AT_ACT = {2: AT_ROWS + 2 * PACK * (CHUNK - STEP) - ALIGN, 3: AT_LATER_ROWS + 2 * PACK * CHUNK - ALIGN}
 AT_WD_SCALES = AT_ACT[3] + ACT_BYTES
 AT_SCALES = AT_WD_SCALES + N
 AT_PAGE_3 = AT_SCALES + R
@@ -55,7 +55,8 @@ AT_PAGE_2 = AT_FIRST_H + 2 * PACK * CHUNK - ALIGN
 AT_PAIRS_0 = AT_PAGE_2 + 4 * T
 AT_TURNED = AT_PAIRS_0 + 2 * PACK * SHARE - ALIGN
 AT_PAIRS_1 = AT_TURNED + 4 * CHUNK - ALIGN
-AT_MORE_ZEROS = AT_PAIRS_1 + 2 * PACK * SIDE
+AT_APART = AT_PAIRS_1 + 2 * PACK * SIDE
+AT_MORE_ZEROS = AT_APART + 4 * P - ALIGN
 AT_WGO = AT_MORE_ZEROS + 4 * ZEROS - ALIGN
 
 
@@ -101,9 +102,9 @@ def tile_list_modp_gelu_noneP_kernel(
             wd_s_raw[:].bitcast(I32).rearrange("p (a z) -> p a z", z=ZEROS),
             more_zeros[:].unsqueeze(1).to_broadcast([P, N // 4 // ZEROS, ZEROS]),
         )
-        apart = tile([P, P], F32, "apart")
-        nc.gpsimd.iota(apart[:], [[1, P]], base=0, channel_multiplier=-1, allow_small_or_imprecise_dtypes=True)
 
+        apart = placed([P, P], F32, "apart", AT_APART)
+        nc.gpsimd.iota(apart[:], [[1, P]], base=0, channel_multiplier=-1, allow_small_or_imprecise_dtypes=True)
         wu_raw = tile([P, 2 * R], U8, "wu_raw")
         nc.sync.dma_start(out=wu_raw[:].bitcast(I32), in_=wu_words[0].bitcast(I32))
         for q in range(QUADS):
@@ -274,14 +275,16 @@ def tile_list_modp_gelu_noneP_kernel(
         with nc.allow_non_contiguous_dma(reason="one weight a partition"):
             nc.sync.dma_start(out=wgo_by_token[:], in_=wgo[0].rearrange("(b p) -> p b", p=P))
         second_h = placed([P, CHUNK * PACK], BF16, "h1", AT_SECOND_H)
-        act = tile([P, HALF, PACK], F32, "act1_0")
-        nc.scalar.activation(act[:], up_half(1, 0)[:].rearrange("p t n -> p n t"), GELU)
+        act = tile([P, STEP, PACK], F32, "act1_0")
+        acc = up_half(1, 0)
+        nc.scalar.activation(act[:], acc[:, :, :STEP].rearrange("p t n -> p n t"), GELU)
         times_sm(
-            second_h[:, : HALF * PACK].rearrange("p (n u e) -> p n u e", u=2, e=2),
+            second_h[:, : STEP * PACK].rearrange("p (n u e) -> p n u e", u=2, e=2),
             act[:].rearrange("p n (u e) -> p n u e", e=2),
         )
-        act = tile([P, PACK, HALF], F32, "act1_1")
-        nc.scalar.activation(act[:], up_half(1, 1)[:], GELU)
+        act = tile([P, PACK, CHUNK - STEP], F32, "act1_1")
+        nc.scalar.activation(act[:, :, :STEP], acc[:, :, STEP:], GELU)
+        nc.scalar.activation(act[:, :, STEP:], up_half(1, 1)[:], GELU)
 
         def place(t, first, count, bank, after=None):
             name = "y%d_%d" % (t, first)
@@ -294,10 +297,10 @@ def tile_list_modp_gelu_noneP_kernel(
             down(first_y[:, first:end], 0, first, end - first, bank)
         scatter(pages[0], first_y[:], 0, CHUNK)
 
-        rows = placed([P, PACK, HALF], BF16, "rows1", AT_ROWS)
+        rows = placed([P, PACK, CHUNK - STEP], BF16, "rows1", AT_ROWS)
         scaled_rows(rows, lambda t: act[:, t, :])
         place(1, 0, CHUNK, "y0")
-        group(second_h[:, HALF * PACK :], rows)
+        group(second_h[:, STEP * PACK :], rows)
         quantize_h(second_h[:], CHUNK, CHUNK)
         cleared_page(placed([P, T], F32, "page3", AT_PAGE_3))
         sums = up_chunk(2)

from contextlib import ExitStack

import concourse.mybir as mybir

K, R, N, T, J = 512, 512, 512, 2048, 1024
FLOPS = 2 * K * R * J + 2 * R * N * J

F32 = mybir.dt.float32
BF16 = mybir.dt.bfloat16
I32 = mybir.dt.int32
U32 = mybir.dt.uint32
U16 = mybir.dt.uint16
U8 = mybir.dt.uint8
FP8X4 = mybir.dt.float8_e4m3fn_x4
FP4X4 = mybir.dt.float4_e2m1fn_x4
GELU = mybir.ActivationFunctionType.Gelu_apprx_tanh
COPY = mybir.ActivationFunctionType.Copy
ABS = mybir.ActivationFunctionType.Abs
RELU = mybir.ActivationFunctionType.Relu
MULT = mybir.AluOpType.mult
ADD = mybir.AluOpType.add

P = 128
PACK = 4
QUADS = 4
LANES = 16
CHUNK = 256
CHUNKS = J // CHUNK
HALF = CHUNK // 2
STEP = HALF // 2
BANK = 512
SIDE = T // 2
QUARTER = T // 4
BLOCK = 32
SHARE = 960
RUN = 4
ALIGN = 64
LOWER = 96
ZEROS = 64
AT_TABLE = 0
AT_SM = AT_TABLE + 4 * T
AT_ZEROS = AT_SM - ALIGN
AT_WD = AT_ZEROS + 4 * ZEROS - ALIGN
ACT_BYTES = 4 * PACK * CHUNK
AT_ROWS = AT_WD + 4 * N - ALIGN
AT_LATER_ROWS = AT_ROWS + 2 * PACK * (CHUNK - STEP) + ACT_BYTES
AT_ACT = {2: AT_ROWS + 2 * PACK * (CHUNK - STEP) - ALIGN, 3: AT_LATER_ROWS + 2 * PACK * CHUNK - ALIGN}
AT_WD_SCALES = AT_ACT[3] + ACT_BYTES
AT_SCALES = AT_WD_SCALES + N
AT_PAGE_3 = AT_SCALES + R
AT_SECOND_H = AT_PAGE_3 + 4 * T - ALIGN
AT_FIRST_H = AT_SECOND_H + 2 * PACK * CHUNK - ALIGN
AT_LAST_WORDS = AT_FIRST_H + ALIGN
AT_PAGE_2 = AT_FIRST_H + 2 * PACK * CHUNK - ALIGN
AT_PAIRS_0 = AT_PAGE_2 + 4 * T
AT_TURNED = AT_PAIRS_0 + 2 * PACK * SHARE - ALIGN
AT_PAIRS_1 = AT_TURNED + 4 * CHUNK - ALIGN
AT_APART = AT_PAIRS_1 + 2 * PACK * SIDE
AT_MORE_ZEROS = AT_APART + 4 * P - ALIGN
AT_WGO = AT_MORE_ZEROS + 4 * ZEROS - ALIGN


def tile_list_modp_gelu_noneP_kernel(
    tc, tab_words, tab_scales, wu_words, wu_scales, sm, wd_words, wd_scales, wgo, offs, out_0, out_1, out_2
):
    nc = tc.nc
    with ExitStack() as ctx:
        sb = ctx.enter_context(tc.tile_pool(name="sb", bufs=1))
        ps = ctx.enter_context(tc.psum_pool(name="ps", bufs=1))
        by_hand = ctx.enter_context(tc.tile_pool(name="by_hand", bufs=1))

        def placed(shape, dtype, name, offset):
            return by_hand.tile(shape, dtype, name=name, tag=name, align_bytes=ALIGN, offset=offset)

        def tile(shape, dtype, name, after=None):
            return sb.tile(shape, dtype, name=name, tag=after or name, align_bytes=ALIGN)

        def load_scale_rows(plane, rows, r, queue):
            queue.dma_start(out=plane[r:P:32].bitcast(I32), in_=rows[0, r : 4 * QUADS : 4, :].bitcast(I32))

        def load_quadrant(plane, rows, q, queue):
            queue.dma_start(out=plane[32 * q : 32 * q + 4].bitcast(I32), in_=rows[0, 4 * q : 4 * q + 4, :].bitcast(I32))

        offsets = sb.tile([P, J // LANES], U16, name="offsets")
        nc.sync.dma_start(offsets[:], offs)

        zeros = placed([P, ZEROS], I32, "zeros", AT_ZEROS)
        nc.vector.memset(zeros[:], 0)
        tab_s = tile([P, T], U8, "tab_s")
        nc.vector.memset(tab_s[:].bitcast(I32), 0)
        w_s_raw = placed([P, R], U8, "w_s_raw", AT_SCALES)
        nc.gpsimd.memset(w_s_raw[LOWER:P].bitcast(I32), 0)
        nc.vector.tensor_copy(
            w_s_raw[:LOWER].bitcast(I32).rearrange("p (a z) -> p a z", z=ZEROS),
            zeros[:LOWER].unsqueeze(1).to_broadcast([LOWER, R // 4 // ZEROS, ZEROS]),
        )
        load_quadrant(w_s_raw[:], wu_scales, QUADS - 1, nc.scalar)
        wd_s_raw = placed([P, N], U8, "wd_s_raw", AT_WD_SCALES)
        more_zeros = placed([P, ZEROS], I32, "more_zeros", AT_MORE_ZEROS)
        nc.vector.memset(more_zeros[:], 0)
        nc.vector.tensor_copy(
            wd_s_raw[:].bitcast(I32).rearrange("p (a z) -> p a z", z=ZEROS),
            more_zeros[:].unsqueeze(1).to_broadcast([P, N // 4 // ZEROS, ZEROS]),
        )

        apart = placed([P, P], F32, "apart", AT_APART)
        nc.gpsimd.iota(apart[:], [[1, P]], base=0, channel_multiplier=-1, allow_small_or_imprecise_dtypes=True)
        wu_raw = tile([P, 2 * R], U8, "wu_raw")
        nc.sync.dma_start(out=wu_raw[:].bitcast(I32), in_=wu_words[0].bitcast(I32))
        for q in range(QUADS):
            load_scale_rows(tab_s[:], tab_scales, q, nc.scalar if q >= QUADS // 2 else nc.sync)
        tab_w = placed([P, T], I32, "tab_w", AT_TABLE)
        nc.scalar.dma_start(out=tab_w[:], in_=tab_words[0].rearrange("p t i -> p (t i)").bitcast(I32))
        for q in range(QUADS - 1):
            load_quadrant(w_s_raw[:], wu_scales, q, nc.sync)

        pages = [tile([P, T], F32, "page0"), tile([P, T], F32, "page1")]
        for page in pages:
            nc.vector.memset(page[:], 0.0)

        def cleared_page(page):
            nc.gpsimd.memset(page[:], 0.0)
            pages.append(page)

        wu_w = tile([P, 2 * R], U8, "wu_w")
        nc.scalar.copy(
            wu_w[:].bitcast(U16).rearrange("p (t m) -> p t m", t=PACK),
            wu_raw[:].bitcast(U16).rearrange("p (m t) -> p t m", t=PACK),
        )
        wd_raw = placed([P, N], I32, "wd_raw", AT_WD)
        nc.sync.dma_start(out=wd_raw[:], in_=wd_words[0].rearrange("p n i -> p (n i)").bitcast(I32))
        sm_t = placed([P, PACK], F32, "sm_t", AT_SM)
        nc.sync.dma_start(out=sm_t[:], in_=sm.rearrange("(p t) -> p t", t=PACK))
        for q in range(QUADS):
            load_scale_rows(wd_s_raw[:], wd_scales, q, nc.sync)

        def listed(first, count):
            return offsets[:, first // LANES : (first + count) // LANES]

        def gather_words(first, count, words):
            nc.vector.tensor_copy(words, tab_w[:].bitcast(U32).indirect(listed(first, count)))
            return words

        def gather_scales(first, count, scales):
            nc.vector.tensor_copy(scales[:], tab_s[:].indirect(listed(first, count)))
            return scales

        all_s = gather_scales(0, J, tile([P, J], U8, "all_s"))
        v_s = {c: all_s[:, c * CHUNK : (c + 1) * CHUNK] for c in range(CHUNKS)}
        v_w = {0: tile([P, CHUNK], U32, "v_w0")[:]}
        for half in range(2):
            gather_words(half * HALF, HALF, v_w[0][:, half * HALF : (half + 1) * HALF])
        w_s = tile([P, R], U8, "w_s")
        for u in range(2):
            nc.gpsimd.tensor_copy(
                w_s[:].rearrange("p (t m) -> p t m", t=PACK)[:, 2 * u : 2 * u + 2, :],
                w_s_raw[:].rearrange("p (m t) -> p t m", t=PACK)[:, 2 * u : 2 * u + 2, :],
            )

        def up_sums(out, c, t, first, count):
            nc.tensor.matmul_mx(
                out=out,
                lhsT=wu_w[:, 2 * P * t : 2 * P * (t + 1)].bitcast(FP4X4),
                lhsT_scale=w_s[:, P * t : P * (t + 1)],
                rhs=v_w[c][:, first : first + count].bitcast(FP8X4),
                rhs_scale=v_s[c][:, first : first + count],
                start=True,
                stop=True,
            )

        h_w = tile([P, J], U32, "h_w")
        h_s = tile([P, J], U8, "h_s")

        def quantize_h(grouped, first, count):
            nc.vector.quantize_mx(
                out=h_w[:, first : first + count].bitcast(FP8X4), scales=h_s[:, first : first + count], in_=grouped
            )

        def up_chunk(c):
            sums = []
            for u in range(2):
                acc = ps.tile([P, 2, CHUNK], F32, name="a%d_%d" % (c, u), tag="ab"[c % 2] + str(u))
                for e in range(2):
                    up_sums(acc[:, e, :], c, u + 2 * (1 - e), 0, CHUNK)
                sums.append(acc)
            return sums

        def scaled_rows(rows, act_of):
            for t in range(PACK):
                nc.scalar.activation(rows[:, t, :], act_of(t), COPY, scale=sm_t[:, t : t + 1])

        def hidden_rows(c, sums):
            shape = [P, PACK, CHUNK]
            rows = placed(shape, BF16, "rows2", AT_LATER_ROWS) if c == 2 else tile(shape, BF16, "rows%d" % c)
            act = placed([P, 2, 2, CHUNK], F32, "act%d" % c, AT_ACT[c])
            for u, acc in enumerate(sums):
                nc.scalar.activation(act[:, u], acc[:], GELU)
            scaled_rows(rows, lambda t: act[:, t % 2, 1 - t // 2, :])
            return rows

        def group(grouped, rows):
            nc.scalar.copy(
                grouped.rearrange("p (n i t) -> p n t i", t=PACK, i=RUN),
                rows[:].rearrange("p t (n i) -> p n t i", i=RUN),
            )

        def group_and_quantize_h(c, rows):
            grouped = tile([P, CHUNK * PACK], BF16, "h%d" % c)
            group(grouped[:], rows)
            quantize_h(grouped[:], c * CHUNK, CHUNK)

        def down(y, t, first, count, bank):
            acc = ps.tile([P, count], F32, name="y%d_%d" % (t, first), tag=bank)
            nc.tensor.matmul_mx(
                out=acc[:],
                lhsT=wd_w[:, P * t : P * (t + 1)].bitcast(FP8X4),
                lhsT_scale=wd_s[:, t, :],
                rhs=h_w[:, first : first + count].bitcast(FP8X4),
                rhs_scale=h_s[:, first : first + count],
                start=True,
                stop=True,
            )
            nc.scalar.copy(y, acc[:])

        def scatter(page, y, first, count):
            nc.vector.tensor_tensor(page[:].indirect(listed(first, count)), y, wgo_t[:, first : first + count], MULT)

        for c in range(1, CHUNKS - 1):
            v_w[c] = gather_words(c * CHUNK, CHUNK, tile([P, CHUNK], U32, "v_w%d" % c)[:])
        wgo_t = placed([P, J], F32, "wgo_t", AT_WGO)
        nc.sync.dma_start(out=wgo_t[:], in_=wgo)
        wd_w = tile([P, N], I32, "wd_w")
        nc.gpsimd.tensor_copy(
            wd_w[:].rearrange("p (t m) -> p t m", t=PACK), wd_raw[:].rearrange("p (m t) -> p t m", t=PACK)
        )

        def up_half(c, half):
            acc = ps.tile([P, PACK, HALF], F32, name="a%d_%d" % (c, half), tag="ab"[c % 2] + str(half))
            for t in reversed(range(PACK)):
                up_sums(acc[:, t, :], c, t, half * HALF, HALF)
            return acc

        def times_sm(grouped, act):
            by_pair = sm_t[:].rearrange("p (u e) -> p u e", e=2)
            nc.vector.tensor_tensor(grouped, act, by_pair.unsqueeze(1).to_broadcast(list(act.shape)), MULT)

        whole_h = placed([P, 2, HALF, 2, 2], BF16, "h0", AT_FIRST_H)
        first_h = [whole_h[:, half] for half in range(2)]
        act = tile([P, 2, HALF, 2], F32, "act0_0")
        for u, bank in enumerate(("a0", "n0")):
            acc = ps.tile([P, 2, HALF], F32, name="first_sums%d" % u, tag=bank)
            for e in range(2):
                up_sums(acc[:, e, :], 0, 2 * u + e, 0, HALF)
            for first in range(0, HALF, STEP if u else HALF):
                end = first + (STEP if u else HALF)
                nc.scalar.activation(act[:, u, first:end, :], acc[:, :, first:end].rearrange("p e n -> p n e"), GELU)
        for first in range(0, HALF, STEP):
            part = slice(first, first + STEP)
            times_sm(first_h[0][:, part], act[:, :, part, :].rearrange("p u n e -> p n u e"))
        acc = up_half(0, 1)
        for first in range(0, HALF, STEP):
            act = tile([P, STEP, PACK], F32, "act0_%d" % (HALF + first))
            nc.scalar.activation(act[:], acc[:, :, first : first + STEP].rearrange("p t n -> p n t"), GELU)
            times_sm(first_h[1][:, first : first + STEP], act[:].rearrange("p n (u e) -> p n u e", e=2))
        wd_s = tile([P, PACK, P], U8, "wd_s")
        raw_s = wd_s_raw[:].rearrange("p (m t) -> p t m", t=PACK)
        quantize_h(first_h[0].rearrange("p n u e -> p (n u e)"), 0, HALF)
        nc.vector.tensor_copy(wd_s[:], raw_s)
        quantize_h(first_h[1][:, :STEP].rearrange("p n u e -> p (n u e)"), HALF, STEP)
        quantize_h(first_h[1][:, STEP:].rearrange("p n u e -> p (n u e)"), HALF + STEP, STEP)
        cleared_page(placed([P, T], F32, "page2", AT_PAGE_2))
        last = CHUNKS - 1
        v_w[last] = gather_words(last * CHUNK, CHUNK, placed([P, CHUNK], U32, "v_w_last", AT_LAST_WORDS)[:])
        wgo_by_token = tile([P, J // P], F32, "wgo_by_token", "act0_%d" % (HALF + STEP))
        with nc.allow_non_contiguous_dma(reason="one weight a partition"):
            nc.sync.dma_start(out=wgo_by_token[:], in_=wgo[0].rearrange("(b p) -> p b", p=P))
        second_h = placed([P, CHUNK * PACK], BF16, "h1", AT_SECOND_H)
        act = tile([P, STEP, PACK], F32, "act1_0")
        acc = up_half(1, 0)
        nc.scalar.activation(act[:], acc[:, :, :STEP].rearrange("p t n -> p n t"), GELU)
        times_sm(
            second_h[:, : STEP * PACK].rearrange("p (n u e) -> p n u e", u=2, e=2),
            act[:].rearrange("p n (u e) -> p n u e", e=2),
        )
        act = tile([P, PACK, CHUNK - STEP], F32, "act1_1")
        nc.scalar.activation(act[:, :, :STEP], acc[:, :, STEP:], GELU)
        nc.scalar.activation(act[:, :, STEP:], up_half(1, 1)[:], GELU)

        def place(t, first, count, bank, after=None):
            name = "y%d_%d" % (t, first)
            y = placed([P, count], F32, name, after) if isinstance(after, int) else tile([P, count], F32, name, after)
            down(y[:], t, first, count, bank)
            scatter(pages[t], y[:], first, count)

        first_y = tile([P, CHUNK], F32, "y0_0")
        for first, end, bank in ((0, HALF, "a0"), (HALF, HALF + STEP, "n0"), (HALF + STEP, CHUNK, "a1")):
            down(first_y[:, first:end], 0, first, end - first, bank)
        scatter(pages[0], first_y[:], 0, CHUNK)

        rows = placed([P, PACK, CHUNK - STEP], BF16, "rows1", AT_ROWS)
        scaled_rows(rows, lambda t: act[:, t, :])
        place(1, 0, CHUNK, "y0")
        group(second_h[:, STEP * PACK :], rows)
        quantize_h(second_h[:], CHUNK, CHUNK)
        cleared_page(placed([P, T], F32, "page3", AT_PAGE_3))
        sums = up_chunk(2)
        place(2, 0, CHUNK, "y2", AT_ROWS + ALIGN - 4 * CHUNK)
        for c in range(1, CHUNKS):
            if c + 1 < CHUNKS:
                rows = hidden_rows(c + 1, sums)
            place(0, c * CHUNK, CHUNK, "y0", AT_ACT[c + 1] + ALIGN if c < last else None)
            place(1, c * CHUNK, CHUNK, "y0")
            if c + 1 < CHUNKS:
                group_and_quantize_h(c + 1, rows)
            if c + 2 < CHUNKS:
                sums = up_chunk(c + 2)
            if c < last:
                place(2, c * CHUNK, CHUNK, "y2", AT_LATER_ROWS + ALIGN if c == 1 else "rows3")

        distance = placed([P, P], F32, "distance", AT_ACT[2] + 2 * 4 * CHUNK)
        nc.scalar.activation(distance[:], apart[:], ABS)
        identity = tile([P, P], F32, "identity")
        nc.scalar.activation(identity[:], distance[:], RELU, bias=1.0, scale=-1.0)

        def turned_back(first, count, t, turned, banks, outs):
            blocks, wide = count // P, PACK - t
            acc = ps.tile([P, blocks, wide * P], F32, name="turned_sums%d" % first, tag=banks[0])
            for b in range(blocks):
                at = first + b * P
                nc.tensor.matmul_mx(
                    out=acc[:, b, :],
                    lhsT=h_w[:, at : at + P].bitcast(FP8X4),
                    lhsT_scale=h_s[:, at : at + P],
                    rhs=wd_w[:, P * t :].bitcast(FP8X4),
                    rhs_scale=wd_s[:, t:, :].rearrange("p t m -> p (t m)"),
                    start=True,
                    stop=True,
                )
            for b in range(blocks):
                at = first // P + b
                nc.scalar.activation(turned[:, b, :], acc[:, b, :], COPY, scale=wgo_by_token[:, at : at + 1])
            back = ps.tile([P, wide, count], F32, name="back%d" % first, tag=banks[1])
            for e in range(wide):
                for b in range(blocks):
                    nc.tensor.transpose(back[:, e, b * P : (b + 1) * P], turned[:, b, e * P : (e + 1) * P], identity[:])
            for e in range(wide):
                nc.scalar.copy(outs[e], back[:, e, :])

        last_y = tile([P, J], F32, "y3")
        y2_last = tile([P, CHUNK], F32, "y2_last")
        tail = last * CHUNK
        turned_back(tail, CHUNK, 2, tile([P, 2, 2 * P], F32, "turned_c"), ("b0", "a0"), [y2_last[:], last_y[:, tail:]])
        nc.vector.tensor_copy(pages[2][:].indirect(listed(tail, CHUNK)), y2_last[:])
        turned_back(0, BANK, 3, tile([P, BANK // P, P], F32, "turned_a", "h2"), ("n0", "n1"), [last_y[:, :BANK]])
        turned_back(BANK, CHUNK, 3, placed([P, 2, P], F32, "turned_b", AT_TURNED), ("b1", "a1"), [last_y[:, BANK:tail]])
        nc.vector.tensor_copy(pages[3][:].indirect(offsets[:]), last_y[:])

        out_rows = out_0.rearrange("(p t) n -> p t n", t=PACK)
        out_words = out_1[0].rearrange("p t i -> p (t i)")
        grouped = tile([P, T * PACK], BF16, "out_grouped")
        by_column = grouped[:].rearrange("p (n t) -> p n t", t=PACK)

        def gpsimd_copy(out, in_):
            nc.gpsimd.tensor_scalar(out, in_, 1.0, 0.0, MULT, ADD)

        def blocks_of(columns, part):
            first, count, step = part
            names = "p (b n) u -> p b n u" if columns.ndim == 3 else "p (b n) -> p b n"
            return columns.rearrange(names, n=BLOCK)[:, first : first + (count - 1) * step + 1 : step]

        odd = (T - SHARE) // BLOCK // 2
        parts = [(0, SHARE // BLOCK, 1), (SHARE // BLOCK, odd, 2), (SHARE // BLOCK + 1, odd, 2)]
        pairs = [
            placed([P, parts[0][1], 2, BLOCK, 2], BF16, "out_pairs0", AT_PAIRS_0),
            placed([P, odd, 2, BLOCK, 2], BF16, "out_pairs1", AT_PAIRS_1),
            tile([P, odd, 2, BLOCK, 2], BF16, "out_pairs2", "y2_last"),
        ]
        for t in range(PACK):
            nc.sync.dma_start(out=out_rows[:, t, :], in_=pages[t][:])
        for part, rounded, copy in zip(parts, pairs, (nc.scalar.copy, gpsimd_copy, gpsimd_copy)):
            for t in range(2):
                copy(rounded[:, :, 0, :, t], blocks_of(pages[t][:], part))
            copy(rounded[:, :, 1, :, :], blocks_of(pages[2][:], part).unsqueeze(3).to_broadcast([P, part[1], BLOCK, 2]))
        words = grouped[:].bitcast(F32).rearrange("p (n u) -> p n u", u=2)
        for part, rounded in zip(parts, pairs):
            nc.scalar.copy(
                blocks_of(words, part),
                rounded[:].rearrange("p b u n e -> p b (u n e)").bitcast(F32).rearrange("p b (u n) -> p b n u", u=2),
            )
        for first, end in ((0, QUARTER), (QUARTER, SHARE)):
            nc.vector.tensor_copy(by_column[:, first:end, PACK - 1], pages[3][:, first:end])
        for first, end in ((SHARE, 3 * QUARTER), (3 * QUARTER, T - CHUNK), (T - CHUNK, T)):
            nc.scalar.copy(by_column[:, first:end, PACK - 1], pages[3][:, first:end])

        out_s = tile([P, SIDE], U8, "out_s")
        for cuts in ((0, QUARTER), (QUARTER, SIDE), (SIDE, 3 * QUARTER), (3 * QUARTER, T - CHUNK), (T - CHUNK, T)):
            codes = tile([P, cuts[-1] - cuts[0]], U32, "out_w%d" % cuts[0])
            for first, end in zip(cuts, cuts[1:]):
                side, col = divmod(first, SIDE)
                nc.vector.quantize_mx(
                    out=codes[:, first - cuts[0] : end - cuts[0]].bitcast(FP8X4),
                    scales=out_s[4 * side : P, col : col + end - first],
                    in_=grouped[:, PACK * first : PACK * end],
                )
            nc.sync.dma_start(out=out_words[:, PACK * cuts[0] : PACK * cuts[-1]].bitcast(I32), in_=codes[:].bitcast(I32))
        for q in range(QUADS):
            queue = nc.scalar if q >= QUADS // 2 else nc.sync
            queue.dma_start(
                out=out_2[0, 4 * q : 4 * q + 4, :].rearrange("r (side n) -> side r n", side=2).bitcast(I32),
                in_=out_s[32 * q : 32 * q + 8, :].bitcast(I32),
            )
